import numpy as np, ml_dtypes
CORES = [48,51,52,55]
N = 4
BF = ml_dtypes.bfloat16
CAP, S, Q, M, W, RO = 96, 384, 8, 4, 4096, 4
def blocks(m):
    return np.stack([m[:, 16 * g:16 * g + 16, 16 * g:16 * g + 16] for g in range(8)], axis=1)
def diag(m):
    z = np.zeros((N, 8, 16, 8, 16), m.dtype)
    for g in range(8): z[:, g, :, g, :] = m[:, g]
    return z.reshape(N, 128, 128)
def play(b, lu, pb, ob):
    live = b[:, :, 0, :] >= 0
    num = np.maximum(np.matmul(pb.swapaxes(2, 3), b), 0)
    h = np.zeros(b.shape, np.int64)
    for j in range(16): h = h + np.take_along_axis(lu, num[:, :, j:j + 1, :], axis=3)
    fire = (np.matmul(ob.swapaxes(2, 3), np.maximum(h, 0)) > 0) & live[:, :, None, :]
    b = np.where(fire, (b + 1) & (Q - 1), b)
    return b, np.where(live, np.add.reduce(b, axis=2) & (N - 1), -1)
def parts(rng):
    cells = np.argsort(rng.random((N, 8, 16, 16)), axis=-1)[..., :M]
    pb = np.zeros((N, 8, 16, 16), np.int64); np.put_along_axis(pb, cells, np.broadcast_to(Q ** np.arange(M), cells.shape), axis=-1)
    lu = np.clip(rng.integers(-127, 128, (N, 8, 16, W)) + rng.integers(-16, 17, (N, 8, 16, 1)), -127, 127)
    return np.ascontiguousarray(pb.swapaxes(2, 3)), lu, rng.integers(-1, 2, (N, 8, 16, 16))
def boards(rng, m):
    return np.where(m[:, :, None, :], rng.integers(0, Q, (N, 8, 16, S)), -1)
def pack(b, lu, pb, ob):
    w = lambda a: np.ascontiguousarray(a).astype(np.float32).astype(BF)
    return {"x": w(b.reshape(N, 128, S)), "lut": w(lu.reshape(N, 128, W)), "pl": w(diag(pb)), "pol": w(diag(ob))}
def setup_inputs(rng):
    pb, lu, ob = parts(rng); fill = rng.choice(np.array([0.6, 0.75, 0.9, 1.0]), (N, 8, 1))
    return pack(boards(rng, rng.random((N, 8, S)) < fill), lu, pb, ob)
def setup_inputs_room(rng):
    pb, lu, ob = parts(rng); lu[:, 7] = -np.abs(lu[:, 7]); pool = rng.integers(0, Q, (N, 8, 16, 3 * S)); to = play(pool, lu, pb, ob)[1]
    b = np.full((N, 8, 16, S), -1, np.int64)
    for a in range(N):
        for g in range(7):
            seq = rng.permutation(N); left = S; ix = [np.zeros(0, np.int64)]
            if a == 0: seq = np.concatenate([np.array([1]), seq[seq != 1]])
            for i in range(N):
                n = int(rng.choice(np.array([0, 1, CAP - 1, CAP, CAP + 1, 2 * CAP])))
                if a == 0 and i == 0: n = (CAP, CAP + 1, 2 * CAP, CAP - 1, 1, 0, CAP)[g]
                if g == 6: n = CAP
                n = min(n, left); left -= n
                if n > 0: ix.append(np.resize(np.flatnonzero(to[a, g] == seq[i]), n).astype(np.int64))
            ix = rng.permutation(np.concatenate(ix)); pos = rng.permutation(S)[:len(ix)]
            b[a, g][:, pos] = pool[a, g][:, ix]
        e = 2 * int(rng.integers(0, N // 2))
        if a == 0: e = 2
        if e == a: e = (a + 2) % N
        some = rng.integers(0, Q, (16, 16 * S)); s = np.add.reduce(some, axis=0) & (N - 1)
        b[a, 7] = some[:, np.concatenate([np.flatnonzero(s == e)[:270], np.flatnonzero(s == e + 1)[:S - 270]])]
    return pack(b, lu, pb, ob)
def setup_inputs_ties(rng):
    pb, lu, ob = parts(rng)
    lu[:, :2] = rng.integers(-1, 2, (N, 2, 16, W)); lu[:, 2] = rng.choice(np.array([-127, 127]), (N, 16, W)); ob[:, 2] = rng.choice(np.array([-1, 1]), (N, 16, 16))
    lu[:, 3] = lu[:, 3, :1]; lu[:, 4] = -np.abs(lu[:, 4]); lu[:, 5] = 127; ob[:, 5] = 1; ob[:, 5, :, 8:] = -1
    ob[:, 6, :, :4] = 0; ob[:, 6, :, 4:8] = -1; ob[:, 6, :, 8:12] = 1
    lu[:, 7] = np.abs(lu[:, 7]); lu[:, 7, 8:] = lu[:, 7, :8]; ob[:, 7, :8, :8] = 1; ob[:, 7, 8:, :8] = -1
    fill = rng.choice(np.array([0.7, 0.9, 1.0]), (N, 8, 1))
    b = boards(rng, rng.random((N, 8, S)) < fill)
    b[:, 4, :, 0] = 0; b[:, 4, :, 1:Q + 1] = Q - 1; b[:, 4, 15, 1:Q + 1] = np.arange(Q)
    b[:, 5, :8, 0] = Q - 1; b[:, 5, 8:, 0] = 0; b[:, 5, :8, 1] = Q - 2; b[:, 5, 8:, 1] = Q - 1
    return pack(b, lu, pb, ob)
def setup_inputs_alike(rng):
    pb, lu, ob = parts(rng); m = rng.random((N, 8, S)) < rng.choice(np.array([0.75, 0.95]), (N, 8, 1)); m[:, :3] = True
    b = boards(rng, m)
    b[:, 0] = b[:, 0, :, :1]; b[:, 1] = np.tile(b[:, 1, :, :2], (1, 1, S // 2)); b[:, 2] = (Q - 1) * rng.integers(0, 2, (N, 1, S))
    pb[:, 4] = pb[:, 4, :, :1]
    return pack(b, lu, pb, ob)
def setup_inputs_thin(rng):
    pb, lu, ob = parts(rng); q = rng.permutation(N); fill = np.zeros((N, 8, 1))
    fill[:, 4:, 0] = np.stack([rng.permutation(np.array([0.1, 0.4, 0.7, 1.0])) for i in range(N)])
    fill[:, 7, 0] = 0.9; fill[q[0]] = 0.0; fill[q[1], 2] = 1.0
    m = rng.random((N, 8, S)) < fill; m[:, 0, S - 1] = True; m[:, 1, 0] = True
    return pack(boards(rng, m), lu, pb, ob)
def setup_inputs_spread(rng):
    pb, lu, ob = parts(rng)
    lu = ((2 * rng.random((N, 8, 16, W)) - 1) * np.exp2(7 * rng.random((N, 8, 1, W)))).astype(np.int64) * (rng.random((N, 8, 1, W)) > 0.0625)
    m = rng.random((N, 8, 1, S)) < rng.choice(np.array([0.3, 0.8, 1.0]), (N, 8, 1, 1))
    v = np.minimum((Q * rng.random((N, 8, 16, S)) ** np.exp2(rng.integers(-2, 3, (N, 8, 16, 1)))).astype(np.int64), Q - 1)
    return pack(np.where(m, v, -1), lu, pb, ob)
def check_inputs(d):
    bad = []; v = {k: np.asarray(d[k]).astype(np.float32) for k in ("x", "lut", "pl", "pol")}
    for k, lo, hi in (("x", -1, Q - 1), ("lut", -127, 127), ("pol", -1, 1)):
        if not np.all((v[k] >= lo) & (v[k] <= hi) & (v[k] == np.floor(v[k]))): bad.append("range of " + k)
    e = v["x"].reshape(N, 8, 16, S) == -1
    if np.any(np.any(e, axis=2) != np.all(e, axis=2)): bad.append("empty slots of x")
    for k in ("pl", "pol"):
        if not np.all(diag(blocks(v[k])) == v[k]): bad.append("zeros outside the blocks of " + k)
    want = np.concatenate([np.zeros(16 - M), Q ** np.arange(M)])
    if not np.all(np.sort(blocks(v["pl"]), axis=2) == want[:, None]): bad.append("weights of pl")
    return bad
def reference(x, lut, pl, pol):
    whole = lambda a: a.astype(np.float32).astype(np.int64)
    b = whole(x).reshape(N, 8, 16, S); lu = whole(lut).reshape(N, 8, 16, W); pb = blocks(whole(pl)); ob = blocks(whole(pol))
    for ply in range(RO):
        b, to = play(b, lu, pb, ob)
        come = np.full((N, 8, 16, S), -1, np.int64)
        for a in range(N):
            for r in range(N):
                for g in range(8):
                    ix = np.flatnonzero(to[a, g] == r)[:CAP]
                    come[r, g, :, a * CAP:a * CAP + len(ix)] = b[a, g][:, ix]
        b = come
    return {"y": b.reshape(N, 128, S).astype(np.float32).astype(BF)}

@@ -1,0 +1,347 @@
+from concourse.bass import DstId, RemoteDMATransfer
+from concourse.mybir import AluOpType, ActivationFunctionType
+
+A = AluOpType
+F = ActivationFunctionType
+NP, CAP, NR = 4, 96, 4
+WIN, BASE, REG = 1856, 320, 384
+FILL, SHIFT = -64.0, 6.125
+HDT = "float16"
+NV = [[[48, 48], [24, 24, 24]], [[24, 24, 24], [24, 24, 24]], [[24, 24, 24], [24, 24, 24]], [[24, 24, 24], [48, 48]]]
+ES = [[48, 48]] * 4
+JOINT = [[1, 1]] * 4
+
+ORDER = {
+    "y": "ldx lutA lutB st4A st4B",
+    "v": "z1 one z2 dl gt z3 cl ident ii ones xm evac0A i2 lb castO0A zz qo cvA castE0B evac0B cvB castE0A castO0B inc0A go gva0A gvb0A gvc0B reluE0A gvb0B reluO0A fireE0A um fireO0A gva0B cp0A inc0B and0A eq0A scan0A tE0A tO0A smax0A reluE0B cidx0A scat0A reluO0B fireE0B fireO0B tO0B cp0B and0B eq0B scan0B tE0B smax0B cidx0B scat0B castE1A castO1A inc1A gvc1A gva1A gvb1A castO1B castE1B gvc1B reluO1A reluE1A fireE1A fireO1A gvb1B cp1A and1A eq1A tE1A scan1A gva1B smax1A tO1A cidx1A scat1A reluE1B reluO1B fireE1B fireO1B inc1B tO1B cp1B and1B eq1B scan1B tE1B smax1B cidx1B scat1B castE2A inc2A castO2A gvc2A gvb2A gva2A castO2B castE2B gvb2B gvc2B reluE2A reluO2A fireE2A fireO2A gva2B cp2A and2A eq2A inc2B scan2A tE2A tO2A smax2A cidx2A scat2A reluE2B reluO2B fireE2B fireO2B tO2B cp2B and2B eq2B scan2B tE2B smax2B cidx2B scat2B castE3A castO3A gvc3A gva3A gvb3A castE3B castO3B gva3B reluE3A reluO3A inc3A fireE3A fireO3A gvb3B cp3A and3A tE3A eq3A reluE3B scan3A tO3A reluO3B inc3B smax3A fireO3B cidx3A fireE3B scat3A cp3B and3B eq3B tO3B scan3B tE3B smax3B cidx3B scat3B yev4A yev4B",
+    "s": "plA plB polA plA2 polB plB2 gathE0A gathF0A gathE0B gathF0B gathL0B evac1A gathE1A gathL1A gathF1A gathE1B gathF1B evac1B gathL1B evac2A gathE2A gathL2A gathF2A gathE2B evac2B gathF2B gathL2B evac3A gathE3A gathF3A gathL3A gathE3B gathF3B evac3B",
+    "g": "kc qc rt rs beta tr fill0A fill0B send0A own0A send0B own0B fill1B fill1A send1A own1A fill2A send1B own1B fill2B send2A own2A send2B fill3A own2B fill3B send3A own3A send3B own3B",
+    "p": "kr numE0A numO0B merge0A numO0A merge0B qr numE0B sua0A sua0B su0B su0A redEa0A redE0A redFa0A redF0A redVa0A redV0A polE0A redEa0B polO0A sfE0A sfO0A redE0B redFa0B redF0B rank00A rankM0A rankE0A redVa0B redV0B polE0B polO0B sfE0B sfO0B rank00B rankM0B rankE0B merge1A numE1A numO1A redEa1A redE1A redVa1A numE1B numO1B redV1A redFa1A redF1A sua1A polE1A polO1A su1A sfE1A sfO1A merge1B redEa1B rank01A redE1B rankM1A rankE1A redFa1B redF1B sua1B redVa1B redV1B polE1B su1B polO1B sfE1B sfO1B rank01B rankM1B rankE1B merge2A numO2A numE2A sua2A redEa2A redE2A numO2B numE2B redVa2A redV2A redFa2A redF2A merge2B polE2A polO2A su2A sfE2A sfO2A redEa2B redE2B sua2B rank02A rankM2A rankE2A redFa2B redF2B redVa2B redV2B polE2B su2B polO2B sfE2B sfO2B rank02B rankM2B rankE2B merge3A numE3A numO3A sua3A redEa3A redE3A numE3B numO3B redFa3A redF3A redVa3A redV3A merge3B su3A polE3A polO3A redEa3B redE3B sfE3A sfO3A redFa3B redF3B redVa3B redV3B rank03A rankM3A rankE3A polO3B polE3B sua3B su3B sfE3B sfO3B rank03B rankM3B rankE3B fin4A fin4B",
+}
+
+SCRATCH = {
+    "lutw": ("sbuf", [128, 2 * 4096], "bfloat16"),
+    "xs": ("sbuf", [128, 384], "bfloat16"),
+    "xm": ("sbuf", [128, 384], "bfloat16"),
+    "plb": ("sbuf", [128, 320], "bfloat16"),
+    "pob": ("sbuf", [128, 256], "bfloat16"),
+    "po": ("sbuf", [128, 256], HDT),
+    "cz": ("sbuf", [128, 480], "bfloat16"),
+    "kc": ("sbuf", [128, 128], "bfloat16"),
+    "qc": ("sbuf", [128, 128], "bfloat16"),
+    "one": ("sbuf", [128, 16], "bfloat16"),
+    "dl": ("sbuf", [128, 128], "bfloat16"),
+    "ident": ("sbuf", [128, 128], "bfloat16"),
+    "cl": ("sbuf", [128, 128], "bfloat16"),
+    "ones": ("sbuf", [128, 128], "bfloat16"),
+    "gt": ("sbuf", [128, 128], "bfloat16"),
+    "i2": ("sbuf", [128, 128], "bfloat16"),
+    "go": ("sbuf", [128, 128], "bfloat16"),
+    "um": ("sbuf", [128, 128], "bfloat16"),
+    "beta": ("sbuf", [128, 48], "bfloat16"),
+    "rt": ("sbuf", [128, 64], "float32"),
+    "rs": ("sbuf", [128, 64], "float32"),
+    "tr": ("sbuf", [128, 48], "float32"),
+    "qo": ("sbuf", [128, 4], "uint16"),
+    "off": ("sbuf", [128, 8 * 192], "uint16"),
+    "gat": ("sbuf", [128, 8 * 3072], "bfloat16"),
+    "v": ("sbuf", [128, 8 * 192], "bfloat16"),
+    "inc": ("sbuf", [128, 8 * 192], "bfloat16"),
+    "rh": ("sbuf", [128, 8 * 192], HDT),
+    "fire": ("sbuf", [128, 8 * 192], "bfloat16"),
+    "t": ("sbuf", [128, 8 * 192], "bfloat16"),
+    "si": ("sbuf", [128, 8 * 16], "int32"),
+    "d": ("sbuf", [128, 8 * 16], "int32"),
+    "m": ("sbuf", [128, 8 * 64], "bfloat16"),
+    "e": ("sbuf", [128, 8 * 64], "bfloat16"),
+    "sm": ("sbuf", [128, 8 * 48], "float32"),
+    "idx": ("sbuf", [128, 8 * 16], "uint16"),
+    "win": ("sbuf", [128, 8 * WIN], "bfloat16"),
+    "land": ("sbuf", [128, 8 * 384], "bfloat16"),
+    "yb": ("sbuf", [128, 2 * 192], "bfloat16"),
+}
+for _h in "AB":
+    for _b in "XYZW":
+        SCRATCH["p" + _b + _h] = ("psum", [128, 512], "float32")
+
+START = ["z1", "z2", "z3", "one", "kc", "qc", "beta", "rt", "rs", "tr", "kr", "qr", "qo", "dl", "ident", "ii", "cl", "ones",
+         "lb", "zz", "gt", "i2", "go", "um", "xm", "ldx", "lutA", "lutB", "plA", "plB", "plA2", "plB2", "polA", "polB",
+         "cvA", "cvB"]
+ROLES = ["numE", "numO", "castE", "castO", "merge", "evac", "inc", "gathE", "gathF", "gathL", "gva", "gvb", "gvc", "gvd",
+         "redE", "redF", "redV", "redL", "reluE", "reluO", "polE", "polO", "fireE", "fireO", "tE", "tO", "sfO", "cp",
+         "and", "eq", "scan", "rankE", "smax", "cidx", "scat", "own", "fill", "fin", "yev", "st"]
+SEMAPHORES = (["s_" + n for n in START] + ["r_" + r + x for r in ROLES for x in "AB"]
+              + ["arr%d%s" % (k, x) for k in range(NP) for x in "AB"] + ["sentA", "sentB"])
+
+
+def plan(cores, me, topo):
+    out, far = {}, 0
+    for r in range(NR):
+        if r == me:
+            continue
+        eng = topo.engines(cores[me], cores[r])
+        if topo.die(cores[r]) == topo.die(cores[me]):
+            out[r] = eng[1::2]
+        else:
+            quarter = len(eng) // 4
+            out[r] = eng[0::2][far * quarter:(far + 1) * quarter]
+            far += 1
+    return out
+
+
+def graph(g, T, me, topo):
+    ops = {}
+    V, S, P = g.vector, g.scalar, g.tensor
+
+    def op(name, q, kind, n, hard, emit, soft=(), sem=None, inc=1):
+        ops[name] = dict(q=q, kind=kind, n=n, hard=list(hard), soft=list(soft), emit=emit, sem=sem, inc=inc)
+
+    def st(name, q, kind, n, hard, emit, inc=1):
+        op(name, q, kind, n, hard, emit, sem="s_" + name, inc=inc)
+
+    II, LB, ZZ = 0, 192, 336
+    cz = T.cz
+    iota = lambda o, pat, b, cm: g.iota(o, pat, b, cm, allow_small_or_imprecise_dtypes=True)
+    st("z1", "v", "half", 320, [], lambda: [V.memset(T.plb[:], 0.0)])
+    st("z2", "v", "half", 256, [], lambda: [V.memset(T.pob[:], 0.0)])
+    st("ldx", "y", "dma", 96, [], lambda: [g.sync.dma_start(T.xs[:], T.x[:])], inc=16)
+    for i, X in enumerate("AB"):
+        st("lut" + X, "y", "dma", 1024, [], lambda i=i: [
+            g.sync.dma_start(T.lutw[64 * h:64 * h + 64, 4096 * i:4096 * i + 4096], T.lut[64 * i:64 * i + 64, :])
+            for h in range(2)], inc=16)
+        for nm, h in (("pl" + X, i), ("pl" + X + "2", 1 - i)):
+            st(nm, "s", "dma", 8, ["z1"], lambda i=i, h=h: [
+                S.dma_start(T.plb[64 * h:64 * h + 64, 64 + 128 * i:128 + 128 * i],
+                            T.pl[64 * i:64 * i + 64, 64 * i:64 * i + 64])], inc=16)
+        st("pol" + X, "s", "dma", 16, ["z2"], lambda i=i: [
+            S.dma_start(T.pob[64 * h:64 * h + 64, 128 * i + 64 * h:128 * i + 64 * h + 64],
+                        T.pol[64 * i:64 * i + 64, 64 * i:64 * i + 64]) for h in range(2)], inc=16)
+        st("cv" + X, "v", "half", 128, ["pol" + X],
+           lambda i=i: [V.tensor_copy(T.po[:, 128 * i:128 * i + 128], T.pob[:, 128 * i:128 * i + 128])])
+    ops["lutA"]["soft"] = ["ldx"]
+    ops["lutB"]["soft"] = ["lutA"]
+    st("z3", "v", "half2", 480, [], lambda: [V.memset(cz[:], 0.0), V.memset(T.d[:], 0)])
+    st("one", "v", "half", 16, [], lambda: [V.memset(T.one[:], 1.0)])
+    st("kc", "g", "iota", 128, [], lambda: [iota(T.kc[:], [[1, 2], [64, 4], [2, 16]], 0, 0)])
+    st("qc", "g", "iota", 128, [], lambda: [iota(T.qc[:], [[0, 8], [1, 16]], 0, 0)])
+    st("beta", "g", "iota", 48, [], lambda: [iota(T.beta[:], [[0, 12], [REG // 32, 4]], BASE // 32 - 64, 0)])
+    st("rt", "g", "iota", 64, [], lambda: [iota(T.rt[:], [[1, 4], [0, 16]], 0, 0)])
+    st("rs", "g", "iota", 64, [], lambda: [iota(T.rs[:], [[0, 4], [16, 16]], 0, 0)])
+    st("tr", "g", "iota", 48, [], lambda: [iota(T.tr[:], [[-16, 12], [4096, 4]], BASE, -1)])
+    st("kr", "p", "mm", 64, ["kc", "one"], lambda: [P.matmul(T.pWA[:, 0:2], T.kc[0:1, :], T.one[0:1, 0:2], True, True)])
+    st("qr", "p", "mm", 64, ["qc", "one"], lambda: [P.matmul(T.pWB[:, 0:4], T.qc[0:1, :], T.one[0:1, 0:4], True, True)])
+    st("qo", "v", "full", 4, ["qr"], lambda: [V.tensor_copy(T.qo[:], T.pWB[:, 0:4])])
+    st("dl", "v", "half", 128, ["kr", "kc"],
+       lambda: [V.tensor_scalar(T.dl[:], T.kc[:], T.pWA[:, 0:1], -1.0, A.subtract, A.mult)])
+    st("ident", "v", "half", 128, ["dl"], lambda: [V.tensor_scalar(T.ident[:], T.dl[:], 0.0, None, A.is_equal)])
+    st("ii", "v", "two", 64, ["ident", "z3"],
+       lambda: [V.tensor_tensor(cz[:, II + 64:II + 128], T.ident[:, 0:64], T.ident[:, 64:128], A.add)])
+    st("cl", "v", "half", 128, ["dl"], lambda: [V.tensor_scalar(T.cl[:], T.dl[:], -31.5, 31.5, A.max, A.min)])
+    st("ones", "v", "two", 128, ["cl", "dl"], lambda: [V.tensor_tensor(T.ones[:], T.cl[:], T.dl[:], A.is_equal)])
+    st("lb", "v", "half2", 8, ["ones", "z3"], lambda: [
+        V.tensor_copy(cz[64 * h:64 * h + 64, LB + 15 + 64 * h:LB + 79 + 64 * h:16],
+                      T.ones[64 * h:64 * h + 64, 64 * h:64 * h + 64:16]) for h in range(2)])
+    st("zz", "v", "half", 64, ["ii", "z3"], lambda: [V.tensor_copy(cz[:, ZZ + 1:ZZ + 129:2], cz[:, II + 64:II + 128])])
+    st("gt", "v", "half", 128, ["dl"], lambda: [V.tensor_scalar(T.gt[:], T.dl[:], 0.0, None, A.is_gt)])
+    st("i2", "v", "half", 128, ["dl"], lambda: [V.tensor_scalar(T.i2[:], T.dl[:], 0.0, 2048.0, A.is_equal, A.mult)])
+    st("go", "v", "two", 128, ["gt", "ones"], lambda: [V.tensor_tensor(T.go[:], T.gt[:], T.ones[:], A.mult)])
+    st("um", "v", "two", 128, ["go", "i2"], lambda: [V.tensor_tensor(T.um[:], T.i2[:], T.go[:], A.subtract)])
+    st("xm", "v", "half", 384, ["ldx"], lambda: [V.tensor_scalar(T.xm[:], T.xs[:], 0.0, 63.0, A.min, A.mult)])
+
+    engs = plan(T.cores, me, topo)
+    come = sum(len(plan(T.cores, a, topo)[me]) for a in range(NR) if a != me)
+
+    def half(k, i, X):
+        n = lambda r, kk=k: "%s%d%s" % (r, kk, X)
+        j = 2 * k + i
+
+        def ro(r, q, kind, sz, hard, emit, soft=(), sem=True, inc=1):
+            op(n(r), q, kind, sz, hard, emit, soft, ("r_" + r + X) if sem else None, inc)
+
+        prev = lambda *rs: [n(r, k - 1) for r in rs] if k > 0 else []
+        pX, pY, pZ, pW = (T["p" + b + X] for b in "XYZW")
+        pl = lambda h, a=0, b=128: T.plb[a:b, 64 + 128 * i - 64 * h:192 + 128 * i - 64 * h]
+        ii = lambda h, a=0, b=128: cz[a:b, II + 64 - 64 * h:II + 192 - 64 * h]
+        L0 = 384 * (j - 2)
+        src = prev("arr", "own")
+        if k == NP:
+            ro("fin", "p", "mm", 384, src + ["zz"] + prev("fireO"), lambda: [[
+                P.matmul(pX[:, 0:192], cz[:, ZZ + 1 - h:ZZ + 129 - h], T.land[:, L0 + 192 * h:L0 + 192 * h + 192],
+                         h == 0, h == 1) for h in range(2)][-1]])
+            ro("yev", "v", "full", 192, [n("fin")], lambda: [
+                V.tensor_scalar(T.yb[:, 192 * i:192 * i + 192], pX[:, 0:192], SHIFT - FILL, -1.0, A.add, A.max)])
+            ro("st", "y", "dma", 48, [n("yev")], lambda: [
+                g.sync.dma_start(T.y[64 * i:64 * i + 64, :], T.yb[:, 192 * i:192 * i + 192])], inc=16)
+            return
+        c0 = 192 * j
+        a, b = 64 * i, 64 * i + 64
+        for e, E, pn in ((0, "E", pX), (1, "O", pZ)):
+            free = prev("fireO" if e == 0 else "fireE")
+            if k == 0:
+                ro("num" + E, "p", "mm", 192, ["ldx", "pl" + X], lambda e=e, pn=pn: [[
+                    P.matmul(pn[:, 0:96], pl(h, a, b), T.xs[a:b, 2 * e + h::4], h == 0, h == 1) for h in range(2)][-1]])
+            else:
+                ro("num" + E, "p", "mm", 192, src + free + ["pl" + X, "pl" + X + "2"], lambda e=e, pn=pn: [[
+                    P.matmul(pn[:, 0:96], pl(h), T.land[:, L0 + 2 * e + h:L0 + 384:4], h == 0, h == 1)
+                    for h in range(2)][-1]])
+            ro("cast" + E, "v", "full", 96, [n("num" + E)], lambda e=e, pn=pn: [
+                V.tensor_scalar(T.off[:, c0 + 96 * e:c0 + 96 * e + 96], pn[:, 0:96],
+                                585.0 * (SHIFT - FILL) if k > 0 else 0.0, 0.0, A.add, A.max)])
+        if k == 0:
+            ro("merge", "p", "mm", 768, ["ldx", "xm", "ii"], lambda: [[
+                P.matmul(pY[:, 0:192], ii(h, a, b), s[a:b, h::2], w == 0 and h == 0, w == 1 and h == 1)
+                for w, s in enumerate((T.xs, T.xm)) for h in range(2)][-1]])
+            ro("evac", "v", "full", 192, [n("merge")], lambda: [
+                V.tensor_scalar(T.v[:, c0:c0 + 192], pY[:, 0:192], -SHIFT, FILL, A.add, A.max)])
+        else:
+            ro("merge", "p", "mm", 384, src + prev("reluO") + ["ii"], lambda: [[
+                P.matmul(pY[:, 0:192], ii(h), T.land[:, L0 + h:L0 + 384:2], h == 0, h == 1) for h in range(2)][-1]])
+            ro("evac", "s", "full", 192, [n("merge")], lambda: [
+                S.activation(T.v[:, c0:c0 + 192], pY[:, 0:192], F.Identity, bias=-FILL)])
+        ro("inc", "v", "half", 192, [n("evac")], lambda: [
+            V.tensor_scalar(T.inc[:, c0:c0 + 192], T.v[:, c0:c0 + 192], -8.0, 1.0, A.mult, A.min)])
+        lq = lambda q: cz[:, LB + 15 - q:LB + 143 - q]
+        for nm, q0, dep, soft in (("sua", 0, [n("evac"), "lb"] + (prev("smax") or ["dl" if i == 0 else "qo"]), []),
+                                  ("su", 8, [], [n("sua")])):
+            ro(nm, "p", "mm", 512, dep, lambda q0=q0: [[
+                P.matmul(pW[:, 0:12], lq(q), T.v[:, c0 + q:c0 + 192:16], q == 0, False) for q in range(q0, q0 + 8)][-1]],
+               soft=soft, sem=False)
+        G0 = 3072 * j
+        tab = T.lutw[:, 4096 * i:4096 * i + 4096]
+
+        def gather(nm, q, c, w):
+            out = T.gat[:, G0 + 16 * c:G0 + 16 * (c + w)]
+            win = lambda: tab.indirect(T.off[:, c0 + c:c0 + c + w])
+            ro(nm, q, "gath", 16 * w, [n("castE" if c < 96 else "castO"), "lut" + X],
+               (lambda: [S.activation(out, win(), F.Copy)]) if q == "s" else (lambda: [V.tensor_copy(out, win())]))
+            return n(nm)
+
+        def summed(nm, dep, c, w, soft):
+            ph, pc = (pX, c) if c < 96 else (pY, c - 96)
+            for sfx, u0 in (("a", 0), ("", 8)):
+                ro(nm + sfx, "p", "mm", 8 * max(64, w), dep + ["ident"] if sfx else [], lambda u0=u0: [[
+                    P.matmul(ph[:, pc:pc + w], T.ident[:], T.gat[:, G0 + 16 * c + u:G0 + 16 * (c + w):16], u == 0, u == 15)
+                    for u in range(u0, u0 + 8)][-1]], soft=soft if sfx else [n(nm + "a")], sem=not sfx)
+            return n(nm)
+
+        w1 = ES[k][i]
+        redE = [summed("redE", [gather("gathE", "s", 0, w1)], 0, w1, [])]
+        if w1 < 96:
+            redE.append(summed("redF", [gather("gathF", "s", w1, 96 - w1)], w1, 96 - w1, list(redE)))
+        c, gv, reds = 96, [], []
+        for w, nm in zip(NV[k][i], ("gva", "gvb", "gvc", "gvd")):
+            gv.append(gather(nm, "v", c, w))
+            c += w
+        todo = [("redV", gv, 96, c - 96)] if gv else []
+        if c < 192:
+            todo.append(("redL", [gather("gathL", "s", c, 192 - c)], c, 192 - c))
+        if JOINT[k][i] == 1 and len(todo) == 2:
+            todo = [("redV", todo[0][1] + todo[1][1], 96, 96)]
+        for nm, dep, cc, w in todo:
+            reds.append(summed(nm, dep + [n("evac")], cc, w, list(reds)))
+        for e, E, ph, pz, dep, free in ((0, "E", pX, pZ, redE, n("castO")), (1, "O", pY, pX, reds, n("reluE"))):
+            rh = T.rh[:, c0 + 96 * e:c0 + 96 * e + 96]
+            ro("relu" + E, "v", "full", 96, dep, lambda rh=rh, ph=ph: [
+                V.tensor_scalar(rh, ph[:, 0:96], 0.0, None, A.max)])
+            ro("pol" + E, "p", "mm", 96, [n("relu" + E), "cv" + X, free],
+               lambda rh=rh, pz=pz: [P.matmul(pz[:, 0:96], T.po[:, 128 * i:128 * i + 128], rh, True, True)])
+            ro("fire" + E, "v", "full", 96, [n("pol" + E)], lambda e=e, pz=pz: [
+                V.tensor_scalar(T.fire[:, c0 + e:c0 + 192:2], pz[:, 0:96], 0.0, None, A.is_gt)])
+            ro("t" + E, "v", "two", 96, [n("fire" + E), n("inc")], lambda e=e: [
+                V.tensor_tensor(T.t[:, c0 + e:c0 + 192:2], T.fire[:, c0 + e:c0 + 192:2], T.inc[:, c0 + e:c0 + 192:2],
+                                A.mult)])
+            ro("sf" + E, "p", "mm", 512, [n("fire" + E)], lambda e=e: [[
+                P.matmul(pW[:, 0:12], lq(q), T.fire[:, c0 + q:c0 + 192:16], False, q == 15)
+                for q in range(e, 16, 2)][-1]], soft=[n("su")] if e == 0 else [n("sfE")], sem=(e == 1))
+        s0, m0, x0, W0 = 16 * j, 64 * j, 48 * j, WIN * j
+        ro("cp", "v", "full", 12, [n("sfO")], lambda: [
+            V.tensor_scalar(T.si[:, s0:s0 + 12], pW[:, 0:12], 16 * SHIFT, None, A.add)])
+        ro("and", "v", "full", 12, [n("cp"), "z3"], lambda: [
+            V.tensor_scalar(T.d[:, s0:s0 + 12], T.si[:, s0:s0 + 12], 1027, None, A.bitwise_and)])
+        ro("eq", "v", "gath", 64, [n("and"), "qo", "rt"], lambda: [
+            V.tensor_tensor(T.m[:, m0:m0 + 64], T.d[:, s0:s0 + 16].indirect(T.qo[:, 0:4]), T.rt[:], A.is_equal)])
+        ro("scan", "v", "full", 64, [n("eq"), "rs"], lambda: [
+            V.tensor_tensor_scan(T.e[:, m0:m0 + 64], T.rs[:], T.m[:, m0:m0 + 64], 0.0, A.min, A.add)])
+        ro("rank0", "p", "mm", 64, [n("cp"), "ones", "beta"], lambda: [
+            P.matmul(pW[:, 64:112], T.ones[:], T.beta[:], True, False)], sem=False)
+        ro("rankM", "p", "mm", 256, [n("eq"), "um"], lambda: [[
+            P.matmul(pW[:, 64 + r:112:4], T.um[:], T.m[:, m0 + 16 * r:m0 + 16 * r + 12], False, False)
+            for r in range(4)][-1]], soft=[n("rank0")], sem=False)
+        ro("rankE", "p", "mm", 256, [n("scan")], lambda: [[
+            P.matmul(pW[:, 64 + r:112:4], T.ones[:], T.e[:, m0 + 16 * r:m0 + 16 * r + 12], False, r == 3)
+            for r in range(4)][-1]], soft=[n("rankM")])
+        ro("smax", "v", "full", 48, [n("rankE"), "tr"], lambda: [
+            V.tensor_tensor_scan(T.sm[:, x0:x0 + 48], T.tr[:], pW[:, 64:112], 1.0e6, A.min, A.max)])
+        ro("cidx", "v", "full", 12, [n("smax")], lambda: [
+            V.tensor_scalar(T.idx[:, s0:s0 + 12], T.sm[:, x0 + 3:x0 + 48:4], -1.0, None, A.add)])
+        reg = lambda r: T.win[:, W0 + BASE + REG * r:W0 + BASE + REG * r + CAP]
+        ro("fill", "g", "iota4", CAP, prev("scat"), lambda: [iota(reg(r), [[0, CAP]], int(FILL), 0) for r in range(NR)],
+           soft=prev("own"))
+        ro("scat", "v", "scat", 192, [n("cidx"), n("tE"), n("tO"), n("fill"), n("evac")], lambda: [
+            V.tensor_tensor(T.win[:, W0:W0 + WIN].indirect(T.idx[:, s0:s0 + 12]), T.v[:, c0:c0 + 192],
+                            T.t[:, c0:c0 + 192], A.add)])
+        mine = T.land[:, 384 * j + CAP * me:384 * j + CAP * me + CAP]
+
+        def send():
+            tr = []
+            for r in sorted(engs):
+                rid, pid, _ = topo.addr(T.cores[r])
+                tr.append(RemoteDMATransfer(dst_ids=[DstId(rid=rid, pnc=pid)], dma_engine_mask=sum(1 << e for e in engs[r]),
+                                            remote_sem=T.sem["arr%d%s" % (k, X)], src=reg(r), dst=mine))
+            g.remote_dma_fused(tr, local_sem=T.sem["sent" + X])
+            return []
+
+        ro("send", "g", "send", 0, [n("scat")], send, sem=False)
+        ro("own", "g", "iota", CAP, [n("scat")], lambda: [
+            g.affine_select(mine, reg(me), [[0, CAP]], A.is_ge, 0.0, 0, 0)], soft=[n("send")])
+        op(n("arr"), None, "arr", 0, [], None, soft=[n("send")], sem="arr%d%s" % (k, X), inc=come)
+
+    for k in range(NP + 1):
+        for i, X in enumerate("AB"):
+            half(k, i, X)
+    return ops, sum(len(e) for e in engs.values())
+
+
+def topo_order(ops):
+    seen, out = set(), []
+    while len(out) < len(ops):
+        for n in ops:
+            if n not in seen and all(d in seen for d in ops[n]["hard"] + ops[n]["soft"]):
+                seen.add(n)
+                out.append(n)
+    return out
+
+
+def rank_program(g, core, T, topo):
+    me = T.rank_of(core)
+    if me is None:
+        return
+    ops, sent = graph(g, T, me, topo)
+    queue = {"v": g.vector, "s": g.scalar, "p": g.tensor, "y": g.sync, "g": g}
+    many = {"half2": 2, "iota4": 4}
+    total, mark = {}, {}
+    for n in topo_order(ops):
+        o = ops[n]
+        if o["sem"]:
+            k = many.get(o["kind"], 2 if n[:3] in ("lut", "pol") and o["kind"] == "dma" else 1)
+            total[o["sem"]] = total.get(o["sem"], 0) + k * o["inc"]
+            mark[n] = total[o["sem"]]
+    waited = {}
+    for q in ORDER:
+        seen = {}
+        for n in ORDER[q].split():
+            o = ops[n]
+            for d in o["hard"]:
+                s = ops[d]["sem"]
+                if seen.get(s, 0) < mark[d]:
+                    queue[q].wait_ge(T.sem[s], mark[d])
+                    seen[s] = mark[d]
+                    waited[s] = max(waited.get(s, 0), mark[d])
+            for ins in o["emit"]():
+                if o["sem"]:
+                    ins.then_inc(T.sem[o["sem"]], o["inc"])
+    for X in "AB":
+        g.wait_ge(T.sem["sent" + X], NP * sent)
+    for s in total:
+        if waited.get(s, 0) < total[s]:
+            g.wait_ge(T.sem[s], total[s])

@@ -5,7 +5,7 @@ A = AluOpType
 F = ActivationFunctionType
 NP, CAP, NR = 4, 96, 4
 WIN, BASE, REG = 1856, 320, 384
-FILL, SHIFT = -64.0, 6.125
+FILL, SHIFT = -1024.0, 6.125
 HDT = "float16"
 NV = [[[48, 48], [24, 24, 24]], [[24, 24, 24], [24, 24, 24]], [[24, 24, 24], [24, 24, 24]], [[24, 24, 24], [48, 48]]]
 ES = [[48, 48]] * 4
@@ -13,10 +13,10 @@ JOINT = [[1, 1]] * 4
 
 ORDER = {
     "y": "ldx lutA lutB st4A st4B",
-    "v": "z1 one z2 dl gt z3 cl ident ii ones xm evac0A i2 lb castO0A zz qo cvA castE0B evac0B cvB castE0A castO0B inc0A go gva0A gvb0A gvc0B reluE0A gvb0B reluO0A fireE0A um fireO0A gva0B cp0A inc0B and0A eq0A scan0A tE0A tO0A smax0A reluE0B cidx0A scat0A reluO0B fireE0B fireO0B tO0B cp0B and0B eq0B scan0B tE0B smax0B cidx0B scat0B castE1A castO1A inc1A gvc1A gva1A gvb1A castO1B castE1B gvc1B reluO1A reluE1A fireE1A fireO1A gvb1B cp1A and1A eq1A tE1A scan1A gva1B smax1A tO1A cidx1A scat1A reluE1B reluO1B fireE1B fireO1B inc1B tO1B cp1B and1B eq1B scan1B tE1B smax1B cidx1B scat1B castE2A inc2A castO2A gvc2A gvb2A gva2A castO2B castE2B gvb2B gvc2B reluE2A reluO2A fireE2A fireO2A gva2B cp2A and2A eq2A inc2B scan2A tE2A tO2A smax2A cidx2A scat2A reluE2B reluO2B fireE2B fireO2B tO2B cp2B and2B eq2B scan2B tE2B smax2B cidx2B scat2B castE3A castO3A gvc3A gva3A gvb3A castE3B castO3B gva3B reluE3A reluO3A inc3A fireE3A fireO3A gvb3B cp3A and3A tE3A eq3A reluE3B scan3A tO3A reluO3B inc3B smax3A fireO3B cidx3A fireE3B scat3A cp3B and3B eq3B tO3B scan3B tE3B smax3B cidx3B scat3B yev4A yev4B",
-    "s": "plA plB polA plA2 polB plB2 gathE0A gathF0A gathE0B gathF0B gathL0B evac1A gathE1A gathL1A gathF1A gathE1B gathF1B evac1B gathL1B evac2A gathE2A gathL2A gathF2A gathE2B evac2B gathF2B gathL2B evac3A gathE3A gathF3A gathL3A gathE3B gathF3B evac3B",
-    "g": "kc qc rt rs beta tr fill0A fill0B send0A own0A send0B own0B fill1B fill1A send1A own1A fill2A send1B own1B fill2B send2A own2A send2B fill3A own2B fill3B send3A own3A send3B own3B",
-    "p": "kr numE0A numO0B merge0A numO0A merge0B qr numE0B sua0A sua0B su0B su0A redEa0A redE0A redFa0A redF0A redVa0A redV0A polE0A redEa0B polO0A sfE0A sfO0A redE0B redFa0B redF0B rank00A rankM0A rankE0A redVa0B redV0B polE0B polO0B sfE0B sfO0B rank00B rankM0B rankE0B merge1A numE1A numO1A redEa1A redE1A redVa1A numE1B numO1B redV1A redFa1A redF1A sua1A polE1A polO1A su1A sfE1A sfO1A merge1B redEa1B rank01A redE1B rankM1A rankE1A redFa1B redF1B sua1B redVa1B redV1B polE1B su1B polO1B sfE1B sfO1B rank01B rankM1B rankE1B merge2A numO2A numE2A sua2A redEa2A redE2A numO2B numE2B redVa2A redV2A redFa2A redF2A merge2B polE2A polO2A su2A sfE2A sfO2A redEa2B redE2B sua2B rank02A rankM2A rankE2A redFa2B redF2B redVa2B redV2B polE2B su2B polO2B sfE2B sfO2B rank02B rankM2B rankE2B merge3A numE3A numO3A sua3A redEa3A redE3A numE3B numO3B redFa3A redF3A redVa3A redV3A merge3B su3A polE3A polO3A redEa3B redE3B sfE3A sfO3A redFa3B redF3B redVa3B redV3B rank03A rankM3A rankE3A polO3B polE3B sua3B su3B sfE3B sfO3B rank03B rankM3B rankE3B fin4A fin4B",
+    "g": "kc qc rt beta tr fill0A fill0B send0A own0A fill1A send0B own0B fill1B send1A own1A fill2A send1B own1B fill2B send2A own2A fill3A send2B own2B fill3B send3A own3A send3B own3B",
+    "v": "z1 one z2 z3 dl cl ident ii gt zz ones i2 lb go um un qo rp xm castE0A castO0A evac0A castE0B cvA evac0B castO0B cvB gvb0A gva0A inc0A inc0B reluE0A gvc0B reluO0A fireE0A fireO0A gvb0B cp0A eq0A tE0A scan0A gva0B smax0A tO0A cidx0A reluE0B scat0A reluO0B fireE0B fireO0B tO0B cp0B eq0B scan0B tE0B smax0B cidx0B scat0B castE1A castO1A gvb1A gvc1A gva1A reluO1A castO1B castE1B gvc1B reluE1A inc1A fireE1A fireO1A gva1B cp1A eq1A tO1A scan1A gvb1B smax1A tE1A cidx1A reluE1B scat1A reluO1B inc1B fireE1B fireO1B tO1B cp1B eq1B scan1B tE1B smax1B cidx1B scat1B castE2A castO2A gva2A inc2A gvc2A gvb2A castO2B castE2B gvc2B reluE2A gvb2B reluO2A fireE2A fireO2A gva2B cp2A eq2A scan2A tE2A tO2A smax2A cidx2A scat2A reluO2B reluE2B inc2B fireE2B fireO2B cp2B eq2B tE2B scan2B tO2B smax2B cidx2B scat2B castE3A castO3A gvc3A gvb3A gva3A castO3B castE3B gva3B reluE3A reluO3A fireE3A fireO3A gvb3B inc3A cp3A eq3A scan3A tE3A reluE3B reluO3B tO3A inc3B smax3A fireE3B cidx3A fireO3B scat3A cp3B eq3B tO3B scan3B tE3B smax3B cidx3B scat3B yev4A yev4B",
+    "s": "plA plB polA polB plA2 plB2 gathE0A gathF0A gathE0B gathF0B gathL0B gathE1A evac1A gathL1A gathF1A evac1B gathE1B gathF1B gathL1B evac2A gathE2A gathF2A gathL2A gathE2B gathL2B evac2B gathF2B evac3A gathE3A gathF3A gathL3A gathE3B gathF3B evac3B",
+    "p": "kr qr numE0A numO0A merge0A numE0B merge0B numO0B sua0A su0A redEa0A redE0A redFa0A redF0A redVa0A redV0A sua0B polE0A polO0A su0B sfE0A sfO0A redEa0B redE0B rank00A rankM0A rankE0A redFa0B redF0B redVa0B redV0B polE0B polO0B sfE0B sfO0B rank00B rankM0B rankE0B numE1A numO1A merge1A redEa1A redE1A redVa1A redV1A numO1B numE1B merge1B redFa1A redF1A sua1A polE1A polO1A su1A sfE1A sfO1A redEa1B redE1B rank01A rankM1A rankE1A redFa1B redF1B redVa1B redV1B polE1B sua1B polO1B su1B sfE1B sfO1B rank01B rankM1B rankE1B numE2A merge2A numO2A sua2A redEa2A redE2A numO2B numE2B redFa2A redF2A redVa2A redV2A polE2A su2A polO2A sfE2A sfO2A merge2B redEa2B redE2B rank02A rankM2A rankE2A redVa2B redV2B redFa2B redF2B sua2B polE2B polO2B su2B sfE2B sfO2B rank02B rankM2B rankE2B numE3A merge3A numO3A sua3A redEa3A redE3A su3A numO3B numE3B redFa3A redF3A redVa3A redV3A merge3B polE3A polO3A redEa3B redE3B sfE3A sfO3A redFa3B redF3B redVa3B redV3B rank03A rankM3A rankE3A polE3B polO3B sua3B su3B sfE3B sfO3B rank03B rankM3B rankE3B fin4A fin4B",
 }
 
 SCRATCH = {
@@ -38,11 +38,11 @@ SCRATCH = {
     "i2": ("sbuf", [128, 128], "bfloat16"),
     "go": ("sbuf", [128, 128], "bfloat16"),
     "um": ("sbuf", [128, 128], "bfloat16"),
+    "un": ("sbuf", [128, 128], "bfloat16"),
     "beta": ("sbuf", [128, 48], "bfloat16"),
-    "rt": ("sbuf", [128, 64], "float32"),
-    "rs": ("sbuf", [128, 64], "float32"),
+    "rt": ("sbuf", [128, 80], "float32"),
     "tr": ("sbuf", [128, 48], "float32"),
-    "qo": ("sbuf", [128, 4], "uint16"),
+    "qo": ("sbuf", [128, 6], "uint16"),
     "off": ("sbuf", [128, 8 * 192], "uint16"),
     "gat": ("sbuf", [128, 8 * 3072], "bfloat16"),
     "v": ("sbuf", [128, 8 * 192], "bfloat16"),
@@ -50,9 +50,8 @@ SCRATCH = {
     "rh": ("sbuf", [128, 8 * 192], HDT),
     "fire": ("sbuf", [128, 8 * 192], "bfloat16"),
     "t": ("sbuf", [128, 8 * 192], "bfloat16"),
-    "si": ("sbuf", [128, 8 * 16], "int32"),
-    "d": ("sbuf", [128, 8 * 16], "int32"),
-    "m": ("sbuf", [128, 8 * 64], "bfloat16"),
+    "si": ("sbuf", [128, 8 * 16], "float32"),
+    "m": ("sbuf", [128, 8 * 80], "bfloat16"),
     "e": ("sbuf", [128, 8 * 64], "bfloat16"),
     "sm": ("sbuf", [128, 8 * 48], "float32"),
     "idx": ("sbuf", [128, 8 * 16], "uint16"),
@@ -64,29 +63,25 @@ for _h in "AB":
     for _b in "XYZW":
         SCRATCH["p" + _b + _h] = ("psum", [128, 512], "float32")
 
-START = ["z1", "z2", "z3", "one", "kc", "qc", "beta", "rt", "rs", "tr", "kr", "qr", "qo", "dl", "ident", "ii", "cl", "ones",
-         "lb", "zz", "gt", "i2", "go", "um", "xm", "ldx", "lutA", "lutB", "plA", "plB", "plA2", "plB2", "polA", "polB",
-         "cvA", "cvB"]
+START = ["z1", "z2", "z3", "one", "kc", "qc", "beta", "rt", "rp", "tr", "kr", "qr", "qo", "dl", "ident", "ii", "cl", "ones",
+         "lb", "zz", "gt", "i2", "go", "um", "un", "xm", "ldx", "lutA", "lutB", "plA", "plB", "plA2", "plB2", "polA",
+         "polB", "cvA", "cvB"]
 ROLES = ["numE", "numO", "castE", "castO", "merge", "evac", "inc", "gathE", "gathF", "gathL", "gva", "gvb", "gvc", "gvd",
          "redE", "redF", "redV", "redL", "reluE", "reluO", "polE", "polO", "fireE", "fireO", "tE", "tO", "sfO", "cp",
-         "and", "eq", "scan", "rankE", "smax", "cidx", "scat", "own", "fill", "fin", "yev", "st"]
+         "eq", "scan", "rankE", "smax", "cidx", "scat", "own", "fill", "fin", "yev", "st"]
 SEMAPHORES = (["s_" + n for n in START] + ["r_" + r + x for r in ROLES for x in "AB"]
               + ["arr%d%s" % (k, x) for k in range(NP) for x in "AB"] + ["sentA", "sentB"])
 
 
 def plan(cores, me, topo):
-    out, far = {}, 0
-    for r in range(NR):
-        if r == me:
-            continue
+    far = [r for r in range(NR) if topo.die(cores[r]) != topo.die(cores[me])]
+    near = [r for r in range(NR) if r != me and r not in far]
+    first = {}
+    for i, r in enumerate(far):
         eng = topo.engines(cores[me], cores[r])
-        if topo.die(cores[r]) == topo.die(cores[me]):
-            out[r] = eng[1::2]
-        else:
-            quarter = len(eng) // 4
-            out[r] = eng[0::2][far * quarter:(far + 1) * quarter]
-            far += 1
-    return out
+        w = len(eng) // len(far)
+        first[r] = eng[i * w:(i + 1) * w]
+    return [first] + [{r: topo.engines(cores[me], cores[r])} for r in near]
 
 
 def graph(g, T, me, topo):
@@ -120,17 +115,17 @@ def graph(g, T, me, topo):
            lambda i=i: [V.tensor_copy(T.po[:, 128 * i:128 * i + 128], T.pob[:, 128 * i:128 * i + 128])])
     ops["lutA"]["soft"] = ["ldx"]
     ops["lutB"]["soft"] = ["lutA"]
-    st("z3", "v", "half2", 480, [], lambda: [V.memset(cz[:], 0.0), V.memset(T.d[:], 0)])
+    st("z3", "v", "half2", 480, [], lambda: [V.memset(cz[:], 0.0), V.memset(T.si[:], 0.0)])
     st("one", "v", "half", 16, [], lambda: [V.memset(T.one[:], 1.0)])
     st("kc", "g", "iota", 128, [], lambda: [iota(T.kc[:], [[1, 2], [64, 4], [2, 16]], 0, 0)])
     st("qc", "g", "iota", 128, [], lambda: [iota(T.qc[:], [[0, 8], [1, 16]], 0, 0)])
-    st("beta", "g", "iota", 48, [], lambda: [iota(T.beta[:], [[0, 12], [REG // 32, 4]], BASE // 32 - 64, 0)])
-    st("rt", "g", "iota", 64, [], lambda: [iota(T.rt[:], [[1, 4], [0, 16]], 0, 0)])
-    st("rs", "g", "iota", 64, [], lambda: [iota(T.rs[:], [[0, 4], [16, 16]], 0, 0)])
-    st("tr", "g", "iota", 48, [], lambda: [iota(T.tr[:], [[-16, 12], [4096, 4]], BASE, -1)])
+    st("beta", "g", "iota", 48, [], lambda: [iota(T.beta[:], [[0, 12], [REG // 8, 4]], BASE // 8 - 256, 0)])
+    st("rt", "g", "iota", 80, [], lambda: [iota(T.rt[:], [[1, 5], [0, 16]], 0, 0)])
+    st("rp", "v", "half", 5, ["rt"], lambda: [V.memset(T.rt[:, 15:80:16], 2.0 ** 30)])
+    st("tr", "g", "iota", 48, [], lambda: [iota(T.tr[:], [[-64, 12], [16384, 4]], 4 * BASE, -4)])
     st("kr", "p", "mm", 64, ["kc", "one"], lambda: [P.matmul(T.pWA[:, 0:2], T.kc[0:1, :], T.one[0:1, 0:2], True, True)])
-    st("qr", "p", "mm", 64, ["qc", "one"], lambda: [P.matmul(T.pWB[:, 0:4], T.qc[0:1, :], T.one[0:1, 0:4], True, True)])
-    st("qo", "v", "full", 4, ["qr"], lambda: [V.tensor_copy(T.qo[:], T.pWB[:, 0:4])])
+    st("qr", "p", "mm", 64, ["qc", "one"], lambda: [P.matmul(T.pWB[:, 0:6], T.qc[0:1, :], T.one[0:1, 0:6], True, True)])
+    st("qo", "v", "full", 6, ["qr"], lambda: [V.tensor_copy(T.qo[:], T.pWB[:, 0:6])])
     st("dl", "v", "half", 128, ["kr", "kc"],
        lambda: [V.tensor_scalar(T.dl[:], T.kc[:], T.pWA[:, 0:1], -1.0, A.subtract, A.mult)])
     st("ident", "v", "half", 128, ["dl"], lambda: [V.tensor_scalar(T.ident[:], T.dl[:], 0.0, None, A.is_equal)])
@@ -146,10 +141,11 @@ def graph(g, T, me, topo):
     st("i2", "v", "half", 128, ["dl"], lambda: [V.tensor_scalar(T.i2[:], T.dl[:], 0.0, 2048.0, A.is_equal, A.mult)])
     st("go", "v", "two", 128, ["gt", "ones"], lambda: [V.tensor_tensor(T.go[:], T.gt[:], T.ones[:], A.mult)])
     st("um", "v", "two", 128, ["go", "i2"], lambda: [V.tensor_tensor(T.um[:], T.i2[:], T.go[:], A.subtract)])
-    st("xm", "v", "half", 384, ["ldx"], lambda: [V.tensor_scalar(T.xm[:], T.xs[:], 0.0, 63.0, A.min, A.mult)])
+    st("un", "v", "half", 128, ["um"], lambda: [V.tensor_scalar(T.un[:], T.um[:], -1.0, None, A.mult)])
+    st("xm", "v", "half", 384, ["ldx"], lambda: [V.tensor_scalar(T.xm[:], T.xs[:], 0.0, -FILL, A.min, A.mult)])
 
-    engs = plan(T.cores, me, topo)
-    come = sum(len(plan(T.cores, a, topo)[me]) for a in range(NR) if a != me)
+    calls = plan(T.cores, me, topo)
+    come = sum(len(c[me]) for a in range(NR) if a != me for c in plan(T.cores, a, topo) if me in c)
 
     def half(k, i, X):
         n = lambda r, kk=k: "%s%d%s" % (r, kk, X)
@@ -253,27 +249,26 @@ def graph(g, T, me, topo):
             ro("sf" + E, "p", "mm", 512, [n("fire" + E)], lambda e=e: [[
                 P.matmul(pW[:, 0:12], lq(q), T.fire[:, c0 + q:c0 + 192:16], False, q == 15)
                 for q in range(e, 16, 2)][-1]], soft=[n("su")] if e == 0 else [n("sfE")], sem=(e == 1))
-        s0, m0, x0, W0 = 16 * j, 64 * j, 48 * j, WIN * j
-        ro("cp", "v", "full", 12, [n("sfO")], lambda: [
-            V.tensor_scalar(T.si[:, s0:s0 + 12], pW[:, 0:12], 16 * SHIFT, None, A.add)])
-        ro("and", "v", "full", 12, [n("cp"), "z3"], lambda: [
-            V.tensor_scalar(T.d[:, s0:s0 + 12], T.si[:, s0:s0 + 12], 1027, None, A.bitwise_and)])
-        ro("eq", "v", "gath", 64, [n("and"), "qo", "rt"], lambda: [
-            V.tensor_tensor(T.m[:, m0:m0 + 64], T.d[:, s0:s0 + 16].indirect(T.qo[:, 0:4]), T.rt[:], A.is_equal)])
-        ro("scan", "v", "full", 64, [n("eq"), "rs"], lambda: [
-            V.tensor_tensor_scan(T.e[:, m0:m0 + 64], T.rs[:], T.m[:, m0:m0 + 64], 0.0, A.min, A.add)])
+        s0, m0, e0, x0, W0 = 16 * j, 80 * j, 64 * j, 48 * j, WIN * j
+        ro("cp", "v", "full", 12, [n("sfO"), "z3"], lambda: [
+            V.tensor_scalar(T.si[:, s0:s0 + 12], pW[:, 0:12], 16 * SHIFT + 768 - 1.5, None, A.add)])
+        ro("eq", "v", "gath", 80, [n("cp"), "qo", "rp"], lambda: [
+            V.tensor_tensor(T.m[:, m0:m0 + 80], T.si[:, s0:s0 + 16].indirect(T.qo[:, 0:5]), T.rt[:], A.add)])
+        ro("scan", "v", "full", 64, [n("eq")], lambda: [
+            V.tensor_tensor_scan(T.e[:, e0:e0 + 64], T.m[:, m0 + 16:m0 + 80], T.m[:, m0:m0 + 64], 0.0, A.add,
+                                 A.subtract)])
         ro("rank0", "p", "mm", 64, [n("cp"), "ones", "beta"], lambda: [
             P.matmul(pW[:, 64:112], T.ones[:], T.beta[:], True, False)], sem=False)
-        ro("rankM", "p", "mm", 256, [n("eq"), "um"], lambda: [[
-            P.matmul(pW[:, 64 + r:112:4], T.um[:], T.m[:, m0 + 16 * r:m0 + 16 * r + 12], False, False)
-            for r in range(4)][-1]], soft=[n("rank0")], sem=False)
+        ro("rankM", "p", "mm", 512, [n("eq"), "um", "un"], lambda: [[
+            P.matmul(pW[:, 64 + r:112:4], u[:], T.m[:, m0 + 16 * (w - r):m0 + 16 * (w - r) + 12], False, False)
+            for r in range(4) for u, w in ((T.um, 4), (T.un, 3))][-1]], soft=[n("rank0")], sem=False)
         ro("rankE", "p", "mm", 256, [n("scan")], lambda: [[
-            P.matmul(pW[:, 64 + r:112:4], T.ones[:], T.e[:, m0 + 16 * r:m0 + 16 * r + 12], False, r == 3)
+            P.matmul(pW[:, 64 + r:112:4], T.ones[:], T.e[:, e0 + 16 * (3 - r):e0 + 16 * (3 - r) + 12], False, r == 3)
             for r in range(4)][-1]], soft=[n("rankM")])
         ro("smax", "v", "full", 48, [n("rankE"), "tr"], lambda: [
             V.tensor_tensor_scan(T.sm[:, x0:x0 + 48], T.tr[:], pW[:, 64:112], 1.0e6, A.min, A.max)])
         ro("cidx", "v", "full", 12, [n("smax")], lambda: [
-            V.tensor_scalar(T.idx[:, s0:s0 + 12], T.sm[:, x0 + 3:x0 + 48:4], -1.0, None, A.add)])
+            V.tensor_scalar(T.idx[:, s0:s0 + 12], T.sm[:, x0 + 3:x0 + 48:4], 0.25, -1.0, A.mult, A.add)])
         reg = lambda r: T.win[:, W0 + BASE + REG * r:W0 + BASE + REG * r + CAP]
         ro("fill", "g", "iota4", CAP, prev("scat"), lambda: [iota(reg(r), [[0, CAP]], int(FILL), 0) for r in range(NR)],
            soft=prev("own"))
@@ -283,12 +278,14 @@ def graph(g, T, me, topo):
         mine = T.land[:, 384 * j + CAP * me:384 * j + CAP * me + CAP]
 
         def send():
-            tr = []
-            for r in sorted(engs):
-                rid, pid, _ = topo.addr(T.cores[r])
-                tr.append(RemoteDMATransfer(dst_ids=[DstId(rid=rid, pnc=pid)], dma_engine_mask=sum(1 << e for e in engs[r]),
-                                            remote_sem=T.sem["arr%d%s" % (k, X)], src=reg(r), dst=mine))
-            g.remote_dma_fused(tr, local_sem=T.sem["sent" + X])
+            for call in calls:
+                tr = []
+                for r in sorted(call):
+                    rid, pid, _ = topo.addr(T.cores[r])
+                    tr.append(RemoteDMATransfer(dst_ids=[DstId(rid=rid, pnc=pid)],
+                                                dma_engine_mask=sum(1 << e for e in call[r]),
+                                                remote_sem=T.sem["arr%d%s" % (k, X)], src=reg(r), dst=mine))
+                g.remote_dma_fused(tr, local_sem=T.sem["sent" + X])
             return []
 
         ro("send", "g", "send", 0, [n("scat")], send, sem=False)
@@ -299,7 +296,7 @@ def graph(g, T, me, topo):
     for k in range(NP + 1):
         for i, X in enumerate("AB"):
             half(k, i, X)
-    return ops, sum(len(e) for e in engs.values())
+    return ops, sum(len(e) for c in calls for e in c.values())
 
 
 def topo_order(ops):
@@ -312,11 +309,34 @@ def topo_order(ops):
     return out
 
 
+def waits(ops):
+    order = {q: ORDER[q].split() for q in ORDER}
+    at, known, done, need = {q: 0 for q in order}, {q: set() for q in order}, {}, {}
+    for n in ops:
+        if ops[n]["q"] is None:
+            done[n] = {n}
+    moved = True
+    while moved:
+        moved = False
+        for q in order:
+            while at[q] < len(order[q]) and all(d in done for d in ops[order[q][at[q]]]["hard"]):
+                n = order[q][at[q]]
+                hard = ops[n]["hard"]
+                need[n] = [d for d in hard if d not in known[q] and not any(d != e and d in done[e] for e in hard)]
+                for d in hard:
+                    known[q] |= done[d]
+                done[n] = known[q] | {n}
+                at[q] += 1
+                moved = True
+    return order, need
+
+
 def rank_program(g, core, T, topo):
     me = T.rank_of(core)
     if me is None:
         return
     ops, sent = graph(g, T, me, topo)
+    order, need = waits(ops)
     queue = {"v": g.vector, "s": g.scalar, "p": g.tensor, "y": g.sync, "g": g}
     many = {"half2": 2, "iota4": 4}
     total, mark = {}, {}
@@ -327,16 +347,13 @@ def rank_program(g, core, T, topo):
             total[o["sem"]] = total.get(o["sem"], 0) + k * o["inc"]
             mark[n] = total[o["sem"]]
     waited = {}
-    for q in ORDER:
-        seen = {}
-        for n in ORDER[q].split():
+    for q in order:
+        for n in order[q]:
             o = ops[n]
-            for d in o["hard"]:
+            for d in need[n]:
                 s = ops[d]["sem"]
-                if seen.get(s, 0) < mark[d]:
-                    queue[q].wait_ge(T.sem[s], mark[d])
-                    seen[s] = mark[d]
-                    waited[s] = max(waited.get(s, 0), mark[d])
+                queue[q].wait_ge(T.sem[s], mark[d])
+                waited[s] = max(waited.get(s, 0), mark[d])
             for ins in o["emit"]():
                 if o["sem"]:
                     ins.then_inc(T.sem[o["sem"]], o["inc"])

@@ -5,22 +5,35 @@ A = AluOpType
 F = ActivationFunctionType
 NP, CAP, NR = 4, 96, 4
 WIN, BASE, REG = 1856, 320, 384
-FILL, SHIFT = -1024.0, 6.125
+FILL, SHIFT = 1024.0, 6.125
+TAB = 4112
+SEG = 13
 HDT = "float16"
-NV = [[[48, 48], [24, 24, 24]], [[24, 24, 24], [24, 24, 24]], [[24, 24, 24], [24, 24, 24]], [[24, 24, 24], [48, 48]]]
-ES = [[48, 48]] * 4
-JOINT = [[1, 1]] * 4
-
-ORDER = {
-    "y": "ldx lutA lutB st4A st4B",
-    "g": "kc qc rt beta tr fill0A fill0B send0A own0A fill1A send0B own0B fill1B send1A own1A fill2A send1B own1B fill2B send2A own2A fill3A send2B own2B fill3B send3A own3A send3B own3B",
-    "v": "z1 one z2 z3 dl cl ident ii gt zz ones i2 lb go um un qo rp xm castE0A castO0A evac0A castE0B cvA evac0B castO0B cvB gvb0A gva0A inc0A inc0B reluE0A gvc0B reluO0A fireE0A fireO0A gvb0B cp0A eq0A tE0A scan0A gva0B smax0A tO0A cidx0A reluE0B scat0A reluO0B fireE0B fireO0B tO0B cp0B eq0B scan0B tE0B smax0B cidx0B scat0B castE1A castO1A gvb1A gvc1A gva1A reluO1A castO1B castE1B gvc1B reluE1A inc1A fireE1A fireO1A gva1B cp1A eq1A tO1A scan1A gvb1B smax1A tE1A cidx1A reluE1B scat1A reluO1B inc1B fireE1B fireO1B tO1B cp1B eq1B scan1B tE1B smax1B cidx1B scat1B castE2A castO2A gva2A inc2A gvc2A gvb2A castO2B castE2B gvc2B reluE2A gvb2B reluO2A fireE2A fireO2A gva2B cp2A eq2A scan2A tE2A tO2A smax2A cidx2A scat2A reluO2B reluE2B inc2B fireE2B fireO2B cp2B eq2B tE2B scan2B tO2B smax2B cidx2B scat2B castE3A castO3A gvc3A gvb3A gva3A castO3B castE3B gva3B reluE3A reluO3A fireE3A fireO3A gvb3B inc3A cp3A eq3A scan3A tE3A reluE3B reluO3B tO3A inc3B smax3A fireE3B cidx3A fireO3B scat3A cp3B eq3B tO3B scan3B tE3B smax3B cidx3B scat3B yev4A yev4B",
-    "s": "plA plB polA polB plA2 plB2 gathE0A gathF0A gathE0B gathF0B gathL0B gathE1A evac1A gathL1A gathF1A evac1B gathE1B gathF1B gathL1B evac2A gathE2A gathF2A gathL2A gathE2B gathL2B evac2B gathF2B evac3A gathE3A gathF3A gathL3A gathE3B gathF3B evac3B",
-    "p": "kr qr numE0A numO0A merge0A numE0B merge0B numO0B sua0A su0A redEa0A redE0A redFa0A redF0A redVa0A redV0A sua0B polE0A polO0A su0B sfE0A sfO0A redEa0B redE0B rank00A rankM0A rankE0A redFa0B redF0B redVa0B redV0B polE0B polO0B sfE0B sfO0B rank00B rankM0B rankE0B numE1A numO1A merge1A redEa1A redE1A redVa1A redV1A numO1B numE1B merge1B redFa1A redF1A sua1A polE1A polO1A su1A sfE1A sfO1A redEa1B redE1B rank01A rankM1A rankE1A redFa1B redF1B redVa1B redV1B polE1B sua1B polO1B su1B sfE1B sfO1B rank01B rankM1B rankE1B numE2A merge2A numO2A sua2A redEa2A redE2A numO2B numE2B redFa2A redF2A redVa2A redV2A polE2A su2A polO2A sfE2A sfO2A merge2B redEa2B redE2B rank02A rankM2A rankE2A redVa2B redV2B redFa2B redF2B sua2B polE2B polO2B su2B sfE2B sfO2B rank02B rankM2B rankE2B numE3A merge3A numO3A sua3A redEa3A redE3A su3A numO3B numE3B redFa3A redF3A redVa3A redV3A merge3B polE3A polO3A redEa3B redE3B sfE3A sfO3A redFa3B redF3B redVa3B redV3B rank03A rankM3A rankE3A polE3B polO3B sua3B su3B sfE3B sfO3B rank03B rankM3B rankE3B fin4A fin4B",
-}
+PIECES = ([[{'o': 's24 v24', 'n': 's48', 'e': 's12 v36', 'f': 'v24 s24'},
+            {'o': 's12 s24 s12', 'n': 's36 v12', 'e': 's36 s12', 'f': 's12 s24 s12'}]]
+          + [[{'o': 's48', 'n': 'v12 s36', 'e': 'v24 s24', 'f': 's36 v12'},
+              {'o': 's36 v12', 'n': 'v12 s36', 'e': 's48', 'f': 'v12 s36'}]] * (NP - 1))
+LOADS = {"s": "ldx plA", "y": "lutA plB polA lutB polB plA2 plB2"}
+APART = [0, 1, 1, 1]
+QUICK = "f"
+RANKM = True
+JOINF = False
+ONE = True
+TIME = {
+    '0A': 'fill0_ 0.91 fill1_ 1.22 fill2_ 1.54 numf 2.11 numo 2.35 numn 2.48 castf 2.55 mergen 2.6 casto 2.77 castn 2.83 ge0 2.85 ge1 2.89 fill3_ 3.01 go0 3.13 mergef 3.55 gn0 3.67 go1 3.81 redea 4.04 rede 4.28 gf0 4.5 evacf 4.69 gf1 4.87 redna 4.89 relue 5.03 incf 5.09 redn 5.25 redfa 5.62 relun 5.82 redf 5.87 pole 6.11 poln 6.17 su0 6.27 reluf 6.31 firee 6.37 firen 6.47 su8 6.51 te 6.64 tn 6.76 polf 6.76 si1 6.79 firef 6.99 sfe 7.05 sff 7.3 floor 7.74 rank 7.88 scan 8.25 rank0 8.25 rankm 8.28 tf 8.31 smax 8.85 cidx 9.11 scat 9.37 sendn 10.14 sendf 12.34',
+    '0B': 'fill0_ 0.6 fill1_ 2.07 fill2_ 2.38 fill3_ 2.7 numf 2.93 mergen 3.18 numn 3.43 mergef 3.73 castn 3.75 numo 3.92 castf 4.41 gf0 5.41 casto 5.43 go0 5.71 gf1 6 go1 6.52 gf2 6.82 gn0 7.43 rank 7.75 go2 8.21 gn1 8.4 ge0 8.5 redfa 8.65 redf 8.89 redna 9.14 evacf 9.27 ge1 9.46 redn 9.51 reluf 9.94 redea 9.96 relun 10.07 incf 10.17 rede 10.2 poln 10.46 relue 10.65 firen 10.75 pole 10.91 polf 10.97 su0 11 firee 11.17 firef 11.23 tn 11.29 su8 11.31 si1 11.56 te 11.57 sfe 11.83 sff 12.08 floor 12.52 tf 12.83 scan 13.97 rank0 14.02 rankm 14.05 smax 14.71 cidx 15.07 scat 15.33 sendn 16.11 sendf 16.51',
+    'A': 'numo 0.85 casto 1.11 go0 1.37 fill0_ 1.91 numn 2.01 fin 2.17 fill1_ 2.22 castn 2.27 gn0 2.53 gn1 2.53 fill2_ 2.54 mergen 2.79 numf 2.91 mergef 3.04 redoa 3.13 castf 3.3 ge0 3.59 ge1 3.59 redo 3.89 gf0 4.12 redna 4.14 redea 4.39 gf1 4.45 yev 4.58 rede 4.63 redn 4.88 evacf 4.89 st 4.96 redfa 5.12 relun 5.33 redf 5.37 incf 5.42 relue 5.51 poln 5.71 pole 5.8 reluf 5.81 si1 5.86 firen 6 firee 6.09 polf 6.11 tn 6.29 fill3_ 6.33 te 6.38 firef 6.44 sfe 6.64 sff 6.89 floor 7.37 scan 7.88 rank0 7.88 rankm 7.91 tf 7.94 rank 8.16 smax 8.48 cidx 8.74 scat 9 sendn 9.78 sendf 10.18',
+    'B': 'numo 0.88 casto 1.14 go0 1.41 go1 1.78 numn 1.79 fin 1.79 castn 2.08 yev 2.17 gn0 2.34 gn1 2.34 numf 2.41 mergen 2.53 st 2.55 mergef 2.65 redoa 2.74 castf 2.95 evacf 3.11 ge0 3.29 gf0 3.3 redo 3.55 redna 3.79 redn 4.04 incf 4.07 gf1 4.31 si1 4.36 redea 4.61 relun 4.85 rede 4.85 poln 5.16 redfa 5.28 relue 5.3 firen 5.45 redf 5.52 tn 5.74 pole 5.77 fill0_ 5.85 reluf 5.97 firee 6.03 polf 6.23 te 6.29 firef 6.46 sfe 6.55 sff 6.8 fill1_ 7.1 floor 7.24 fill2_ 7.41 fill3_ 7.73 scan 7.75 rank0 7.75 rankm 7.78 rank 8.02 smax 8.37 tf 8.44 cidx 8.64 scat 9 sendn 9.78 sendf 10.18',
+    '': 'z0 0 ldx 0 lutA 0 kc 0 plA 0.05 plB 0.1 z3 0.12 polA 0.15 lutB 0.25 z1 0.35 polB 0.35 tr 0.37 plA2 0.45 plB2 0.5 one 0.53 z2 0.6 kr 0.8 dl 1.03 xm 1.28 cl 1.47 ident 1.53 i2 1.59 ones 1.73 beta 1.85 lt 1.97 ii 2.03 lb 2.65 cvA 4.35 go 5.19 rp 6.56 cvB 7.05 ua 7.11 ub 7.56 zz 10.26'}
+OFFS = [0, 0, 10.59, 15.32, 19.57, 24.3, 28.55, 33.15, 38.15, 42.75]
+SLACK = 0.5
+LEAD = [3.0, 3.0, 3.0, 3.0, 3.0]
+BIAS = {}
+CYC, PEC, GATH, SCAT, HOP = 1.0e-3, 0.5e-3, 1.3e-3, 3.0e-3, 0.18
+DMA0, DMAKB, CALL, NEAR, FAR, FIRST = 1.0, 0.002, 0.4, 1.3, 1.9, 1.5
 
 SCRATCH = {
-    "lutw": ("sbuf", [128, 2 * 4096], "bfloat16"),
+    "lutw": ("sbuf", [128, 2 * TAB], "bfloat16"),
     "xs": ("sbuf", [128, 384], "bfloat16"),
     "xm": ("sbuf", [128, 384], "bfloat16"),
     "plb": ("sbuf", [128, 320], "bfloat16"),
@@ -34,24 +47,20 @@ SCRATCH = {
     "ident": ("sbuf", [128, 128], "bfloat16"),
     "cl": ("sbuf", [128, 128], "bfloat16"),
     "ones": ("sbuf", [128, 128], "bfloat16"),
-    "gt": ("sbuf", [128, 128], "bfloat16"),
+    "lt": ("sbuf", [128, 128], "bfloat16"),
     "i2": ("sbuf", [128, 128], "bfloat16"),
     "go": ("sbuf", [128, 128], "bfloat16"),
-    "um": ("sbuf", [128, 128], "bfloat16"),
-    "un": ("sbuf", [128, 128], "bfloat16"),
+    "ua": ("sbuf", [128, 128], "bfloat16"),
+    "ub": ("sbuf", [128, 128], "bfloat16"),
     "beta": ("sbuf", [128, 48], "bfloat16"),
-    "rt": ("sbuf", [128, 80], "float32"),
     "tr": ("sbuf", [128, 48], "float32"),
-    "qo": ("sbuf", [128, 6], "uint16"),
     "off": ("sbuf", [128, 8 * 192], "uint16"),
     "gat": ("sbuf", [128, 8 * 3072], "bfloat16"),
     "v": ("sbuf", [128, 8 * 192], "bfloat16"),
     "inc": ("sbuf", [128, 8 * 192], "bfloat16"),
     "rh": ("sbuf", [128, 8 * 192], HDT),
-    "fire": ("sbuf", [128, 8 * 192], "bfloat16"),
     "t": ("sbuf", [128, 8 * 192], "bfloat16"),
-    "si": ("sbuf", [128, 8 * 16], "float32"),
-    "m": ("sbuf", [128, 8 * 80], "bfloat16"),
+    "m": ("sbuf", [128, 2 * 5 * SEG], "bfloat16"),
     "e": ("sbuf", [128, 8 * 64], "bfloat16"),
     "sm": ("sbuf", [128, 8 * 48], "float32"),
     "idx": ("sbuf", [128, 8 * 16], "uint16"),
@@ -63,254 +72,351 @@ for _h in "AB":
     for _b in "XYZW":
         SCRATCH["p" + _b + _h] = ("psum", [128, 512], "float32")
 
-START = ["z1", "z2", "z3", "one", "kc", "qc", "beta", "rt", "rp", "tr", "kr", "qr", "qo", "dl", "ident", "ii", "cl", "ones",
-         "lb", "zz", "gt", "i2", "go", "um", "un", "xm", "ldx", "lutA", "lutB", "plA", "plB", "plA2", "plB2", "polA",
-         "polB", "cvA", "cvB"]
-ROLES = ["numE", "numO", "castE", "castO", "merge", "evac", "inc", "gathE", "gathF", "gathL", "gva", "gvb", "gvc", "gvd",
-         "redE", "redF", "redV", "redL", "reluE", "reluO", "polE", "polO", "fireE", "fireO", "tE", "tO", "sfO", "cp",
-         "eq", "scan", "rankE", "smax", "cidx", "scat", "own", "fill", "fin", "yev", "st"]
+START = ["z0", "z1", "z2", "z3", "one", "kc", "beta", "rp", "tr", "kr", "dl", "ident", "ii", "cl", "ones", "lb", "zz",
+         "lt", "i2", "go", "ua", "ub", "xm", "ldx", "lutA", "lutB", "plA", "plB", "plA2", "plB2", "polA", "polB",
+         "cvA", "cvB"]
+ROLES = ([r + b for r in ("num", "cast") for b in "onf"]
+         + ["g" + b + str(p) for b, most in zip("onef", (3, 3, 3, 3)) for p in range(most)]
+         + [r + b for r in ("merge", "evac", "inc") for b in "nf"]
+         + [r + b for r in ("red", "relu", "pol", "fire", "t") for b in "nef"]
+         + ["sff", "floor", "scan", "rank", "smax", "cidx", "scat", "fill", "st"])
 SEMAPHORES = (["s_" + n for n in START] + ["r_" + r + x for r in ROLES for x in "AB"]
-              + ["arr%d%s" % (k, x) for k in range(NP) for x in "AB"] + ["sentA", "sentB"])
+              + ["arr%s%d%s" % (b, k, x) for b in "nf" for k in range(NP) for x in "AB"] + ["sentA", "sentB"])
 
 
-def plan(cores, me, topo):
+def sides(cores, me, topo):
     far = [r for r in range(NR) if topo.die(cores[r]) != topo.die(cores[me])]
-    near = [r for r in range(NR) if r != me and r not in far]
-    first = {}
-    for i, r in enumerate(far):
-        eng = topo.engines(cores[me], cores[r])
-        w = len(eng) // len(far)
-        first[r] = eng[i * w:(i + 1) * w]
-    return [first] + [{r: topo.engines(cores[me], cores[r])} for r in near]
+    return [r for r in range(NR) if r != me and r not in far][0], far
 
 
 def graph(g, T, me, topo):
     ops = {}
     V, S, P = g.vector, g.scalar, g.tensor
+    near, far = sides(T.cores, me, topo)
+    cyc = lambda n, calls=1: calls * CYC * max(64, n)
+    pe = lambda n, calls: calls * PEC * max(64, n)
+    gp = lambda n: 0.13 + 2 * CYC * n
 
-    def op(name, q, kind, n, hard, emit, soft=(), sem=None, inc=1):
-        ops[name] = dict(q=q, kind=kind, n=n, hard=list(hard), soft=list(soft), emit=emit, sem=sem, inc=inc)
+    def op(name, q, dur, hard, emit, soft=(), sem=None, inc=1, calls=1, lat=None):
+        ops[name] = dict(q=q, dur=dur, hard=list(hard), soft=list(soft), emit=emit, sem=sem, inc=inc, calls=calls,
+                         lat=dur if lat is None else lat)
 
-    def st(name, q, kind, n, hard, emit, inc=1):
-        op(name, q, kind, n, hard, emit, sem="s_" + name, inc=inc)
+    def st(name, q, dur, hard, emit, calls=1):
+        op(name, q, dur, hard, emit, sem="s_" + name, calls=calls)
+
+    def load(name, q, kb, hard, emit, calls=1, soft=()):
+        op(name, q, 0.05 * calls, hard, emit, soft, "s_" + name, 16, calls, DMA0 + DMAKB * kb)
 
     II, LB, ZZ = 0, 192, 336
     cz = T.cz
     iota = lambda o, pat, b, cm: g.iota(o, pat, b, cm, allow_small_or_imprecise_dtypes=True)
-    st("z1", "v", "half", 320, [], lambda: [V.memset(T.plb[:], 0.0)])
-    st("z2", "v", "half", 256, [], lambda: [V.memset(T.pob[:], 0.0)])
-    st("ldx", "y", "dma", 96, [], lambda: [g.sync.dma_start(T.xs[:], T.x[:])], inc=16)
+    st("z0", "v", cyc(8, 2), [], lambda: [V.memset(T.lutw[:, TAB * i + 4096:TAB * i + TAB], 0.0) for i in range(2)], 2)
+    st("z1", "v", cyc(32, 3), [], lambda: [V.memset(T.plb[:, c:c + 64], 0.0) for c in (0, 128, 256)], 3)
+    st("z2", "v", cyc(32, 4), [], lambda: [V.memset(T.pob[64 * h:64 * h + 64, c - 64 * h:c - 64 * h + 64], 0.0)
+                                           for h in range(2) for c in (64, 192)], 4)
+    queue = {"s": S, "y": g.sync}
+    src = {"ldx": lambda D: [D.dma_start(T.xs[:], T.x[:])]}
     for i, X in enumerate("AB"):
-        st("lut" + X, "y", "dma", 1024, [], lambda i=i: [
-            g.sync.dma_start(T.lutw[64 * h:64 * h + 64, 4096 * i:4096 * i + 4096], T.lut[64 * i:64 * i + 64, :])
-            for h in range(2)], inc=16)
+        src["lut" + X] = lambda D, i=i: [
+            D.dma_start(T.lutw[64 * h:64 * h + 64, TAB * i:TAB * i + 4096], T.lut[64 * i:64 * i + 64, :])
+            for h in range(2)]
         for nm, h in (("pl" + X, i), ("pl" + X + "2", 1 - i)):
-            st(nm, "s", "dma", 8, ["z1"], lambda i=i, h=h: [
-                S.dma_start(T.plb[64 * h:64 * h + 64, 64 + 128 * i:128 + 128 * i],
-                            T.pl[64 * i:64 * i + 64, 64 * i:64 * i + 64])], inc=16)
-        st("pol" + X, "s", "dma", 16, ["z2"], lambda i=i: [
-            S.dma_start(T.pob[64 * h:64 * h + 64, 128 * i + 64 * h:128 * i + 64 * h + 64],
-                        T.pol[64 * i:64 * i + 64, 64 * i:64 * i + 64]) for h in range(2)], inc=16)
-        st("cv" + X, "v", "half", 128, ["pol" + X],
-           lambda i=i: [V.tensor_copy(T.po[:, 128 * i:128 * i + 128], T.pob[:, 128 * i:128 * i + 128])])
-    ops["lutA"]["soft"] = ["ldx"]
-    ops["lutB"]["soft"] = ["lutA"]
-    st("z3", "v", "half2", 480, [], lambda: [V.memset(cz[:], 0.0), V.memset(T.si[:], 0.0)])
-    st("one", "v", "half", 16, [], lambda: [V.memset(T.one[:], 1.0)])
-    st("kc", "g", "iota", 128, [], lambda: [iota(T.kc[:], [[1, 2], [64, 4], [2, 16]], 0, 0)])
-    st("qc", "g", "iota", 128, [], lambda: [iota(T.qc[:], [[0, 8], [1, 16]], 0, 0)])
-    st("beta", "g", "iota", 48, [], lambda: [iota(T.beta[:], [[0, 12], [REG // 8, 4]], BASE // 8 - 256, 0)])
-    st("rt", "g", "iota", 80, [], lambda: [iota(T.rt[:], [[1, 5], [0, 16]], 0, 0)])
-    st("rp", "v", "half", 5, ["rt"], lambda: [V.memset(T.rt[:, 15:80:16], 2.0 ** 30)])
-    st("tr", "g", "iota", 48, [], lambda: [iota(T.tr[:], [[-64, 12], [16384, 4]], 4 * BASE, -4)])
-    st("kr", "p", "mm", 64, ["kc", "one"], lambda: [P.matmul(T.pWA[:, 0:2], T.kc[0:1, :], T.one[0:1, 0:2], True, True)])
-    st("qr", "p", "mm", 64, ["qc", "one"], lambda: [P.matmul(T.pWB[:, 0:6], T.qc[0:1, :], T.one[0:1, 0:6], True, True)])
-    st("qo", "v", "full", 6, ["qr"], lambda: [V.tensor_copy(T.qo[:], T.pWB[:, 0:6])])
-    st("dl", "v", "half", 128, ["kr", "kc"],
+            src[nm] = lambda D, i=i, h=h: [D.dma_start(T.plb[64 * h:64 * h + 64, 64 + 128 * i:128 + 128 * i],
+                                                       T.pl[64 * i:64 * i + 64, 64 * i:64 * i + 64])]
+        src["pol" + X] = lambda D, i=i: [
+            D.dma_start(T.pob[64 * h:64 * h + 64, 128 * i + 64 * h:128 * i + 64 * h + 64],
+                        T.pol[64 * i:64 * i + 64, 64 * i:64 * i + 64]) for h in range(2)]
+        st("cv" + X, "v", cyc(64), ["pol" + X, "z2"], lambda i=i: [
+            V.tensor_scalar(T.po[:, 128 * i:128 * i + 128], T.pob[:, 128 * i:128 * i + 128], -16.0, None, A.mult)])
+    for q in LOADS:
+        kb, last = 0, []
+        for nm in LOADS[q].split():
+            kb += 1024 if nm[:3] == "lut" else 96
+            load(nm, q, kb, [], lambda nm=nm, q=q: src[nm](queue[q]), 2 if nm[:3] in ("lut", "pol") else 1, last)
+            last = [nm]
+    st("z3", "v", cyc(240), [], lambda: [V.memset(cz[:], 0.0)])
+    st("one", "v", cyc(8), [], lambda: [V.memset(T.one[:], 1.0)])
+    st("kc", "g", gp(128), [], lambda: [iota(T.kc[:], [[1, 2], [64, 4], [2, 16]], 0, 0)])
+    st("beta", "g", gp(48), [], lambda: [iota(T.beta[:], [[0, 12], [REG // 8, 4]], BASE // 8 - 256, 0)])
+    st("rp", "v", cyc(5), [], lambda: [V.memset(T.m[:, 0:10 * SEG:SEG], 2.0 ** 30)])
+    st("tr", "g", gp(48), [], lambda: [iota(T.tr[:], [[-64, 12], [16384, 4]], 4 * BASE - 4, -4)])
+    st("kr", "p", pe(2, 1), ["kc", "one"], lambda: [P.matmul(T.pWA[:, 0:2], T.kc[0:1, :], T.one[0:1, 0:2], True, True)])
+    st("dl", "v", cyc(128), ["kr", "kc"],
        lambda: [V.tensor_scalar(T.dl[:], T.kc[:], T.pWA[:, 0:1], -1.0, A.subtract, A.mult)])
-    st("ident", "v", "half", 128, ["dl"], lambda: [V.tensor_scalar(T.ident[:], T.dl[:], 0.0, None, A.is_equal)])
-    st("ii", "v", "two", 64, ["ident", "z3"],
+    st("ident", "v", cyc(64), ["dl"], lambda: [V.tensor_scalar(T.ident[:], T.dl[:], 0.0, None, A.is_equal)])
+    st("ii", "v", cyc(128), ["ident", "z3"],
        lambda: [V.tensor_tensor(cz[:, II + 64:II + 128], T.ident[:, 0:64], T.ident[:, 64:128], A.add)])
-    st("cl", "v", "half", 128, ["dl"], lambda: [V.tensor_scalar(T.cl[:], T.dl[:], -31.5, 31.5, A.max, A.min)])
-    st("ones", "v", "two", 128, ["cl", "dl"], lambda: [V.tensor_tensor(T.ones[:], T.cl[:], T.dl[:], A.is_equal)])
-    st("lb", "v", "half2", 8, ["ones", "z3"], lambda: [
+    st("cl", "v", cyc(64), ["dl"], lambda: [V.tensor_scalar(T.cl[:], T.dl[:], -31.5, 31.5, A.max, A.min)])
+    st("ones", "v", cyc(256), ["cl", "dl"], lambda: [V.tensor_tensor(T.ones[:], T.cl[:], T.dl[:], A.is_equal)])
+    st("lb", "v", cyc(4, 2), ["ones", "z3"], lambda: [
         V.tensor_copy(cz[64 * h:64 * h + 64, LB + 15 + 64 * h:LB + 79 + 64 * h:16],
-                      T.ones[64 * h:64 * h + 64, 64 * h:64 * h + 64:16]) for h in range(2)])
-    st("zz", "v", "half", 64, ["ii", "z3"], lambda: [V.tensor_copy(cz[:, ZZ + 1:ZZ + 129:2], cz[:, II + 64:II + 128])])
-    st("gt", "v", "half", 128, ["dl"], lambda: [V.tensor_scalar(T.gt[:], T.dl[:], 0.0, None, A.is_gt)])
-    st("i2", "v", "half", 128, ["dl"], lambda: [V.tensor_scalar(T.i2[:], T.dl[:], 0.0, 2048.0, A.is_equal, A.mult)])
-    st("go", "v", "two", 128, ["gt", "ones"], lambda: [V.tensor_tensor(T.go[:], T.gt[:], T.ones[:], A.mult)])
-    st("um", "v", "two", 128, ["go", "i2"], lambda: [V.tensor_tensor(T.um[:], T.i2[:], T.go[:], A.subtract)])
-    st("un", "v", "half", 128, ["um"], lambda: [V.tensor_scalar(T.un[:], T.um[:], -1.0, None, A.mult)])
-    st("xm", "v", "half", 384, ["ldx"], lambda: [V.tensor_scalar(T.xm[:], T.xs[:], 0.0, -FILL, A.min, A.mult)])
+                      T.ones[64 * h:64 * h + 64, 64 * h:64 * h + 64:16]) for h in range(2)], 2)
+    st("zz", "v", cyc(32), ["ii", "z3"], lambda: [V.tensor_copy(cz[:, ZZ + 1:ZZ + 129:2], cz[:, II + 64:II + 128])])
+    st("lt", "v", cyc(64), ["dl"], lambda: [V.tensor_scalar(T.lt[:], T.dl[:], 0.0, None, A.is_lt)])
+    st("i2", "v", cyc(64), ["dl"], lambda: [V.tensor_scalar(T.i2[:], T.dl[:], 0.0, 2048.0, A.is_equal, A.mult)])
+    st("go", "v", cyc(256), ["lt", "ones"], lambda: [V.tensor_tensor(T.go[:], T.lt[:], T.ones[:], A.mult)])
+    st("ua", "v", cyc(256), ["go", "i2"], lambda: [V.tensor_tensor(T.ua[:], T.i2[:], T.go[:], A.add)])
+    if RANKM:
+        st("ub", "v", cyc(64), ["ua"], lambda: [V.tensor_scalar(T.ub[:], T.ua[:], -1.0, None, A.mult)])
+    else:
+        st("ub", "v", cyc(256), ["ua", "ones"], lambda: [V.tensor_tensor(T.ub[:], T.ones[:], T.ua[:], A.subtract)])
+    made = lambda B: ("fire" if B in QUICK else "t") + ("f" if JOINF and B == "e" else B)
+    st("xm", "v", cyc(192), ["ldx"], lambda: [V.tensor_scalar(T.xm[:], T.xs[:], 0.0, -FILL, A.min, A.mult)])
 
-    calls = plan(T.cores, me, topo)
-    come = sum(len(c[me]) for a in range(NR) if a != me for c in plan(T.cores, a, topo) if me in c)
+    lo, fo = 48 * min(me, near), 48 * min(far)
 
     def half(k, i, X):
         n = lambda r, kk=k: "%s%d%s" % (r, kk, X)
         j = 2 * k + i
 
-        def ro(r, q, kind, sz, hard, emit, soft=(), sem=True, inc=1):
-            op(n(r), q, kind, sz, hard, emit, soft, ("r_" + r + X) if sem else None, inc)
+        def ro(r, q, dur, hard, emit, soft=(), sem=True, calls=1, role=None):
+            op(n(r), q, dur, hard, emit, soft, ("r_" + (role or r) + X) if sem else None, 1, calls)
+
+        def group(mms):
+            return [[P.matmul(o, l, r, u == 0, u == len(mms) - 1) for u, (o, l, r) in enumerate(mms)][-1]]
 
         prev = lambda *rs: [n(r, k - 1) for r in rs] if k > 0 else []
         pX, pY, pZ, pW = (T["p" + b + X] for b in "XYZW")
-        pl = lambda h, a=0, b=128: T.plb[a:b, 64 + 128 * i - 64 * h:192 + 128 * i - 64 * h]
-        ii = lambda h, a=0, b=128: cz[a:b, II + 64 - 64 * h:II + 192 - 64 * h]
-        L0 = 384 * (j - 2)
-        src = prev("arr", "own")
+        a, b = (64 * i, 64 * i + 64) if k == 0 else (0, 128)
+        pl = lambda h: T.plb[a:b, 64 + 128 * i - 64 * h:192 + 128 * i - 64 * h]
+        ii = lambda h: cz[a:b, II + 64 - 64 * h:II + 192 - 64 * h]
+
+        def slots(s0, s1, step):
+            if k == 0:
+                return [T.xs[a:b, s0:s1:step], T.xm[a:b, s0:s1:step]]
+            if s0 // CAP == me:
+                w = WIN * (j - 2) + BASE + (REG - CAP) * me
+                return [T.win[:, w + s0:w + s1:step]]
+            return [T.land[:, 384 * (j - 2) + s0:384 * (j - 2) + s1:step]]
+
+        has = {"o": prev("scat"), "n": prev("arrn"), "f": prev("arrf")} if k > 0 else dict.fromkeys("onf", ["ldx", "xm"])
+        twice = 2 if k == 0 else 1
         if k == NP:
-            ro("fin", "p", "mm", 384, src + ["zz"] + prev("fireO"), lambda: [[
-                P.matmul(pX[:, 0:192], cz[:, ZZ + 1 - h:ZZ + 129 - h], T.land[:, L0 + 192 * h:L0 + 192 * h + 192],
-                         h == 0, h == 1) for h in range(2)][-1]])
-            ro("yev", "v", "full", 192, [n("fin")], lambda: [
-                V.tensor_scalar(T.yb[:, 192 * i:192 * i + 192], pX[:, 0:192], SHIFT - FILL, -1.0, A.add, A.max)])
-            ro("st", "y", "dma", 48, [n("yev")], lambda: [
-                g.sync.dma_start(T.y[64 * i:64 * i + 64, :], T.yb[:, 192 * i:192 * i + 192])], inc=16)
+            ro("fin", "p", pe(96, 4), has["o"] + has["n"] + has["f"] + ["zz"], lambda: [
+                group([(pX[:, 96 * c:96 * c + 96], cz[:, ZZ + 1 - h:ZZ + 129 - h],
+                        slots(192 * h + 96 * c, 192 * h + 96 * c + 96, 1)[0]) for h in range(2)])[0]
+                for c in range(2)], calls=2, role="numf")
+            ro("yev", "v", cyc(192), [n("fin")], lambda: [
+                V.tensor_scalar(T.yb[:, 192 * i:192 * i + 192], pX[:, 0:192], FILL + SHIFT, -1.0, A.add, A.max)],
+               role="castf")
+            op(n("st"), "y", 0.05, [n("yev")], lambda: [
+                g.sync.dma_start(T.y[64 * i:64 * i + 64, :], T.yb[:, 192 * i:192 * i + 192])], [], "r_st" + X, 16, 1, DMA0)
             return
         c0 = 192 * j
-        a, b = 64 * i, 64 * i + 64
-        for e, E, pn in ((0, "E", pX), (1, "O", pZ)):
-            free = prev("fireO" if e == 0 else "fireE")
-            if k == 0:
-                ro("num" + E, "p", "mm", 192, ["ldx", "pl" + X], lambda e=e, pn=pn: [[
-                    P.matmul(pn[:, 0:96], pl(h, a, b), T.xs[a:b, 2 * e + h::4], h == 0, h == 1) for h in range(2)][-1]])
-            else:
-                ro("num" + E, "p", "mm", 192, src + free + ["pl" + X, "pl" + X + "2"], lambda e=e, pn=pn: [[
-                    P.matmul(pn[:, 0:96], pl(h), T.land[:, L0 + 2 * e + h:L0 + 384:4], h == 0, h == 1)
-                    for h in range(2)][-1]])
-            ro("cast" + E, "v", "full", 96, [n("num" + E)], lambda e=e, pn=pn: [
-                V.tensor_scalar(T.off[:, c0 + 96 * e:c0 + 96 * e + 96], pn[:, 0:96],
-                                585.0 * (SHIFT - FILL) if k > 0 else 0.0, 0.0, A.add, A.max)])
-        if k == 0:
-            ro("merge", "p", "mm", 768, ["ldx", "xm", "ii"], lambda: [[
-                P.matmul(pY[:, 0:192], ii(h, a, b), s[a:b, h::2], w == 0 and h == 0, w == 1 and h == 1)
-                for w, s in enumerate((T.xs, T.xm)) for h in range(2)][-1]])
-            ro("evac", "v", "full", 192, [n("merge")], lambda: [
-                V.tensor_scalar(T.v[:, c0:c0 + 192], pY[:, 0:192], -SHIFT, FILL, A.add, A.max)])
-        else:
-            ro("merge", "p", "mm", 384, src + prev("reluO") + ["ii"], lambda: [[
-                P.matmul(pY[:, 0:192], ii(h), T.land[:, L0 + h:L0 + 384:2], h == 0, h == 1) for h in range(2)][-1]])
-            ro("evac", "s", "full", 192, [n("merge")], lambda: [
-                S.activation(T.v[:, c0:c0 + 192], pY[:, 0:192], F.Identity, bias=-FILL)])
-        ro("inc", "v", "half", 192, [n("evac")], lambda: [
-            V.tensor_scalar(T.inc[:, c0:c0 + 192], T.v[:, c0:c0 + 192], -8.0, 1.0, A.mult, A.min)])
-        lq = lambda q: cz[:, LB + 15 - q:LB + 143 - q]
-        for nm, q0, dep, soft in (("sua", 0, [n("evac"), "lb"] + (prev("smax") or ["dl" if i == 0 else "qo"]), []),
-                                  ("su", 8, [], [n("sua")])):
-            ro(nm, "p", "mm", 512, dep, lambda q0=q0: [[
-                P.matmul(pW[:, 0:12], lq(q), T.v[:, c0 + q:c0 + 192:16], q == 0, False) for q in range(q0, q0 + 8)][-1]],
-               soft=soft, sem=False)
+        pls = ["pl" + X, "z1"] + (["pl" + X + "2"] if k > 0 else [])
+        col = {"o": 48 * me - lo, "n": 48 * near - lo, "e": 96, "f": 144}
+        for B, r, pn, free in (("o", me, pX, []), ("n", near, pZ, prev(made("f")))):
+            ro("num" + B, "p", pe(48, 2 * twice), has[B] + pls + free, lambda pn=pn, r=r: group(
+                [(pn[:, 96:144], pl(h), s) for h in range(2) for s in slots(96 * r + h, 96 * r + 96, 2)]))
+        ro("numf", "p", pe(48, 4 * twice), has["f"] + pls + prev(made("e")), lambda: [group(
+            [(pY[:, 48 * e:48 * e + 48], pl(h), s) for h in range(2) for s in slots(2 * fo + 2 * e + h, 2 * fo + 192, 4)])[0]
+            for e in range(2)], calls=2)
+        if JOINF:
+            ro("numf", "p", pe(96, 2 * twice), has["f"] + pls + prev(made("f")), lambda: group(
+                [(pY[:, 0:96], pl(h), s) for h in range(2) for s in slots(2 * fo + h, 2 * fo + 192, 2)]))
+        for B, w, src in (("o", 48, pX[:, 96:144]), ("n", 48, pZ[:, 96:144]), ("f", 96, pY[:, 0:96])):
+            c = c0 + (96 if B == "f" else col[B])
+            ro("cast" + B, "v", cyc(w), [n("num" + B)], lambda c=c, w=w, src=src: [
+                V.tensor_scalar(T.off[:, c:c + w], src, 585.0 * (SHIFT - FILL) if k > 0 else 0.0, 4096.0, A.add, A.min)])
+        ro("mergen", "p", pe(48, 4 * twice), has["o"] + has["n"] + ["ii"], lambda: [group(
+            [(pW[:, 128 + 48 * r:176 + 48 * r], ii(h), s)
+             for h in range(2) for s in slots(96 * r + h, 96 * r + 96, 2)])[0] for r in (me, near)], calls=2, sem=not ONE)
+        ro("mergef", "p", pe(96, 2 * twice), has["f"] + ["ii"] + [n("evacn")] * (not ONE), lambda: group(
+            [(pW[:, 128 + fo:224 + fo], ii(h), s) for h in range(2) for s in slots(2 * fo + h, 2 * fo + 192, 2)]),
+           soft=[n("mergen")])
+        evacs, incs = ([n(r + B) for B in ("f" if ONE else "nf")] for r in ("evac", "inc"))
+        for B, c, w in (("f", 0, 192),) if ONE else (("n", lo, 96), ("f", fo, 96)):
+            ro("evac" + B, "s", cyc(w), [n("merge" + B)], lambda c=c, w=w: [
+                S.activation(T.v[:, c0 + c:c0 + c + w], pW[:, 128 + c:128 + c + w], F.Identity,
+                             bias=-FILL if k > 0 else -SHIFT)])
+            ro("inc" + B, "v", cyc(w // 2), [n("evac" + B)], lambda c=c, w=w: [
+                V.tensor_scalar(T.inc[:, c0 + c:c0 + c + w], T.v[:, c0 + c:c0 + c + w], -8.0, 1.0, A.mult, A.min)])
         G0 = 3072 * j
-        tab = T.lutw[:, 4096 * i:4096 * i + 4096]
-
-        def gather(nm, q, c, w):
-            out = T.gat[:, G0 + 16 * c:G0 + 16 * (c + w)]
-            win = lambda: tab.indirect(T.off[:, c0 + c:c0 + c + w])
-            ro(nm, q, "gath", 16 * w, [n("castE" if c < 96 else "castO"), "lut" + X],
-               (lambda: [S.activation(out, win(), F.Copy)]) if q == "s" else (lambda: [V.tensor_copy(out, win())]))
-            return n(nm)
-
-        def summed(nm, dep, c, w, soft):
-            ph, pc = (pX, c) if c < 96 else (pY, c - 96)
-            for sfx, u0 in (("a", 0), ("", 8)):
-                ro(nm + sfx, "p", "mm", 8 * max(64, w), dep + ["ident"] if sfx else [], lambda u0=u0: [[
-                    P.matmul(ph[:, pc:pc + w], T.ident[:], T.gat[:, G0 + 16 * c + u:G0 + 16 * (c + w):16], u == 0, u == 15)
-                    for u in range(u0, u0 + 8)][-1]], soft=soft if sfx else [n(nm + "a")], sem=not sfx)
-            return n(nm)
-
-        w1 = ES[k][i]
-        redE = [summed("redE", [gather("gathE", "s", 0, w1)], 0, w1, [])]
-        if w1 < 96:
-            redE.append(summed("redF", [gather("gathF", "s", w1, 96 - w1)], w1, 96 - w1, list(redE)))
-        c, gv, reds = 96, [], []
-        for w, nm in zip(NV[k][i], ("gva", "gvb", "gvc", "gvd")):
-            gv.append(gather(nm, "v", c, w))
-            c += w
-        todo = [("redV", gv, 96, c - 96)] if gv else []
-        if c < 192:
-            todo.append(("redL", [gather("gathL", "s", c, 192 - c)], c, 192 - c))
-        if JOINT[k][i] == 1 and len(todo) == 2:
-            todo = [("redV", todo[0][1] + todo[1][1], 96, 96)]
-        for nm, dep, cc, w in todo:
-            reds.append(summed(nm, dep + [n("evac")], cc, w, list(reds)))
-        for e, E, ph, pz, dep, free in ((0, "E", pX, pZ, redE, n("castO")), (1, "O", pY, pX, reds, n("reluE"))):
-            rh = T.rh[:, c0 + 96 * e:c0 + 96 * e + 96]
-            ro("relu" + E, "v", "full", 96, dep, lambda rh=rh, ph=ph: [
-                V.tensor_scalar(rh, ph[:, 0:96], 0.0, None, A.max)])
-            ro("pol" + E, "p", "mm", 96, [n("relu" + E), "cv" + X, free],
-               lambda rh=rh, pz=pz: [P.matmul(pz[:, 0:96], T.po[:, 128 * i:128 * i + 128], rh, True, True)])
-            ro("fire" + E, "v", "full", 96, [n("pol" + E)], lambda e=e, pz=pz: [
-                V.tensor_scalar(T.fire[:, c0 + e:c0 + 192:2], pz[:, 0:96], 0.0, None, A.is_gt)])
-            ro("t" + E, "v", "two", 96, [n("fire" + E), n("inc")], lambda e=e: [
-                V.tensor_tensor(T.t[:, c0 + e:c0 + 192:2], T.fire[:, c0 + e:c0 + 192:2], T.inc[:, c0 + e:c0 + 192:2],
-                                A.mult)])
-            ro("sf" + E, "p", "mm", 512, [n("fire" + E)], lambda e=e: [[
-                P.matmul(pW[:, 0:12], lq(q), T.fire[:, c0 + q:c0 + 192:16], False, q == 15)
-                for q in range(e, 16, 2)][-1]], soft=[n("su")] if e == 0 else [n("sfE")], sem=(e == 1))
-        s0, m0, e0, x0, W0 = 16 * j, 80 * j, 64 * j, 48 * j, WIN * j
-        ro("cp", "v", "full", 12, [n("sfO"), "z3"], lambda: [
-            V.tensor_scalar(T.si[:, s0:s0 + 12], pW[:, 0:12], 16 * SHIFT + 768 - 1.5, None, A.add)])
-        ro("eq", "v", "gath", 80, [n("cp"), "qo", "rp"], lambda: [
-            V.tensor_tensor(T.m[:, m0:m0 + 80], T.si[:, s0:s0 + 16].indirect(T.qo[:, 0:5]), T.rt[:], A.add)])
-        ro("scan", "v", "full", 64, [n("eq")], lambda: [
-            V.tensor_tensor_scan(T.e[:, e0:e0 + 64], T.m[:, m0 + 16:m0 + 80], T.m[:, m0:m0 + 64], 0.0, A.add,
-                                 A.subtract)])
-        ro("rank0", "p", "mm", 64, [n("cp"), "ones", "beta"], lambda: [
+        tab = T.lutw[:, TAB * i:TAB * i + TAB]
+        got = {}
+        for B in "onef":
+            c, got[B] = col[B], []
+            for p, piece in enumerate(PIECES[k][i][B].split()):
+                q, w = piece[0], int(piece[1:])
+                out, win = T.gat[:, G0 + 16 * c:G0 + 16 * (c + w)], tab.indirect(T.off[:, c0 + c:c0 + c + w])
+                ro("g%s%d" % (B, p), q, 0.06 + GATH * 16 * w, [n("cast" + B.replace("e", "f")), "lut" + X, "z0"],
+                   (lambda out=out, win=win: [S.activation(out, win, F.Copy)]) if q == "s" else
+                   (lambda out=out, win=win: [V.tensor_copy(out, win)]))
+                got[B].append(n("g%s%d" % (B, p)))
+                c += w
+        lq = lambda q: cz[:, LB + 15 - q:LB + 143 - q]
+        for B, c, w, at, ph, pz, dep, hfree, zfree in (
+                ("n", 0, 96, slice(c0 + lo, c0 + lo + 96), pX, pX, got["o"] + got["n"], [], []),
+                ("f", 96, 96, slice(c0 + fo, c0 + fo + 96), pY, pY, got["e"] + got["f"], [], [])) if JOINF else (
+                ("n", 0, 96, slice(c0 + lo, c0 + lo + 96), pX, pX, got["o"] + got["n"], [], []),
+                ("e", 96, 48, slice(c0 + fo, c0 + fo + 96, 2), pY, pY, got["e"], [], []),
+                ("f", 144, 48, slice(c0 + fo + 1, c0 + fo + 96, 2), pZ, pZ, got["f"], [n("castn")], [])):
+            parts = [(B, c, w, dep, [])]
+            if B == "n" and APART[k]:
+                parts = [("o", col["o"], 48, got["o"], []), ("n", col["n"], 48, got["n"], [n("redo")])]
+            for R, rc, rw, rdep, after in parts:
+                for sfx, u0 in (("a", 0), ("", 8)):
+                    ro("red" + R + sfx, "p", pe(rw, 8), rdep + hfree + ["ident"] if sfx else [],
+                       lambda u0=u0, rc=rc, rw=rw, out=ph[:, rc - c:rc - c + rw]: [[
+                           P.matmul(out, T.ident[:], T.gat[:, G0 + 16 * rc + u:G0 + 16 * (rc + rw):16], u == 0, u == 15)
+                           for u in range(u0, u0 + 8)][-1]], soft=after if sfx else [n("red" + R + "a")],
+                       sem=not sfx and R == B)
+            rh, step = T.rh[:, c0 + c:c0 + c + w], T.inc[:, at]
+            ro("relu" + B, "v", cyc(w), [n("red" + B)], lambda rh=rh, ph=ph, w=w: [
+                V.tensor_scalar(rh, ph[:, 0:w], 0.0, None, A.max)])
+            if B in QUICK:
+                ro("pol" + B, "p", pe(w, 1), [n("relu" + B), "cv" + X] + zfree, lambda rh=rh, pz=pz, w=w: group(
+                    [(pz[:, 0:w], T.po[:, 128 * i:128 * i + 128], rh)]))
+                ro("fire" + B, "v", cyc(w), [n("pol" + B)], lambda pz=pz, w=w, at=at: [
+                    V.tensor_scalar(T.t[:, at], pz[:, 0:w], -8.0, None, A.is_lt)])
+                if B == "f":
+                    at = at if QUICK == "f" else slice(c0 + fo, c0 + fo + 96) if QUICK == "ef" else slice(c0, c0 + 192)
+                    ro("tf", "v", cyc(96 * {"f": 1, "ef": 2, "nef": 4}[QUICK]), [n("sff")] + incs, lambda at=at: [
+                        V.tensor_tensor(T.t[:, at], T.t[:, at], T.inc[:, at], A.mult)])
+                continue
+            ro("pol" + B, "p", pe(w, 2), [n("relu" + B), "cv" + X, n("incn" if B == "n" and not ONE else "incf")] + zfree,
+               lambda rh=rh, pz=pz, w=w, step=step: group(
+                   [(pz[:, 0:w], T.ident[:], step), (pz[:, 0:w], T.po[:, 128 * i:128 * i + 128], rh)]))
+            ro("fire" + B, "v", cyc(w), [n("pol" + B)], lambda pz=pz, w=w: [
+                V.tensor_scalar(pz[:, 0:w], pz[:, 0:w], -8.0, None, A.is_lt)])
+            ro("t" + B, "v", cyc(w), [n("fire" + B)], lambda pz=pz, w=w, step=step, at=at: [
+                V.tensor_tensor(T.t[:, at], pz[:, 0:w], step, A.mult)])
+        wfree = ["lb", n("evacf")]
+        sums = []
+        if k == 0:
+            sums += [("su", q0, range(q0, q0 + 8), T.v, 0, 12, evacs) for q0 in (0, 8)]
+        sums += [("si", e, range(e, 16, 2), T.inc, 0, 12, incs)
+                 for e, B in enumerate("ef") if B in QUICK]
+        sums.append(("sf", "e", range(0, 16, 2), T.t, 0, 12, [n(made("n")), n(made("e"))]))
+        sums.append(("sf", "f", range(1, 16, 2), T.t, 0, 12, [n(made("n")), n(made("f"))]))
+        last = []
+        for u, (nm, tag, qs, buf, cc, w, dep) in enumerate(sums):
+            ro(nm + str(tag), "p", pe(12, 8), dep + wfree, lambda u=u, qs=qs, buf=buf, cc=cc, w=w: [[
+                P.matmul(pW[:, cc:cc + w], lq(q), buf[:, c0 + 16 * cc + q:c0 + 16 * (cc + w):16], u == 0 and q == qs[0],
+                         u == len(sums) - 1 and q == 15) for q in qs][-1]], soft=last, sem=u == len(sums) - 1)
+            last = [n(nm + str(tag))]
+        m0, e0, x0, s0, W0 = 5 * SEG * i, 64 * j, 48 * j, 16 * j, WIN * j
+        ro("floor", "v", cyc(12, 5), [n("sff")], lambda: [
+            V.tensor_scalar(T.m[:, m0 + SEG * u + 1:m0 + SEG * u + SEG], pW[:, 0:12],
+                            768 - 1.5 + 4 - u + (me if k > 0 else 16 * SHIFT), 512.0, A.add, A.max)
+            for u in range(5)], calls=5)
+        ro("scan", "v", cyc(26), [n("floor"), "rp"], lambda: [
+            V.tensor_tensor_scan(T.e[:, e0:e0 + 4 * SEG], T.m[:, m0:m0 + 4 * SEG], T.m[:, m0 + SEG:m0 + 5 * SEG], 0.0,
+                                 A.add, A.subtract)])
+        ro("rank0", "p", pe(48, 1), [n("floor"), "ones", "beta"], lambda: [
             P.matmul(pW[:, 64:112], T.ones[:], T.beta[:], True, False)], sem=False)
-        ro("rankM", "p", "mm", 512, [n("eq"), "um", "un"], lambda: [[
-            P.matmul(pW[:, 64 + r:112:4], u[:], T.m[:, m0 + 16 * (w - r):m0 + 16 * (w - r) + 12], False, False)
-            for r in range(4) for u, w in ((T.um, 4), (T.un, 3))][-1]], soft=[n("rank0")], sem=False)
-        ro("rankE", "p", "mm", 256, [n("scan")], lambda: [[
-            P.matmul(pW[:, 64 + r:112:4], T.ones[:], T.e[:, e0 + 16 * (3 - r):e0 + 16 * (3 - r) + 12], False, r == 3)
-            for r in range(4)][-1]], soft=[n("rankM")])
-        ro("smax", "v", "full", 48, [n("rankE"), "tr"], lambda: [
+        if RANKM:
+            ro("rankm", "p", pe(12, 8), [n("floor"), "ua", "ub"], lambda: [[
+                P.matmul(pW[:, 64 + r:112:4], u[:], T.m[:, m0 + SEG * (r + d) + 1:m0 + SEG * (r + d) + 13], False, False)
+                for r in range(4) for u, d in ((T.ua, 0), (T.ub, 1))][-1]], soft=[n("rank0")], sem=False)
+            ro("rank", "p", pe(12, 4), [n("scan")], lambda: [[
+                P.matmul(pW[:, 64 + r:112:4], T.ones[:], T.e[:, e0 + SEG * r:e0 + SEG * r + 12], False, r == 3)
+                for r in range(4)][-1]], soft=[n("rankm")])
+        else:
+            ro("rank", "p", pe(12, 8), [n("scan"), "ua", "ub"], lambda: [[
+                P.matmul(pW[:, 64 + r:112:4], u[:], T.e[:, e0 + SEG * r + d:e0 + SEG * r + d + 12], False, r == 3 and d == 1)
+                for r in range(4) for u, d in ((T.ub, 0), (T.ua, 1))][-1]], soft=[n("rank0")])
+        ro("smax", "v", cyc(48), [n("rank"), "tr"], lambda: [
             V.tensor_tensor_scan(T.sm[:, x0:x0 + 48], T.tr[:], pW[:, 64:112], 1.0e6, A.min, A.max)])
-        ro("cidx", "v", "full", 12, [n("smax")], lambda: [
-            V.tensor_scalar(T.idx[:, s0:s0 + 12], T.sm[:, x0 + 3:x0 + 48:4], 0.25, -1.0, A.mult, A.add)])
+        ro("cidx", "v", cyc(12), [n("smax")], lambda: [
+            V.tensor_scalar(T.idx[:, s0:s0 + 12], T.sm[:, x0 + 3:x0 + 48:4], 0.25, None, A.mult)])
         reg = lambda r: T.win[:, W0 + BASE + REG * r:W0 + BASE + REG * r + CAP]
-        ro("fill", "g", "iota4", CAP, prev("scat"), lambda: [iota(reg(r), [[0, CAP]], int(FILL), 0) for r in range(NR)],
-           soft=prev("own"))
-        ro("scat", "v", "scat", 192, [n("cidx"), n("tE"), n("tO"), n("fill"), n("evac")], lambda: [
-            V.tensor_tensor(T.win[:, W0:W0 + WIN].indirect(T.idx[:, s0:s0 + 12]), T.v[:, c0:c0 + 192],
-                            T.t[:, c0:c0 + 192], A.add)])
+        mark = int(FILL) if k < NP - 1 else -int(FILL)
+        for r in range(NR):
+            ro("fill%d_" % r, "g", gp(CAP), prev("scat"), lambda r=r: [iota(reg(r), [[0, CAP]], mark, 0)],
+               soft=[n("fill%d_" % (r - 1))] if r else prev("sendf"), role="fill")
+        ro("scat", "v", 0.05 + SCAT * 192, [n("cidx"), n(made("n")), n(made("e")), n("tf"), n("fill3_")] + evacs,
+           lambda: [V.tensor_tensor(T.win[:, W0:W0 + WIN].indirect(T.idx[:, s0:s0 + 12]), T.v[:, c0:c0 + 192],
+                                    T.t[:, c0:c0 + 192], A.add)])
         mine = T.land[:, 384 * j + CAP * me:384 * j + CAP * me + CAP]
 
-        def send():
-            for call in calls:
-                tr = []
-                for r in sorted(call):
-                    rid, pid, _ = topo.addr(T.cores[r])
-                    tr.append(RemoteDMATransfer(dst_ids=[DstId(rid=rid, pnc=pid)],
-                                                dma_engine_mask=sum(1 << e for e in call[r]),
-                                                remote_sem=T.sem["arr%d%s" % (k, X)], src=reg(r), dst=mine))
-                g.remote_dma_fused(tr, local_sem=T.sem["sent" + X])
+        def send(B, to):
+            tr = []
+            for u, r in enumerate(to):
+                eng = topo.engines(T.cores[me], T.cores[r])
+                w = len(eng) // len(to)
+                rid, pid, _ = topo.addr(T.cores[r])
+                tr.append(RemoteDMATransfer(dst_ids=[DstId(rid=rid, pnc=pid)],
+                                            dma_engine_mask=sum(1 << e for e in eng[u * w:(u + 1) * w]),
+                                            remote_sem=T.sem[n("arr" + B)], src=reg(r), dst=mine))
+            g.remote_dma_fused(tr, local_sem=T.sem["sent" + X])
             return []
 
-        ro("send", "g", "send", 0, [n("scat")], send, sem=False)
-        ro("own", "g", "iota", CAP, [n("scat")], lambda: [
-            g.affine_select(mine, reg(me), [[0, CAP]], A.is_ge, 0.0, 0, 0)], soft=[n("send")])
-        op(n("arr"), None, "arr", 0, [], None, soft=[n("send")], sem="arr%d%s" % (k, X), inc=come)
+        for B, to, lat, soft in (("n", [near], NEAR, []), ("f", far, FAR - CALL, [n("sendn")])):
+            ro("send" + B, "g", CALL + (FIRST if j == 0 and B == "n" else 0.0), [n("scat")], lambda B=B, to=to: send(B, to), soft=soft, sem=False)
+            come = sum(len(topo.engines(T.cores[r], T.cores[me])) // len(to) for r in to)
+            op(n("arr" + B), None, 0.0, [], None, [n("send" + B)], n("arr" + B), come, lat=lat - CALL)
 
     for k in range(NP + 1):
         for i, X in enumerate("AB"):
             half(k, i, X)
-    return ops, sum(len(e) for c in calls for e in c.values())
+    return ops, sum(len(topo.engines(T.cores[me], T.cores[r])) for r in (near, far[0]))
 
 
-def topo_order(ops):
-    seen, out = set(), []
-    while len(out) < len(ops):
-        for n in ops:
-            if n not in seen and all(d in seen for d in ops[n]["hard"] + ops[n]["soft"]):
-                seen.add(n)
-                out.append(n)
+def schedule(ops):
+    deps = {n: o["hard"] + o["soft"] for n, o in ops.items()}
+    users = {n: [] for n in ops}
+    for n in ops:
+        for d in deps[n]:
+            users[d].append(n)
+    way = {}
+    left, order = dict((n, len(set(deps[n]))) for n in ops), []
+    todo = [n for n in ops if left[n] == 0]
+    while todo:
+        n = todo.pop()
+        order.append(n)
+        for u in set(users[n]):
+            left[u] -= 1
+            if left[u] == 0:
+                todo.append(u)
+    for n in reversed(order):
+        way[n] = ops[n]["lat"] + max([HOP + way[u] for u in users[n]] + [0.0])
+    for n in way:
+        way[n] += BIAS.get(n[:-2], 0.0) + (LEAD[int(n[-2])] if n[-1] == "A" and n[-2].isdigit() else 0.0)
+        if not n[-2].isdigit():
+            way[n] += LEAD[0]
+    end, issued, free, out = {}, {}, {}, {}
+    left = dict((n, len(set(deps[n]))) for n in ops)
+    todo = [n for n in ops if left[n] == 0]
+    while todo:
+        start = {n: max([free.get(ops[n]["q"], 0.0)] + [end[d] + HOP for d in ops[n]["hard"]]
+                        + [issued[d] for d in ops[n]["soft"]]) for n in todo}
+        first = min(todo, key=lambda n: start[n] + ops[n]["dur"])
+        q = ops[first]["q"]
+        n = max([m for m in todo if ops[m]["q"] == q and start[m] <= start[first] + SLACK * ops[first]["dur"]],
+                key=lambda m: way[m]) if q else first
+        end[n], issued[n] = start[n] + ops[n]["lat"], start[n] + ops[n]["dur"]
+        if q:
+            free[q] = issued[n]
+            out.setdefault(q, []).append(n)
+        todo.remove(n)
+        for u in set(users[n]):
+            left[u] -= 1
+            if left[u] == 0:
+                todo.append(u)
     return out
 
 
-def waits(ops):
-    order = {q: ORDER[q].split() for q in ORDER}
+def timetable(ops):
+    tab = {c: dict(zip(t.split()[::2], map(float, t.split()[1::2]))) for c, t in TIME.items()}
+    key = {}
+    for n in ops:
+        if n in tab[""]:
+            key[n] = tab[""][n]
+        else:
+            k, X = int(n[-2]), n[-1]
+            key[n] = tab[X if k else "0" + X].get(n[:-2], 0.0) + OFFS[2 * k + "AB".index(X)]
+    done, out, todo = set(), {}, sorted(ops, key=lambda n: key[n])
+    while todo:
+        n = next(n for n in todo if all(d in done for d in ops[n]["hard"] + ops[n]["soft"]))
+        todo.remove(n)
+        done.add(n)
+        if ops[n]["q"]:
+            out.setdefault(ops[n]["q"], []).append(n)
+    return out
+
+
+def waits(ops, order):
     at, known, done, need = {q: 0 for q in order}, {q: set() for q in order}, {}, {}
     for n in ops:
         if ops[n]["q"] is None:
@@ -328,7 +434,7 @@ def waits(ops):
                 done[n] = known[q] | {n}
                 at[q] += 1
                 moved = True
-    return order, need
+    return need
 
 
 def rank_program(g, core, T, topo):
@@ -336,21 +442,19 @@ def rank_program(g, core, T, topo):
     if me is None:
         return
     ops, sent = graph(g, T, me, topo)
-    order, need = waits(ops)
+    order = timetable(ops) if TIME else schedule(ops)
+    need = waits(ops, order)
     queue = {"v": g.vector, "s": g.scalar, "p": g.tensor, "y": g.sync, "g": g}
-    many = {"half2": 2, "iota4": 4}
     total, mark = {}, {}
-    for n in topo_order(ops):
-        o = ops[n]
+    for n, o in ops.items():
         if o["sem"]:
-            k = many.get(o["kind"], 2 if n[:3] in ("lut", "pol") and o["kind"] == "dma" else 1)
-            total[o["sem"]] = total.get(o["sem"], 0) + k * o["inc"]
+            total[o["sem"]] = total.get(o["sem"], 0) + o["calls"] * o["inc"]
             mark[n] = total[o["sem"]]
     waited = {}
     for q in order:
         for n in order[q]:
             o = ops[n]
-            for d in need[n]:
+            for d in dict.fromkeys(need[n]):
                 s = ops[d]["sem"]
                 queue[q].wait_ge(T.sem[s], mark[d])
                 waited[s] = max(waited.get(s, 0), mark[d])

@@ -6,52 +6,39 @@ F = ActivationFunctionType
 NP, CAP, NR = 4, 96, 4
 WIN, BASE, REG = 1856, 320, 384
 FILL, SHIFT = 1024.0, 6.125
-TAB = 4112
+TAB = 4096
 SEG = 13
+PL0 = 80
 HDT = "float16"
-PIECES = ([[{'o': 's24 v24', 'n': 's48', 'e': 's12 v36', 'f': 'v24 s24'},
-            {'o': 's12 s24 s12', 'n': 's36 v12', 'e': 's36 s12', 'f': 's12 s24 s12'}]]
-          + [[{'o': 's48', 'n': 'v12 s36', 'e': 'v24 s24', 'f': 's36 v12'},
-              {'o': 's36 v12', 'n': 'v12 s36', 'e': 's48', 'f': 'v12 s36'}]] * (NP - 1))
 LOADS = {"s": "ldx plA", "y": "lutA plB polA lutB polB plA2 plB2"}
-APART = [0, 1, 1, 1]
-QUICK = "f"
-RANKM = True
-JOINF = False
-ONE = True
+PIECES = ([[{'o': 'v48', 'n': 's48', 'e': 's24 v24', 'f': 's24 v12 v12'},
+            {'o': 's48', 'n': 's36 v12', 'e': 's12 s36', 'f': 'v12 s24 s12'}]]
+          + [[{'o': 's36 v12', 'n': 'v16 s32', 'e': 'v16 s32', 'f': 's24 s24'}] * 2] * (NP - 1))
 TIME = {
-    '0A': 'fill0_ 0.91 fill1_ 1.22 fill2_ 1.54 numf 2.11 numo 2.35 numn 2.48 castf 2.55 mergen 2.6 casto 2.77 castn 2.83 ge0 2.85 ge1 2.89 fill3_ 3.01 go0 3.13 mergef 3.55 gn0 3.67 go1 3.81 redea 4.04 rede 4.28 gf0 4.5 evacf 4.69 gf1 4.87 redna 4.89 relue 5.03 incf 5.09 redn 5.25 redfa 5.62 relun 5.82 redf 5.87 pole 6.11 poln 6.17 su0 6.27 reluf 6.31 firee 6.37 firen 6.47 su8 6.51 te 6.64 tn 6.76 polf 6.76 si1 6.79 firef 6.99 sfe 7.05 sff 7.3 floor 7.74 rank 7.88 scan 8.25 rank0 8.25 rankm 8.28 tf 8.31 smax 8.85 cidx 9.11 scat 9.37 sendn 10.14 sendf 12.34',
-    '0B': 'fill0_ 0.6 fill1_ 2.07 fill2_ 2.38 fill3_ 2.7 numf 2.93 mergen 3.18 numn 3.43 mergef 3.73 castn 3.75 numo 3.92 castf 4.41 gf0 5.41 casto 5.43 go0 5.71 gf1 6 go1 6.52 gf2 6.82 gn0 7.43 rank 7.75 go2 8.21 gn1 8.4 ge0 8.5 redfa 8.65 redf 8.89 redna 9.14 evacf 9.27 ge1 9.46 redn 9.51 reluf 9.94 redea 9.96 relun 10.07 incf 10.17 rede 10.2 poln 10.46 relue 10.65 firen 10.75 pole 10.91 polf 10.97 su0 11 firee 11.17 firef 11.23 tn 11.29 su8 11.31 si1 11.56 te 11.57 sfe 11.83 sff 12.08 floor 12.52 tf 12.83 scan 13.97 rank0 14.02 rankm 14.05 smax 14.71 cidx 15.07 scat 15.33 sendn 16.11 sendf 16.51',
-    'A': 'numo 0.85 casto 1.11 go0 1.37 fill0_ 1.91 numn 2.01 fin 2.17 fill1_ 2.22 castn 2.27 gn0 2.53 gn1 2.53 fill2_ 2.54 mergen 2.79 numf 2.91 mergef 3.04 redoa 3.13 castf 3.3 ge0 3.59 ge1 3.59 redo 3.89 gf0 4.12 redna 4.14 redea 4.39 gf1 4.45 yev 4.58 rede 4.63 redn 4.88 evacf 4.89 st 4.96 redfa 5.12 relun 5.33 redf 5.37 incf 5.42 relue 5.51 poln 5.71 pole 5.8 reluf 5.81 si1 5.86 firen 6 firee 6.09 polf 6.11 tn 6.29 fill3_ 6.33 te 6.38 firef 6.44 sfe 6.64 sff 6.89 floor 7.37 scan 7.88 rank0 7.88 rankm 7.91 tf 7.94 rank 8.16 smax 8.48 cidx 8.74 scat 9 sendn 9.78 sendf 10.18',
-    'B': 'numo 0.88 casto 1.14 go0 1.41 go1 1.78 numn 1.79 fin 1.79 castn 2.08 yev 2.17 gn0 2.34 gn1 2.34 numf 2.41 mergen 2.53 st 2.55 mergef 2.65 redoa 2.74 castf 2.95 evacf 3.11 ge0 3.29 gf0 3.3 redo 3.55 redna 3.79 redn 4.04 incf 4.07 gf1 4.31 si1 4.36 redea 4.61 relun 4.85 rede 4.85 poln 5.16 redfa 5.28 relue 5.3 firen 5.45 redf 5.52 tn 5.74 pole 5.77 fill0_ 5.85 reluf 5.97 firee 6.03 polf 6.23 te 6.29 firef 6.46 sfe 6.55 sff 6.8 fill1_ 7.1 floor 7.24 fill2_ 7.41 fill3_ 7.73 scan 7.75 rank0 7.75 rankm 7.78 rank 8.02 smax 8.37 tf 8.44 cidx 8.64 scat 9 sendn 9.78 sendf 10.18',
-    '': 'z0 0 ldx 0 lutA 0 kc 0 plA 0.05 plB 0.1 z3 0.12 polA 0.15 lutB 0.25 z1 0.35 polB 0.35 tr 0.37 plA2 0.45 plB2 0.5 one 0.53 z2 0.6 kr 0.8 dl 1.03 xm 1.28 cl 1.47 ident 1.53 i2 1.59 ones 1.73 beta 1.85 lt 1.97 ii 2.03 lb 2.65 cvA 4.35 go 5.19 rp 6.56 cvB 7.05 ua 7.11 ub 7.56 zz 10.26'}
-OFFS = [0, 0, 10.59, 15.32, 19.57, 24.3, 28.55, 33.15, 38.15, 42.75]
-SLACK = 0.5
-LEAD = [3.0, 3.0, 3.0, 3.0, 3.0]
-BIAS = {}
-CYC, PEC, GATH, SCAT, HOP = 1.0e-3, 0.5e-3, 1.3e-3, 3.0e-3, 0.18
-DMA0, DMAKB, CALL, NEAR, FAR, FIRST = 1.0, 0.002, 0.4, 1.3, 1.9, 1.5
+    '': 'z2 -0.12 ldx 0 lutA 0 z1 0.01 plA 0.05 tr 0.05 plB 0.1 polA 0.15 lutB 0.25 z3 0.25 polB 0.35 plA2 0.45 plB2 0.5 all 0.64 xm 1.34 ident 1.41 gmm 1.55 gsel 1.82 ones 1.96 ii 1.97 beta 2.11 go 2.13 z4 2.82 ua 3.5 cvA 4.79 lb 5.34 zz 6.21 cvB 6.54 pw 6.64 plm0 6.84 ub 7.17 rp 7.47 plm1 8.62',
+    '0A': 'numn 1.92 nume 1.97 castn 2.37 numo 2.42 ge0 2.61 castf 2.66 mergen 2.69 casto 2.79 caste 2.81 numf 2.91 ge1 3.19 mergef 3.35 go0 3.54 gn0 3.72 redea 4.03 rede 4.2 gf1 4.47 gf2 4.67 gf0 4.7 redn 4.81 evac 4.9 fill0_ 4.93 redna 5.01 fill2_ 5.08 relue 5.16 fill1_ 5.35 redf 5.37 redfa 5.59 inc 5.8 fill3_ 5.92 poln 5.95 polf 6.01 relun 6.07 pole 6.2 su0 6.2 reluf 6.25 su8 6.55 firen 6.75 sff 6.78 firee 6.89 firef 6.9 sfe 6.94 tf 7.39 rankb 7.67 floor 7.89 tn 8.28 scan 8.38 cidx 8.46 rankm 8.47 rank 8.64 smax 8.71 scat 9.32 sendn 10.25 sendf 11.9',
+    '0B': 'mergef 2.46 mergen 3.02 nume 3.49 numn 3.69 fill0_ 3.92 numo 3.94 fill1_ 4.09 caste 4.37 castn 4.77 ge0 5.13 ge1 5.85 casto 5.88 numf 5.96 castf 6.35 go0 6.75 redea 7.14 gf0 7.28 rede 7.65 gn0 7.75 fill2_ 8.14 gn1 8.44 redn 8.52 gf2 8.53 gf1 9 redna 9.02 evac 9.09 redfa 9.14 redf 9.15 relun 9.34 fill3_ 9.42 relue 9.49 inc 9.84 firen 9.93 reluf 10.16 poln 10.18 pole 10.42 su0 10.59 firee 10.72 polf 10.87 su8 10.91 firef 11.1 sfe 11.14 sff 11.44 floor 11.89 scan 11.98 tf 12.49 rankb 12.53 rankm 12.68 rank 12.91 smax 12.92 tn 13.12 cidx 13.16 scat 14 sendn 15.3 sendf 15.61',
+    '*': 'numo 0.79 casto 1.25 fill0_ 1.28 go0 1.57 fill1_ 2 go1 2.04 castn 2.12 numn 2.16 fill2_ 2.23 fill3_ 2.76 mergen 2.78 gn1 2.84 caste 2.9 gn0 2.98 finn 3 nume 3.08 numf 3.23 mergef 3.45 castf 3.52 finf 3.53 ge0 3.54 yevn 3.56 stn 3.76 yevf 3.87 ge1 3.97 redna 3.99 redn 4.26 stf 4.57 redea 4.65 redfa 4.84 rede 4.85 gf0 4.86 relun 4.88 relue 5.32 gf1 5.38 evac 5.39 poln 5.57 redf 5.58 firee 5.69 inc 5.77 firen 6.05 reluf 6.09 pole 6.24 turn 6.25 firef 6.3 sff 6.45 polf 6.53 sfe 6.91 tn 7.04 sj 7.14 floor 7.46 scan 7.62 rank 8.02 rankm 8.07 smax 8.19 rankb 8.27 tf 8.88 cidx 9.08 scat 9.24 sendf 9.86 sendn 10.15'}
+OFFS = [0, 0, 9.84, 14.3, 18.72, 23.11, 27.51, 31.78, 40.69, 52.82]
 
 SCRATCH = {
     "lutw": ("sbuf", [128, 2 * TAB], "bfloat16"),
     "xs": ("sbuf", [128, 384], "bfloat16"),
     "xm": ("sbuf", [128, 384], "bfloat16"),
-    "plb": ("sbuf", [128, 320], "bfloat16"),
+    "plb": ("sbuf", [128, 352], "bfloat16"),
+    "plm": ("sbuf", [128, 2 * 352], "bfloat16"),
     "pob": ("sbuf", [128, 256], "bfloat16"),
     "po": ("sbuf", [128, 256], HDT),
     "cz": ("sbuf", [128, 480], "bfloat16"),
-    "kc": ("sbuf", [128, 128], "bfloat16"),
-    "qc": ("sbuf", [128, 128], "bfloat16"),
-    "one": ("sbuf", [128, 16], "bfloat16"),
-    "dl": ("sbuf", [128, 128], "bfloat16"),
+    "full": ("sbuf", [128, 128], "bfloat16"),
+    "gsel": ("sbuf", [128, 128], "bfloat16"),
     "ident": ("sbuf", [128, 128], "bfloat16"),
-    "cl": ("sbuf", [128, 128], "bfloat16"),
     "ones": ("sbuf", [128, 128], "bfloat16"),
-    "lt": ("sbuf", [128, 128], "bfloat16"),
-    "i2": ("sbuf", [128, 128], "bfloat16"),
     "go": ("sbuf", [128, 128], "bfloat16"),
     "ua": ("sbuf", [128, 128], "bfloat16"),
     "ub": ("sbuf", [128, 128], "bfloat16"),
+    "pw": ("sbuf", [128, 320], "bfloat16"),
+    "it": ("sbuf", [128, 8 * 192], "bfloat16"),
     "beta": ("sbuf", [128, 48], "bfloat16"),
     "tr": ("sbuf", [128, 48], "float32"),
     "off": ("sbuf", [128, 8 * 192], "uint16"),
@@ -59,6 +46,7 @@ SCRATCH = {
     "v": ("sbuf", [128, 8 * 192], "bfloat16"),
     "inc": ("sbuf", [128, 8 * 192], "bfloat16"),
     "rh": ("sbuf", [128, 8 * 192], HDT),
+    "fire": ("sbuf", [128, 8 * 192], "bfloat16"),
     "t": ("sbuf", [128, 8 * 192], "bfloat16"),
     "m": ("sbuf", [128, 2 * 5 * SEG], "bfloat16"),
     "e": ("sbuf", [128, 8 * 64], "bfloat16"),
@@ -66,20 +54,18 @@ SCRATCH = {
     "idx": ("sbuf", [128, 8 * 16], "uint16"),
     "win": ("sbuf", [128, 8 * WIN], "bfloat16"),
     "land": ("sbuf", [128, 8 * 384], "bfloat16"),
-    "yb": ("sbuf", [128, 2 * 192], "bfloat16"),
+    "yb": ("sbuf", [128, 4 * 96], "bfloat16"),
 }
 for _h in "AB":
     for _b in "XYZW":
         SCRATCH["p" + _b + _h] = ("psum", [128, 512], "float32")
 
-START = ["z0", "z1", "z2", "z3", "one", "kc", "beta", "rp", "tr", "kr", "dl", "ident", "ii", "cl", "ones", "lb", "zz",
-         "lt", "i2", "go", "ua", "ub", "xm", "ldx", "lutA", "lutB", "plA", "plB", "plA2", "plB2", "polA", "polB",
-         "cvA", "cvB"]
-ROLES = ([r + b for r in ("num", "cast") for b in "onf"]
-         + ["g" + b + str(p) for b, most in zip("onef", (3, 3, 3, 3)) for p in range(most)]
-         + [r + b for r in ("merge", "evac", "inc") for b in "nf"]
-         + [r + b for r in ("red", "relu", "pol", "fire", "t") for b in "nef"]
-         + ["sff", "floor", "scan", "rank", "smax", "cidx", "scat", "fill", "st"])
+START = ["z1", "z2", "z3", "z4", "pw", "all", "gsel", "gmm", "beta", "rp", "tr", "ident", "ii", "ones", "lb", "zz", "go", "ua",
+         "ub", "xm", "plm0", "plm1", "ldx", "lutA", "lutB", "plA", "plB", "plA2", "plB2", "polA", "polB", "cvA", "cvB"]
+ROLES = ([r + b for r in ("num", "cast") for b in "onef"] + ["g" + b + str(p) for b in "onef" for p in range(3)]
+         + [r + b for r in ("red", "relu", "pol", "fire") for b in "nef"]
+         + ["mergef", "evac", "inc", "turn", "tn", "tf", "sff", "floor", "scan", "rank", "smax", "cidx", "scat", "fill",
+            "stn", "stf"])
 SEMAPHORES = (["s_" + n for n in START] + ["r_" + r + x for r in ROLES for x in "AB"]
               + ["arr%s%d%s" % (b, k, x) for b in "nf" for k in range(NP) for x in "AB"] + ["sentA", "sentB"])
 
@@ -93,84 +79,79 @@ def graph(g, T, me, topo):
     ops = {}
     V, S, P = g.vector, g.scalar, g.tensor
     near, far = sides(T.cores, me, topo)
-    cyc = lambda n, calls=1: calls * CYC * max(64, n)
-    pe = lambda n, calls: calls * PEC * max(64, n)
-    gp = lambda n: 0.13 + 2 * CYC * n
 
-    def op(name, q, dur, hard, emit, soft=(), sem=None, inc=1, calls=1, lat=None):
-        ops[name] = dict(q=q, dur=dur, hard=list(hard), soft=list(soft), emit=emit, sem=sem, inc=inc, calls=calls,
-                         lat=dur if lat is None else lat)
+    def op(name, q, hard, emit, soft=(), sem=None, inc=1, calls=1):
+        ops[name] = dict(q=q, hard=list(hard), soft=list(soft), emit=emit, sem=sem, inc=inc, calls=calls)
 
-    def st(name, q, dur, hard, emit, calls=1):
-        op(name, q, dur, hard, emit, sem="s_" + name, calls=calls)
-
-    def load(name, q, kb, hard, emit, calls=1, soft=()):
-        op(name, q, 0.05 * calls, hard, emit, soft, "s_" + name, 16, calls, DMA0 + DMAKB * kb)
+    def st(name, q, hard, emit, calls=1):
+        op(name, q, hard, emit, sem="s_" + name, calls=calls)
 
     II, LB, ZZ = 0, 192, 336
     cz = T.cz
     iota = lambda o, pat, b, cm: g.iota(o, pat, b, cm, allow_small_or_imprecise_dtypes=True)
-    st("z0", "v", cyc(8, 2), [], lambda: [V.memset(T.lutw[:, TAB * i + 4096:TAB * i + TAB], 0.0) for i in range(2)], 2)
-    st("z1", "v", cyc(32, 3), [], lambda: [V.memset(T.plb[:, c:c + 64], 0.0) for c in (0, 128, 256)], 3)
-    st("z2", "v", cyc(32, 4), [], lambda: [V.memset(T.pob[64 * h:64 * h + 64, c - 64 * h:c - 64 * h + 64], 0.0)
-                                           for h in range(2) for c in (64, 192)], 4)
+    st("z1", "v", [], lambda: [V.memset(T.plb[:, a:b], 0.0)
+                               for a, b in ((0, PL0), (PL0 + 64, PL0 + 128), (PL0 + 192, 352))], 3)
+    st("z2", "v", [], lambda: [V.memset(T.pob[64 * h:64 * h + 64, c - 64 * h:c - 64 * h + 64], 0.0)
+                               for h in range(2) for c in (64, 192)], 4)
     queue = {"s": S, "y": g.sync}
     src = {"ldx": lambda D: [D.dma_start(T.xs[:], T.x[:])]}
     for i, X in enumerate("AB"):
         src["lut" + X] = lambda D, i=i: [
-            D.dma_start(T.lutw[64 * h:64 * h + 64, TAB * i:TAB * i + 4096], T.lut[64 * i:64 * i + 64, :])
+            D.dma_start(T.lutw[64 * h:64 * h + 64, TAB * i:TAB * i + TAB], T.lut[64 * i:64 * i + 64, :])
             for h in range(2)]
         for nm, h in (("pl" + X, i), ("pl" + X + "2", 1 - i)):
-            src[nm] = lambda D, i=i, h=h: [D.dma_start(T.plb[64 * h:64 * h + 64, 64 + 128 * i:128 + 128 * i],
+            src[nm] = lambda D, i=i, h=h: [D.dma_start(T.plb[64 * h:64 * h + 64, PL0 + 128 * i:PL0 + 64 + 128 * i],
                                                        T.pl[64 * i:64 * i + 64, 64 * i:64 * i + 64])]
         src["pol" + X] = lambda D, i=i: [
             D.dma_start(T.pob[64 * h:64 * h + 64, 128 * i + 64 * h:128 * i + 64 * h + 64],
                         T.pol[64 * i:64 * i + 64, 64 * i:64 * i + 64]) for h in range(2)]
-        st("cv" + X, "v", cyc(64), ["pol" + X, "z2"], lambda i=i: [
-            V.tensor_scalar(T.po[:, 128 * i:128 * i + 128], T.pob[:, 128 * i:128 * i + 128], -16.0, None, A.mult)])
+        st("cv" + X, "v", ["pol" + X, "z2"], lambda i=i: [
+            V.tensor_copy(T.po[:, 128 * i:128 * i + 128], T.pob[:, 128 * i:128 * i + 128])])
     for q in LOADS:
-        kb, last = 0, []
+        last = []
         for nm in LOADS[q].split():
-            kb += 1024 if nm[:3] == "lut" else 96
-            load(nm, q, kb, [], lambda nm=nm, q=q: src[nm](queue[q]), 2 if nm[:3] in ("lut", "pol") else 1, last)
+            op(nm, q, [], lambda nm=nm, q=q: src[nm](queue[q]), last, "s_" + nm, 16, 2 if nm[:3] in ("lut", "pol") else 1)
             last = [nm]
-    st("z3", "v", cyc(240), [], lambda: [V.memset(cz[:], 0.0)])
-    st("one", "v", cyc(8), [], lambda: [V.memset(T.one[:], 1.0)])
-    st("kc", "g", gp(128), [], lambda: [iota(T.kc[:], [[1, 2], [64, 4], [2, 16]], 0, 0)])
-    st("beta", "g", gp(48), [], lambda: [iota(T.beta[:], [[0, 12], [REG // 8, 4]], BASE // 8 - 256, 0)])
-    st("rp", "v", cyc(5), [], lambda: [V.memset(T.m[:, 0:10 * SEG:SEG], 2.0 ** 30)])
-    st("tr", "g", gp(48), [], lambda: [iota(T.tr[:], [[-64, 12], [16384, 4]], 4 * BASE - 4, -4)])
-    st("kr", "p", pe(2, 1), ["kc", "one"], lambda: [P.matmul(T.pWA[:, 0:2], T.kc[0:1, :], T.one[0:1, 0:2], True, True)])
-    st("dl", "v", cyc(128), ["kr", "kc"],
-       lambda: [V.tensor_scalar(T.dl[:], T.kc[:], T.pWA[:, 0:1], -1.0, A.subtract, A.mult)])
-    st("ident", "v", cyc(64), ["dl"], lambda: [V.tensor_scalar(T.ident[:], T.dl[:], 0.0, None, A.is_equal)])
-    st("ii", "v", cyc(128), ["ident", "z3"],
+    st("z3", "v", [], lambda: [V.memset(cz[:], 0.0)])
+    st("all", "v", [], lambda: [V.memset(T.full[:], 1.0)])
+    st("beta", "g", [], lambda: [iota(T.beta[:], [[0, 12], [REG // 8, 4]], BASE // 8 - 256, 0)])
+    st("rp", "v", [], lambda: [V.memset(T.m[:, 0:10 * SEG:SEG], 2.0 ** 30)])
+    st("tr", "g", [], lambda: [iota(T.tr[:], [[-64, 12], [16384, 4]], 4 * BASE - 4, -4)])
+    st("ident", "g", ["all"], lambda: [g.affine_select(T.ident[:], T.full[:], [[-1, 128]], A.is_equal, 0.0, 0, 1)])
+    st("gsel", "g", ["all"], lambda: [
+        g.affine_select(T.gsel[0:4, :], T.full[0:4, :], [[0, 2], [1, 4], [0, 16]], A.is_equal, 0.0, 0, -1)])
+    st("gmm", "p", ["gsel"], lambda: [P.matmul(T.pWB[:, 0:128], T.gsel[0:4, :], T.gsel[0:4, :], True, True)])
+    st("ones", "s", ["gmm"], lambda: [S.activation(T.ones[:], T.pWB[:, 0:128], F.Copy)])
+    st("ii", "v", ["ident", "z3"],
        lambda: [V.tensor_tensor(cz[:, II + 64:II + 128], T.ident[:, 0:64], T.ident[:, 64:128], A.add)])
-    st("cl", "v", cyc(64), ["dl"], lambda: [V.tensor_scalar(T.cl[:], T.dl[:], -31.5, 31.5, A.max, A.min)])
-    st("ones", "v", cyc(256), ["cl", "dl"], lambda: [V.tensor_tensor(T.ones[:], T.cl[:], T.dl[:], A.is_equal)])
-    st("lb", "v", cyc(4, 2), ["ones", "z3"], lambda: [
+    st("lb", "v", ["ones", "z3"], lambda: [
         V.tensor_copy(cz[64 * h:64 * h + 64, LB + 15 + 64 * h:LB + 79 + 64 * h:16],
                       T.ones[64 * h:64 * h + 64, 64 * h:64 * h + 64:16]) for h in range(2)], 2)
-    st("zz", "v", cyc(32), ["ii", "z3"], lambda: [V.tensor_copy(cz[:, ZZ + 1:ZZ + 129:2], cz[:, II + 64:II + 128])])
-    st("lt", "v", cyc(64), ["dl"], lambda: [V.tensor_scalar(T.lt[:], T.dl[:], 0.0, None, A.is_lt)])
-    st("i2", "v", cyc(64), ["dl"], lambda: [V.tensor_scalar(T.i2[:], T.dl[:], 0.0, 2048.0, A.is_equal, A.mult)])
-    st("go", "v", cyc(256), ["lt", "ones"], lambda: [V.tensor_tensor(T.go[:], T.lt[:], T.ones[:], A.mult)])
-    st("ua", "v", cyc(256), ["go", "i2"], lambda: [V.tensor_tensor(T.ua[:], T.i2[:], T.go[:], A.add)])
-    if RANKM:
-        st("ub", "v", cyc(64), ["ua"], lambda: [V.tensor_scalar(T.ub[:], T.ua[:], -1.0, None, A.mult)])
-    else:
-        st("ub", "v", cyc(256), ["ua", "ones"], lambda: [V.tensor_tensor(T.ub[:], T.ones[:], T.ua[:], A.subtract)])
-    made = lambda B: ("fire" if B in QUICK else "t") + ("f" if JOINF and B == "e" else B)
-    st("xm", "v", cyc(192), ["ldx"], lambda: [V.tensor_scalar(T.xm[:], T.xs[:], 0.0, -FILL, A.min, A.mult)])
+    st("zz", "v", ["ii", "z3"], lambda: [V.tensor_copy(cz[:, ZZ + 1:ZZ + 129:2], cz[:, II + 64:II + 128])])
+    st("go", "g", ["ones", "ident", "beta", "tr"], lambda: [
+        g.affine_select(T.go[64 * h:64 * h + 64, :], T.ones[64 * h:64 * h + 64, :], [[1, 2], [2, 64]], A.is_gt, 0.0, -h, -2)
+        for h in range(2)], 2)
+    st("ua", "g", ["go"], lambda: [g.affine_select(T.ua[:], T.go[:], [[-1, 128]], A.not_equal, 2048.0, 0, 1)])
+    st("ub", "v", ["ua"], lambda: [V.tensor_scalar(T.ub[:], T.ua[:], -1.0, None, A.mult)])
+    st("xm", "v", ["ldx"], lambda: [V.tensor_scalar(T.xm[:], T.xs[:], 0.0, -FILL, A.min, A.mult)])
+    st("z4", "v", [], lambda: [V.memset(T.pw[:], 0.0)])
+    st("pw", "g", ["ident", "z4", "fill3_0A"], lambda: [
+        g.affine_select(T.pw[:, 160 * w + 16:160 * w + 144], T.ident[:], [[0, 4], [1, 2], [0, 16]], A.is_equal, 0.0, -w, 0)
+        for w in range(2)], 2)
+    for t in range(2):
+        st("plm%d" % t, "g", ["plA", "plB", "plA2", "plB2", "z1", "fill3_0A", "ua"], lambda t=t: [
+            g.affine_select(T.plm[:, 352 * t:352 * t + 352], T.plb[:], [[0, 22], [2 * t - 1, 16]], A.is_ge, 0.0,
+                            7 - 15 * t, 0)])
 
     lo, fo = 48 * min(me, near), 48 * min(far)
+    calls = {"n": [near], "f": far}
 
     def half(k, i, X):
         n = lambda r, kk=k: "%s%d%s" % (r, kk, X)
         j = 2 * k + i
 
-        def ro(r, q, dur, hard, emit, soft=(), sem=True, calls=1, role=None):
-            op(n(r), q, dur, hard, emit, soft, ("r_" + (role or r) + X) if sem else None, 1, calls)
+        def ro(r, q, hard, emit, soft=(), sem=True, calls=1, role=None):
+            op(n(r), q, hard, emit, soft, ("r_" + (role or r) + X) if sem else None, 1, calls)
 
         def group(mms):
             return [[P.matmul(o, l, r, u == 0, u == len(mms) - 1) for u, (o, l, r) in enumerate(mms)][-1]]
@@ -178,7 +159,8 @@ def graph(g, T, me, topo):
         prev = lambda *rs: [n(r, k - 1) for r in rs] if k > 0 else []
         pX, pY, pZ, pW = (T["p" + b + X] for b in "XYZW")
         a, b = (64 * i, 64 * i + 64) if k == 0 else (0, 128)
-        pl = lambda h: T.plb[a:b, 64 + 128 * i - 64 * h:192 + 128 * i - 64 * h]
+        at0 = lambda h: PL0 + 128 * i - 64 * h
+        pl = lambda h: T.plb[a:b, at0(h):at0(h) + 128]
         ii = lambda h: cz[a:b, II + 64 - 64 * h:II + 192 - 64 * h]
 
         def slots(s0, s1, step):
@@ -189,152 +171,129 @@ def graph(g, T, me, topo):
                 return [T.win[:, w + s0:w + s1:step]]
             return [T.land[:, 384 * (j - 2) + s0:384 * (j - 2) + s1:step]]
 
-        has = {"o": prev("scat"), "n": prev("arrn"), "f": prev("arrf")} if k > 0 else dict.fromkeys("onf", ["ldx", "xm"])
-        twice = 2 if k == 0 else 1
+        has = {"o": prev("scat"), "n": prev("arrn"), "f": prev("arrf")} if k > 0 else dict.fromkeys("onf", ["ldx"])
         if k == NP:
-            ro("fin", "p", pe(96, 4), has["o"] + has["n"] + has["f"] + ["zz"], lambda: [
-                group([(pX[:, 96 * c:96 * c + 96], cz[:, ZZ + 1 - h:ZZ + 129 - h],
-                        slots(192 * h + 96 * c, 192 * h + 96 * c + 96, 1)[0]) for h in range(2)])[0]
-                for c in range(2)], calls=2, role="numf")
-            ro("yev", "v", cyc(192), [n("fin")], lambda: [
-                V.tensor_scalar(T.yb[:, 192 * i:192 * i + 192], pX[:, 0:192], FILL + SHIFT, -1.0, A.add, A.max)],
-               role="castf")
-            op(n("st"), "y", 0.05, [n("yev")], lambda: [
-                g.sync.dma_start(T.y[64 * i:64 * i + 64, :], T.yb[:, 192 * i:192 * i + 192])], [], "r_st" + X, 16, 1, DMA0)
+            for u, (B, c, pf, dep) in enumerate((("n", lo, pX, has["o"] + has["n"]),
+                                                 ("f", fo, pY, has["f"] + prev("firee")))):
+                yb = T.yb[:, 192 * i + 96 * u:192 * i + 96 * u + 96]
+                ro("fin" + B, "p", dep + ["zz"], lambda c=c, pf=pf: group(
+                    [(pf[:, 0:96], cz[:, ZZ + 1 - h:ZZ + 129 - h], slots(2 * c + 96 * h, 2 * c + 96 * h + 96, 1)[0])
+                     for h in range(2)]), role="num" + B)
+                ro("yev" + B, "v", [n("fin" + B)], lambda yb=yb, pf=pf: [
+                    V.tensor_scalar(yb, pf[:, 0:96], FILL + SHIFT, -1.0, A.add, A.max)], role="cast" + B)
+                op(n("st" + B), "y", [n("yev" + B)], lambda yb=yb, c=c: [
+                    g.sync.dma_start(T.y[64 * i:64 * i + 64, 2 * c:2 * c + 192], yb)], [], "r_st" + B + X, 16)
             return
         c0 = 192 * j
+        tiles = k > 0
         pls = ["pl" + X, "z1"] + (["pl" + X + "2"] if k > 0 else [])
         col = {"o": 48 * me - lo, "n": 48 * near - lo, "e": 96, "f": 144}
-        for B, r, pn, free in (("o", me, pX, []), ("n", near, pZ, prev(made("f")))):
-            ro("num" + B, "p", pe(48, 2 * twice), has[B] + pls + free, lambda pn=pn, r=r: group(
-                [(pn[:, 96:144], pl(h), s) for h in range(2) for s in slots(96 * r + h, 96 * r + 96, 2)]))
-        ro("numf", "p", pe(48, 4 * twice), has["f"] + pls + prev(made("e")), lambda: [group(
-            [(pY[:, 48 * e:48 * e + 48], pl(h), s) for h in range(2) for s in slots(2 * fo + 2 * e + h, 2 * fo + 192, 4)])[0]
-            for e in range(2)], calls=2)
-        if JOINF:
-            ro("numf", "p", pe(96, 2 * twice), has["f"] + pls + prev(made("f")), lambda: group(
-                [(pY[:, 0:96], pl(h), s) for h in range(2) for s in slots(2 * fo + h, 2 * fo + 192, 2)]))
-        for B, w, src in (("o", 48, pX[:, 96:144]), ("n", 48, pZ[:, 96:144]), ("f", 96, pY[:, 0:96])):
-            c = c0 + (96 if B == "f" else col[B])
-            ro("cast" + B, "v", cyc(w), [n("num" + B)], lambda c=c, w=w, src=src: [
-                V.tensor_scalar(T.off[:, c:c + w], src, 585.0 * (SHIFT - FILL) if k > 0 else 0.0, 4096.0, A.add, A.min)])
-        ro("mergen", "p", pe(48, 4 * twice), has["o"] + has["n"] + ["ii"], lambda: [group(
-            [(pW[:, 128 + 48 * r:176 + 48 * r], ii(h), s)
-             for h in range(2) for s in slots(96 * r + h, 96 * r + 96, 2)])[0] for r in (me, near)], calls=2, sem=not ONE)
-        ro("mergef", "p", pe(96, 2 * twice), has["f"] + ["ii"] + [n("evacn")] * (not ONE), lambda: group(
+        for B, r, pn, free in (("o", me, pX, []), ("n", near, pZ, prev("firef"))):
+            ro("num" + B, "p", has[B] + pls + free, lambda pn=pn, r=r: group(
+                [(pn[:, 96:144], pl(h), slots(96 * r + h, 96 * r + 96, 2)[0]) for h in range(2)]))
+        plain = lambda e, pn: group([(pn, pl(h), slots(2 * fo + 2 * e + h, 2 * fo + 192, 4)[0]) for h in range(2)])
+        tile = lambda t: group([(pZ[:, 48 + 24 * t:72 + 24 * t],
+                                 T.plm[:, 352 * t + at0(h) + 8 * (t - w):352 * t + at0(h) + 8 * (t - w) + 128],
+                                 slots(2 * fo + 2 + 4 * w + h, 2 * fo + 192, 8)[0]) for h in range(2) for w in range(2)])
+        ro("nume", "p", has["f"] + pls + prev("firee"), lambda: plain(0, pY[:, 0:48]))
+        ro("numf", "p", has["f"] + pls + [n("castn")] + ["plm0", "plm1"] * tiles,
+           lambda: tile(0) + tile(1) if tiles else plain(1, pZ[:, 48:96]), calls=1 + tiles)
+        for B, pn in (("o", pX[:, 96:144]), ("n", pZ[:, 96:144]), ("e", pY[:, 0:48]), ("f", pZ[:, 48:96])):
+            ro("cast" + B, "v", [n("num" + B)], lambda c=c0 + col[B], pn=pn: [
+                V.tensor_scalar(T.off[:, c:c + 48], pn, 585.0 * (SHIFT - FILL) if k > 0 else 0.0, TAB - 1.0, A.add, A.min)])
+        ro("mergen", "p", has["o"] + has["n"] + ["ii", "xm"] + ["ones"] * (j == 1), lambda: [group(
+            [(pW[:, 128 + 48 * r:176 + 48 * r], ii(h), s) for h in range(2) for s in slots(96 * r + h, 96 * r + 96, 2)])[0]
+            for r in (me, near)], sem=False)
+        ro("mergef", "p", has["f"], lambda: group(
             [(pW[:, 128 + fo:224 + fo], ii(h), s) for h in range(2) for s in slots(2 * fo + h, 2 * fo + 192, 2)]),
            soft=[n("mergen")])
-        evacs, incs = ([n(r + B) for B in ("f" if ONE else "nf")] for r in ("evac", "inc"))
-        for B, c, w in (("f", 0, 192),) if ONE else (("n", lo, 96), ("f", fo, 96)):
-            ro("evac" + B, "s", cyc(w), [n("merge" + B)], lambda c=c, w=w: [
-                S.activation(T.v[:, c0 + c:c0 + c + w], pW[:, 128 + c:128 + c + w], F.Identity,
-                             bias=-FILL if k > 0 else -SHIFT)])
-            ro("inc" + B, "v", cyc(w // 2), [n("evac" + B)], lambda c=c, w=w: [
-                V.tensor_scalar(T.inc[:, c0 + c:c0 + c + w], T.v[:, c0 + c:c0 + c + w], -8.0, 1.0, A.mult, A.min)])
+        v, inc, t = (buf[:, c0:c0 + 192] for buf in (T.v, T.inc, T.t))
+        ro("evac", "s", [n("mergef")], lambda: [
+            S.activation(v, pW[:, 128:320], F.Identity, bias=-FILL if k > 0 else -SHIFT)])
+        ro("inc", "v", [n("evac")], lambda: [V.tensor_scalar(inc, v, -8.0, 1.0, A.mult, A.min)])
         G0 = 3072 * j
         tab = T.lutw[:, TAB * i:TAB * i + TAB]
-        got = {}
+        got = []
         for B in "onef":
-            c, got[B] = col[B], []
+            c = col[B]
             for p, piece in enumerate(PIECES[k][i][B].split()):
                 q, w = piece[0], int(piece[1:])
                 out, win = T.gat[:, G0 + 16 * c:G0 + 16 * (c + w)], tab.indirect(T.off[:, c0 + c:c0 + c + w])
-                ro("g%s%d" % (B, p), q, 0.06 + GATH * 16 * w, [n("cast" + B.replace("e", "f")), "lut" + X, "z0"],
+                ro("g%s%d" % (B, p), q, [n("cast" + B), "lut" + X],
                    (lambda out=out, win=win: [S.activation(out, win, F.Copy)]) if q == "s" else
                    (lambda out=out, win=win: [V.tensor_copy(out, win)]))
-                got[B].append(n("g%s%d" % (B, p)))
+                got.append((c, c + w, n("g%s%d" % (B, p))))
                 c += w
+        pieces = lambda c, w: [nm for c1, c2, nm in got if c1 < c + w and c < c2]
+        po = T.po[:, 128 * i:128 * i + 128]
+        for B, c, w, at, ph, free in (("n", 0, 96, slice(c0 + lo, c0 + lo + 96), pX, []),
+                                      ("e", 96, 48, slice(c0 + fo, c0 + fo + 96, 2), pY, []),
+                                      ("f", 144, 48, slice(c0 + fo + 1, c0 + fo + 96, 2), pZ, [n("castn")])):
+            rh, z = T.rh[:, c0 + c:c0 + c + w], ph[:, 0:w]
+            for u0, sfx in ((0, "a"), (8, "")):
+                if B == "f" and tiles:
+                    dep, g0 = pieces(c + 3 * u0, 24), G0 + 16 * c + 48 * u0
+                    rhs = [T.gat[:, g0 + u:g0 + 384:8] for u in range(8)]
+                else:
+                    dep = pieces(c, w) if sfx else []
+                    rhs = [T.gat[:, G0 + 16 * c + u:G0 + 16 * (c + w):16] for u in range(u0, u0 + 8)]
+                ro("red" + B + sfx, "p", dep + (free + ["ident"] if sfx else []), lambda u0=u0, rhs=rhs, z=z: [[
+                    P.matmul(z, T.ident[:], r, u0 + u == 0, u0 + u == 15) for u, r in enumerate(rhs)][-1]],
+                   soft=[] if sfx else [n("red" + B + "a")], sem=not sfx)
+            ro("relu" + B, "v", [n("red" + B)], lambda rh=rh, z=z: [V.tensor_scalar(rh, z, 0.0, None, A.max)])
+            ro("pol" + B, "p", [n("relu" + B), "cv" + X], lambda rh=rh, z=z: group([(z, po, rh)]))
+            ro("fire" + B, "v", [n("pol" + B)], lambda z=z, at=at: [V.tensor_scalar(T.fire[:, at], z, 0.0, None, A.is_gt)])
+        for B, c, dep in (("n", c0 + lo, [n("firen")]), ("f", c0 + fo, [n("firee"), n("firef")])):
+            ro("t" + B, "v", dep + [n("inc")], lambda c=c: [
+                V.tensor_tensor(T.t[:, c:c + 96], T.fire[:, c:c + 96], T.inc[:, c:c + 96], A.mult)])
         lq = lambda q: cz[:, LB + 15 - q:LB + 143 - q]
-        for B, c, w, at, ph, pz, dep, hfree, zfree in (
-                ("n", 0, 96, slice(c0 + lo, c0 + lo + 96), pX, pX, got["o"] + got["n"], [], []),
-                ("f", 96, 96, slice(c0 + fo, c0 + fo + 96), pY, pY, got["e"] + got["f"], [], [])) if JOINF else (
-                ("n", 0, 96, slice(c0 + lo, c0 + lo + 96), pX, pX, got["o"] + got["n"], [], []),
-                ("e", 96, 48, slice(c0 + fo, c0 + fo + 96, 2), pY, pY, got["e"], [], []),
-                ("f", 144, 48, slice(c0 + fo + 1, c0 + fo + 96, 2), pZ, pZ, got["f"], [n("castn")], [])):
-            parts = [(B, c, w, dep, [])]
-            if B == "n" and APART[k]:
-                parts = [("o", col["o"], 48, got["o"], []), ("n", col["n"], 48, got["n"], [n("redo")])]
-            for R, rc, rw, rdep, after in parts:
-                for sfx, u0 in (("a", 0), ("", 8)):
-                    ro("red" + R + sfx, "p", pe(rw, 8), rdep + hfree + ["ident"] if sfx else [],
-                       lambda u0=u0, rc=rc, rw=rw, out=ph[:, rc - c:rc - c + rw]: [[
-                           P.matmul(out, T.ident[:], T.gat[:, G0 + 16 * rc + u:G0 + 16 * (rc + rw):16], u == 0, u == 15)
-                           for u in range(u0, u0 + 8)][-1]], soft=after if sfx else [n("red" + R + "a")],
-                       sem=not sfx and R == B)
-            rh, step = T.rh[:, c0 + c:c0 + c + w], T.inc[:, at]
-            ro("relu" + B, "v", cyc(w), [n("red" + B)], lambda rh=rh, ph=ph, w=w: [
-                V.tensor_scalar(rh, ph[:, 0:w], 0.0, None, A.max)])
-            if B in QUICK:
-                ro("pol" + B, "p", pe(w, 1), [n("relu" + B), "cv" + X] + zfree, lambda rh=rh, pz=pz, w=w: group(
-                    [(pz[:, 0:w], T.po[:, 128 * i:128 * i + 128], rh)]))
-                ro("fire" + B, "v", cyc(w), [n("pol" + B)], lambda pz=pz, w=w, at=at: [
-                    V.tensor_scalar(T.t[:, at], pz[:, 0:w], -8.0, None, A.is_lt)])
-                if B == "f":
-                    at = at if QUICK == "f" else slice(c0 + fo, c0 + fo + 96) if QUICK == "ef" else slice(c0, c0 + 192)
-                    ro("tf", "v", cyc(96 * {"f": 1, "ef": 2, "nef": 4}[QUICK]), [n("sff")] + incs, lambda at=at: [
-                        V.tensor_tensor(T.t[:, at], T.t[:, at], T.inc[:, at], A.mult)])
-                continue
-            ro("pol" + B, "p", pe(w, 2), [n("relu" + B), "cv" + X, n("incn" if B == "n" and not ONE else "incf")] + zfree,
-               lambda rh=rh, pz=pz, w=w, step=step: group(
-                   [(pz[:, 0:w], T.ident[:], step), (pz[:, 0:w], T.po[:, 128 * i:128 * i + 128], rh)]))
-            ro("fire" + B, "v", cyc(w), [n("pol" + B)], lambda pz=pz, w=w: [
-                V.tensor_scalar(pz[:, 0:w], pz[:, 0:w], -8.0, None, A.is_lt)])
-            ro("t" + B, "v", cyc(w), [n("fire" + B)], lambda pz=pz, w=w, step=step, at=at: [
-                V.tensor_tensor(T.t[:, at], pz[:, 0:w], step, A.mult)])
-        wfree = ["lb", n("evacf")]
-        sums = []
-        if k == 0:
-            sums += [("su", q0, range(q0, q0 + 8), T.v, 0, 12, evacs) for q0 in (0, 8)]
-        sums += [("si", e, range(e, 16, 2), T.inc, 0, 12, incs)
-                 for e, B in enumerate("ef") if B in QUICK]
-        sums.append(("sf", "e", range(0, 16, 2), T.t, 0, 12, [n(made("n")), n(made("e"))]))
-        sums.append(("sf", "f", range(1, 16, 2), T.t, 0, 12, [n(made("n")), n(made("f"))]))
-        last = []
-        for u, (nm, tag, qs, buf, cc, w, dep) in enumerate(sums):
-            ro(nm + str(tag), "p", pe(12, 8), dep + wfree, lambda u=u, qs=qs, buf=buf, cc=cc, w=w: [[
-                P.matmul(pW[:, cc:cc + w], lq(q), buf[:, c0 + 16 * cc + q:c0 + 16 * (cc + w):16], u == 0 and q == qs[0],
-                         u == len(sums) - 1 and q == 15) for q in qs][-1]], soft=last, sem=u == len(sums) - 1)
-            last = [n(nm + str(tag))]
+        rows = lambda buf, qs: [(pW[:, 0:12], lq(q), buf[:, c0 + q:c0 + 192:16]) for q in qs]
+        sums = [("su%d" % q0, rows(T.v, range(q0, q0 + 8)), [n("evac")]) for q0 in (0, 8) if k == 0]
+        sums.append(("sfe", rows(T.fire, range(0, 16, 2)), [n("firen"), n("firee"), n("evac")]))
+        if k > 0:
+            ro("turn", "v", [n("inc")], lambda: [V.transpose(T.it[:, c0:c0 + 192], inc)])
+            sums.append(("sj", [(pW[:, w:12:2], T.pw[:, 160 * w + 16 + 16 * (w - u):160 * w + 144 + 16 * (w - u)],
+                                 T.it[:, c0 + 16 * u:c0 + 192:32]) for w in range(2) for u in range(2)], [n("turn"), "pw"]))
+        sums.append(("sff", rows(T.fire, range(1, 16, 2)), [n("firen"), n("firef")]))
+        for u, (nm, mms, dep) in enumerate(sums):
+            ro(nm, "p", dep + ["lb"], lambda u=u, mms=mms: [[
+                P.matmul(o, l, r, u == 0 and x == 0, u == len(sums) - 1 and x == 7) for x, (o, l, r) in enumerate(mms)][-1]],
+               soft=[n(sums[u - 1][0])] if u else [], sem=u == len(sums) - 1)
         m0, e0, x0, s0, W0 = 5 * SEG * i, 64 * j, 48 * j, 16 * j, WIN * j
-        ro("floor", "v", cyc(12, 5), [n("sff")], lambda: [
+        ro("floor", "v", [n("sff")], lambda: [
             V.tensor_scalar(T.m[:, m0 + SEG * u + 1:m0 + SEG * u + SEG], pW[:, 0:12],
-                            768 - 1.5 + 4 - u + (me if k > 0 else 16 * SHIFT), 512.0, A.add, A.max)
+                            768 - 1.5 + 4 - u + (me - 1 if k else 16 * SHIFT), 512.0 if k else 1024.0, A.add,
+                            A.max if k else A.min)
             for u in range(5)], calls=5)
-        ro("scan", "v", cyc(26), [n("floor"), "rp"], lambda: [
+        ro("scan", "v", [n("floor"), "rp"], lambda: [
             V.tensor_tensor_scan(T.e[:, e0:e0 + 4 * SEG], T.m[:, m0:m0 + 4 * SEG], T.m[:, m0 + SEG:m0 + 5 * SEG], 0.0,
                                  A.add, A.subtract)])
-        ro("rank0", "p", pe(48, 1), [n("floor"), "ones", "beta"], lambda: [
+        ro("rankb", "p", [n("floor"), "ones", "beta"], lambda: [
             P.matmul(pW[:, 64:112], T.ones[:], T.beta[:], True, False)], sem=False)
-        if RANKM:
-            ro("rankm", "p", pe(12, 8), [n("floor"), "ua", "ub"], lambda: [[
-                P.matmul(pW[:, 64 + r:112:4], u[:], T.m[:, m0 + SEG * (r + d) + 1:m0 + SEG * (r + d) + 13], False, False)
-                for r in range(4) for u, d in ((T.ua, 0), (T.ub, 1))][-1]], soft=[n("rank0")], sem=False)
-            ro("rank", "p", pe(12, 4), [n("scan")], lambda: [[
-                P.matmul(pW[:, 64 + r:112:4], T.ones[:], T.e[:, e0 + SEG * r:e0 + SEG * r + 12], False, r == 3)
-                for r in range(4)][-1]], soft=[n("rankm")])
-        else:
-            ro("rank", "p", pe(12, 8), [n("scan"), "ua", "ub"], lambda: [[
-                P.matmul(pW[:, 64 + r:112:4], u[:], T.e[:, e0 + SEG * r + d:e0 + SEG * r + d + 12], False, r == 3 and d == 1)
-                for r in range(4) for u, d in ((T.ub, 0), (T.ua, 1))][-1]], soft=[n("rank0")])
-        ro("smax", "v", cyc(48), [n("rank"), "tr"], lambda: [
+        ro("rankm", "p", [n("floor"), "ua", "ub"], lambda: [[
+            P.matmul(pW[:, 64 + r:112:4], u[:], T.m[:, m0 + SEG * (r + d) + 1:m0 + SEG * (r + d) + 13], False, False)
+            for r in range(4) for u, d in ((T.ua, 0), (T.ub, 1))][-1]], soft=[n("rankb")], sem=False)
+        ro("rank", "p", [n("scan")], lambda: [[
+            P.matmul(pW[:, 64 + r:112:4], T.ones[:], T.e[:, e0 + SEG * r:e0 + SEG * r + 12], False, r == 3)
+            for r in range(4)][-1]], soft=[n("rankm")])
+        ro("smax", "v", [n("rank"), "tr"], lambda: [
             V.tensor_tensor_scan(T.sm[:, x0:x0 + 48], T.tr[:], pW[:, 64:112], 1.0e6, A.min, A.max)])
-        ro("cidx", "v", cyc(12), [n("smax")], lambda: [
+        ro("cidx", "v", [n("smax")], lambda: [
             V.tensor_scalar(T.idx[:, s0:s0 + 12], T.sm[:, x0 + 3:x0 + 48:4], 0.25, None, A.mult)])
         reg = lambda r: T.win[:, W0 + BASE + REG * r:W0 + BASE + REG * r + CAP]
         mark = int(FILL) if k < NP - 1 else -int(FILL)
         for r in range(NR):
-            ro("fill%d_" % r, "g", gp(CAP), prev("scat"), lambda r=r: [iota(reg(r), [[0, CAP]], mark, 0)],
+            ro("fill%d_" % r, "g", prev("scat") or ["go"], lambda r=r: [iota(reg(r), [[0, CAP]], mark, 0)],
                soft=[n("fill%d_" % (r - 1))] if r else prev("sendf"), role="fill")
-        ro("scat", "v", 0.05 + SCAT * 192, [n("cidx"), n(made("n")), n(made("e")), n("tf"), n("fill3_")] + evacs,
-           lambda: [V.tensor_tensor(T.win[:, W0:W0 + WIN].indirect(T.idx[:, s0:s0 + 12]), T.v[:, c0:c0 + 192],
-                                    T.t[:, c0:c0 + 192], A.add)])
+        ro("scat", "v", [n("cidx"), n("tn"), n("tf"), n("fill3_")], lambda: [
+            V.tensor_tensor(T.win[:, W0:W0 + WIN].indirect(T.idx[:, s0:s0 + 12]), v, t, A.add)])
         mine = T.land[:, 384 * j + CAP * me:384 * j + CAP * me + CAP]
 
-        def send(B, to):
+        def send(B):
             tr = []
-            for u, r in enumerate(to):
+            for u, r in enumerate(calls[B]):
                 eng = topo.engines(T.cores[me], T.cores[r])
-                w = len(eng) // len(to)
+                w = len(eng) // len(calls[B])
                 rid, pid, _ = topo.addr(T.cores[r])
                 tr.append(RemoteDMATransfer(dst_ids=[DstId(rid=rid, pnc=pid)],
                                             dma_engine_mask=sum(1 << e for e in eng[u * w:(u + 1) * w]),
@@ -342,59 +301,15 @@ def graph(g, T, me, topo):
             g.remote_dma_fused(tr, local_sem=T.sem["sent" + X])
             return []
 
-        for B, to, lat, soft in (("n", [near], NEAR, []), ("f", far, FAR - CALL, [n("sendn")])):
-            ro("send" + B, "g", CALL + (FIRST if j == 0 and B == "n" else 0.0), [n("scat")], lambda B=B, to=to: send(B, to), soft=soft, sem=False)
-            come = sum(len(topo.engines(T.cores[r], T.cores[me])) // len(to) for r in to)
-            op(n("arr" + B), None, 0.0, [], None, [n("send" + B)], n("arr" + B), come, lat=lat - CALL)
+        for B, soft in (("n", []), ("f", [n("sendn")])):
+            ro("send" + B, "g", [n("scat")], lambda B=B: send(B), soft=soft, sem=False)
+            come = sum(len(topo.engines(T.cores[r], T.cores[me])) // len(calls[B]) for r in calls[B])
+            op(n("arr" + B), None, [], None, [n("send" + B)], n("arr" + B), come)
 
     for k in range(NP + 1):
         for i, X in enumerate("AB"):
             half(k, i, X)
-    return ops, sum(len(topo.engines(T.cores[me], T.cores[r])) for r in (near, far[0]))
-
-
-def schedule(ops):
-    deps = {n: o["hard"] + o["soft"] for n, o in ops.items()}
-    users = {n: [] for n in ops}
-    for n in ops:
-        for d in deps[n]:
-            users[d].append(n)
-    way = {}
-    left, order = dict((n, len(set(deps[n]))) for n in ops), []
-    todo = [n for n in ops if left[n] == 0]
-    while todo:
-        n = todo.pop()
-        order.append(n)
-        for u in set(users[n]):
-            left[u] -= 1
-            if left[u] == 0:
-                todo.append(u)
-    for n in reversed(order):
-        way[n] = ops[n]["lat"] + max([HOP + way[u] for u in users[n]] + [0.0])
-    for n in way:
-        way[n] += BIAS.get(n[:-2], 0.0) + (LEAD[int(n[-2])] if n[-1] == "A" and n[-2].isdigit() else 0.0)
-        if not n[-2].isdigit():
-            way[n] += LEAD[0]
-    end, issued, free, out = {}, {}, {}, {}
-    left = dict((n, len(set(deps[n]))) for n in ops)
-    todo = [n for n in ops if left[n] == 0]
-    while todo:
-        start = {n: max([free.get(ops[n]["q"], 0.0)] + [end[d] + HOP for d in ops[n]["hard"]]
-                        + [issued[d] for d in ops[n]["soft"]]) for n in todo}
-        first = min(todo, key=lambda n: start[n] + ops[n]["dur"])
-        q = ops[first]["q"]
-        n = max([m for m in todo if ops[m]["q"] == q and start[m] <= start[first] + SLACK * ops[first]["dur"]],
-                key=lambda m: way[m]) if q else first
-        end[n], issued[n] = start[n] + ops[n]["lat"], start[n] + ops[n]["dur"]
-        if q:
-            free[q] = issued[n]
-            out.setdefault(q, []).append(n)
-        todo.remove(n)
-        for u in set(users[n]):
-            left[u] -= 1
-            if left[u] == 0:
-                todo.append(u)
-    return out
+    return ops, sum(len(topo.engines(T.cores[me], T.cores[r])) // len(c) for c in calls.values() for r in c)
 
 
 def timetable(ops):
@@ -405,7 +320,7 @@ def timetable(ops):
             key[n] = tab[""][n]
         else:
             k, X = int(n[-2]), n[-1]
-            key[n] = tab[X if k else "0" + X].get(n[:-2], 0.0) + OFFS[2 * k + "AB".index(X)]
+            key[n] = tab.get(n[-2:], tab["*"]).get(n[:-2], 0.0) + OFFS[2 * k + "AB".index(X)]
     done, out, todo = set(), {}, sorted(ops, key=lambda n: key[n])
     while todo:
         n = next(n for n in todo if all(d in done for d in ops[n]["hard"] + ops[n]["soft"]))
@@ -442,7 +357,7 @@ def rank_program(g, core, T, topo):
     if me is None:
         return
     ops, sent = graph(g, T, me, topo)
-    order = timetable(ops) if TIME else schedule(ops)
+    order = timetable(ops)
     need = waits(ops, order)
     queue = {"v": g.vector, "s": g.scalar, "p": g.tensor, "y": g.sync, "g": g}
     total, mark = {}, {}

from concourse.bass import DstId, RemoteDMATransfer
from concourse.mybir import AluOpType, ActivationFunctionType

A = AluOpType
F = ActivationFunctionType
NP, CAP, NR = 4, 96, 4
WIN, BASE, REG = 1856, 320, 384
FILL, SHIFT = 1024.0, 6.125
TAB = 4096
SEG = 13
PL0 = 80
HDT = "float16"
LOADS = {"s": "ldx plA", "y": "lutA plB polA lutB polB plA2 plB2"}
PIECES = ([[{'o': 'v48', 'n': 's48', 'e': 's24 v24', 'f': 's24 v12 v12'},
            {'o': 's48', 'n': 's36 v12', 'e': 's12 s36', 'f': 'v12 s24 s12'}]]
          + [[{'o': 's36 v12', 'n': 'v16 s32', 'e': 'v16 s32', 'f': 's24 s24'}] * 2] * (NP - 1))
TIME = {
    '': 'z2 -0.12 ldx 0 lutA 0 z1 0.01 plA 0.05 tr 0.05 plB 0.1 polA 0.15 lutB 0.25 z3 0.25 polB 0.35 plA2 0.45 plB2 0.5 all 0.64 xm 1.34 ident 1.41 gmm 1.55 gsel 1.82 ones 1.96 ii 1.97 beta 2.11 go 2.13 z4 2.82 ua 3.5 cvA 4.79 lb 5.34 zz 6.21 cvB 6.54 pw 6.64 plm0 6.84 ub 7.17 rp 7.47 plm1 8.62',
    '0A': 'numn 1.92 nume 1.97 castn 2.37 numo 2.42 ge0 2.61 castf 2.66 mergen 2.69 casto 2.79 caste 2.81 numf 2.91 ge1 3.19 mergef 3.35 go0 3.54 gn0 3.72 redea 4.03 rede 4.2 gf1 4.47 gf2 4.67 gf0 4.7 redn 4.81 evac 4.9 fill0_ 4.93 redna 5.01 fill2_ 5.08 relue 5.16 fill1_ 5.35 redf 5.37 redfa 5.59 inc 5.8 fill3_ 5.92 poln 5.95 polf 6.01 relun 6.07 pole 6.2 su0 6.2 reluf 6.25 su8 6.55 firen 6.75 sff 6.78 firee 6.89 firef 6.9 sfe 6.94 tf 7.39 rankb 7.67 floor 7.89 tn 8.28 scan 8.38 cidx 8.46 rankm 8.47 rank 8.64 smax 8.71 scat 9.32 sendn 10.25 sendf 11.9',
    '0B': 'mergef 2.46 mergen 3.02 nume 3.49 numn 3.69 fill0_ 3.92 numo 3.94 fill1_ 4.09 caste 4.37 castn 4.77 ge0 5.13 ge1 5.85 casto 5.88 numf 5.96 castf 6.35 go0 6.75 redea 7.14 gf0 7.28 rede 7.65 gn0 7.75 fill2_ 8.14 gn1 8.44 redn 8.52 gf2 8.53 gf1 9 redna 9.02 evac 9.09 redfa 9.14 redf 9.15 relun 9.34 fill3_ 9.42 relue 9.49 inc 9.84 firen 9.93 reluf 10.16 poln 10.18 pole 10.42 su0 10.59 firee 10.72 polf 10.87 su8 10.91 firef 11.1 sfe 11.14 sff 11.44 floor 11.89 scan 11.98 tf 12.49 rankb 12.53 rankm 12.68 rank 12.91 smax 12.92 tn 13.12 cidx 13.16 scat 14 sendn 15.3 sendf 15.61',
    '*': 'numo 0.79 casto 1.25 fill0_ 1.28 go0 1.57 fill1_ 2 go1 2.04 castn 2.12 numn 2.16 fill2_ 2.23 fill3_ 2.76 mergen 2.78 gn1 2.84 caste 2.9 gn0 2.98 finn 3 nume 3.08 numf 3.23 mergef 3.45 castf 3.52 finf 3.53 ge0 3.54 yevn 3.56 stn 3.76 yevf 3.87 ge1 3.97 redna 3.99 redn 4.26 stf 4.57 redea 4.65 redfa 4.84 rede 4.85 gf0 4.86 relun 4.88 relue 5.32 gf1 5.38 evac 5.39 poln 5.57 redf 5.58 firee 5.69 inc 5.77 firen 6.05 reluf 6.09 pole 6.24 turn 6.25 firef 6.3 sff 6.45 polf 6.53 sfe 6.91 tn 7.04 sj 7.14 floor 7.46 scan 7.62 rank 8.02 rankm 8.07 smax 8.19 rankb 8.27 tf 8.88 cidx 9.08 scat 9.24 sendf 9.86 sendn 10.15'}
OFFS = [0, 0, 9.84, 14.3, 18.72, 23.11, 27.51, 31.78, 40.69, 52.82]

SCRATCH = {
    "lutw": ("sbuf", [128, 2 * TAB], "bfloat16"),
    "xs": ("sbuf", [128, 384], "bfloat16"),
    "xm": ("sbuf", [128, 384], "bfloat16"),
    "plb": ("sbuf", [128, 352], "bfloat16"),
    "plm": ("sbuf", [128, 2 * 352], "bfloat16"),
    "pob": ("sbuf", [128, 256], "bfloat16"),
    "po": ("sbuf", [128, 256], HDT),
    "cz": ("sbuf", [128, 480], "bfloat16"),
    "full": ("sbuf", [128, 128], "bfloat16"),
    "gsel": ("sbuf", [128, 128], "bfloat16"),
    "ident": ("sbuf", [128, 128], "bfloat16"),
    "ones": ("sbuf", [128, 128], "bfloat16"),
    "go": ("sbuf", [128, 128], "bfloat16"),
    "ua": ("sbuf", [128, 128], "bfloat16"),
    "ub": ("sbuf", [128, 128], "bfloat16"),
    "pw": ("sbuf", [128, 320], "bfloat16"),
    "it": ("sbuf", [128, 8 * 192], "bfloat16"),
    "beta": ("sbuf", [128, 48], "bfloat16"),
    "tr": ("sbuf", [128, 48], "float32"),
    "off": ("sbuf", [128, 8 * 192], "uint16"),
    "gat": ("sbuf", [128, 8 * 3072], "bfloat16"),
    "v": ("sbuf", [128, 8 * 192], "bfloat16"),
    "inc": ("sbuf", [128, 8 * 192], "bfloat16"),
    "rh": ("sbuf", [128, 8 * 192], HDT),
    "fire": ("sbuf", [128, 8 * 192], "bfloat16"),
    "t": ("sbuf", [128, 8 * 192], "bfloat16"),
    "m": ("sbuf", [128, 2 * 5 * SEG], "bfloat16"),
    "e": ("sbuf", [128, 8 * 64], "bfloat16"),
    "sm": ("sbuf", [128, 8 * 48], "float32"),
    "idx": ("sbuf", [128, 8 * 16], "uint16"),
    "win": ("sbuf", [128, 8 * WIN], "bfloat16"),
    "land": ("sbuf", [128, 8 * 384], "bfloat16"),
    "yb": ("sbuf", [128, 4 * 96], "bfloat16"),
}
for _h in "AB":
    for _b in "XYZW":
        SCRATCH["p" + _b + _h] = ("psum", [128, 512], "float32")

START = ["z1", "z2", "z3", "z4", "pw", "all", "gsel", "gmm", "beta", "rp", "tr", "ident", "ii", "ones", "lb", "zz", "go", "ua",
         "ub", "xm", "plm0", "plm1", "ldx", "lutA", "lutB", "plA", "plB", "plA2", "plB2", "polA", "polB", "cvA", "cvB"]
ROLES = ([r + b for r in ("num", "cast") for b in "onef"] + ["g" + b + str(p) for b in "onef" for p in range(3)]
         + [r + b for r in ("red", "relu", "pol", "fire") for b in "nef"]
         + ["mergef", "evac", "inc", "turn", "tn", "tf", "sff", "floor", "scan", "rank", "smax", "cidx", "scat", "fill",
            "stn", "stf"])
SEMAPHORES = (["s_" + n for n in START] + ["r_" + r + x for r in ROLES for x in "AB"]
              + ["arr%s%d%s" % (b, k, x) for b in "nf" for k in range(NP) for x in "AB"] + ["sentA", "sentB"])


def sides(cores, me, topo):
    far = [r for r in range(NR) if topo.die(cores[r]) != topo.die(cores[me])]
    return [r for r in range(NR) if r != me and r not in far][0], far


def graph(g, T, me, topo):
    ops = {}
    V, S, P = g.vector, g.scalar, g.tensor
    near, far = sides(T.cores, me, topo)

    def op(name, q, hard, emit, soft=(), sem=None, inc=1, calls=1):
        ops[name] = dict(q=q, hard=list(hard), soft=list(soft), emit=emit, sem=sem, inc=inc, calls=calls)

    def st(name, q, hard, emit, calls=1):
        op(name, q, hard, emit, sem="s_" + name, calls=calls)

    II, LB, ZZ = 0, 192, 336
    cz = T.cz
    iota = lambda o, pat, b, cm: g.iota(o, pat, b, cm, allow_small_or_imprecise_dtypes=True)
    st("z1", "v", [], lambda: [V.memset(T.plb[:, a:b], 0.0)
                               for a, b in ((0, PL0), (PL0 + 64, PL0 + 128), (PL0 + 192, 352))], 3)
    st("z2", "v", [], lambda: [V.memset(T.pob[64 * h:64 * h + 64, c - 64 * h:c - 64 * h + 64], 0.0)
                               for h in range(2) for c in (64, 192)], 4)
    queue = {"s": S, "y": g.sync}
    src = {"ldx": lambda D: [D.dma_start(T.xs[:], T.x[:])]}
    for i, X in enumerate("AB"):
        src["lut" + X] = lambda D, i=i: [
            D.dma_start(T.lutw[64 * h:64 * h + 64, TAB * i:TAB * i + TAB], T.lut[64 * i:64 * i + 64, :])
            for h in range(2)]
        for nm, h in (("pl" + X, i), ("pl" + X + "2", 1 - i)):
            src[nm] = lambda D, i=i, h=h: [D.dma_start(T.plb[64 * h:64 * h + 64, PL0 + 128 * i:PL0 + 64 + 128 * i],
                                                       T.pl[64 * i:64 * i + 64, 64 * i:64 * i + 64])]
        src["pol" + X] = lambda D, i=i: [
            D.dma_start(T.pob[64 * h:64 * h + 64, 128 * i + 64 * h:128 * i + 64 * h + 64],
                        T.pol[64 * i:64 * i + 64, 64 * i:64 * i + 64]) for h in range(2)]
        st("cv" + X, "v", ["pol" + X, "z2"], lambda i=i: [
            V.tensor_copy(T.po[:, 128 * i:128 * i + 128], T.pob[:, 128 * i:128 * i + 128])])
    for q in LOADS:
        last = []
        for nm in LOADS[q].split():
            op(nm, q, [], lambda nm=nm, q=q: src[nm](queue[q]), last, "s_" + nm, 16, 2 if nm[:3] in ("lut", "pol") else 1)
            last = [nm]
    st("z3", "v", [], lambda: [V.memset(cz[:], 0.0)])
    st("all", "v", [], lambda: [V.memset(T.full[:], 1.0)])
    st("beta", "g", [], lambda: [iota(T.beta[:], [[0, 12], [REG // 8, 4]], BASE // 8 - 256, 0)])
    st("rp", "v", [], lambda: [V.memset(T.m[:, 0:10 * SEG:SEG], 2.0 ** 30)])
    st("tr", "g", [], lambda: [iota(T.tr[:], [[-64, 12], [16384, 4]], 4 * BASE - 4, -4)])
    st("ident", "g", ["all"], lambda: [g.affine_select(T.ident[:], T.full[:], [[-1, 128]], A.is_equal, 0.0, 0, 1)])
    st("gsel", "g", ["all"], lambda: [
        g.affine_select(T.gsel[0:4, :], T.full[0:4, :], [[0, 2], [1, 4], [0, 16]], A.is_equal, 0.0, 0, -1)])
    st("gmm", "p", ["gsel"], lambda: [P.matmul(T.pWB[:, 0:128], T.gsel[0:4, :], T.gsel[0:4, :], True, True)])
    st("ones", "s", ["gmm"], lambda: [S.activation(T.ones[:], T.pWB[:, 0:128], F.Copy)])
    st("ii", "v", ["ident", "z3"],
       lambda: [V.tensor_tensor(cz[:, II + 64:II + 128], T.ident[:, 0:64], T.ident[:, 64:128], A.add)])
    st("lb", "v", ["ones", "z3"], lambda: [
        V.tensor_copy(cz[64 * h:64 * h + 64, LB + 15 + 64 * h:LB + 79 + 64 * h:16],
                      T.ones[64 * h:64 * h + 64, 64 * h:64 * h + 64:16]) for h in range(2)], 2)
    st("zz", "v", ["ii", "z3"], lambda: [V.tensor_copy(cz[:, ZZ + 1:ZZ + 129:2], cz[:, II + 64:II + 128])])
    st("go", "g", ["ones", "ident", "beta", "tr"], lambda: [
        g.affine_select(T.go[64 * h:64 * h + 64, :], T.ones[64 * h:64 * h + 64, :], [[1, 2], [2, 64]], A.is_gt, 0.0, -h, -2)
        for h in range(2)], 2)
    st("ua", "g", ["go"], lambda: [g.affine_select(T.ua[:], T.go[:], [[-1, 128]], A.not_equal, 2048.0, 0, 1)])
    st("ub", "v", ["ua"], lambda: [V.tensor_scalar(T.ub[:], T.ua[:], -1.0, None, A.mult)])
    st("xm", "v", ["ldx"], lambda: [V.tensor_scalar(T.xm[:], T.xs[:], 0.0, -FILL, A.min, A.mult)])
    st("z4", "v", [], lambda: [V.memset(T.pw[:], 0.0)])
    st("pw", "g", ["ident", "z4", "fill3_0A"], lambda: [
        g.affine_select(T.pw[:, 160 * w + 16:160 * w + 144], T.ident[:], [[0, 4], [1, 2], [0, 16]], A.is_equal, 0.0, -w, 0)
        for w in range(2)], 2)
    for t in range(2):
        st("plm%d" % t, "g", ["plA", "plB", "plA2", "plB2", "z1", "fill3_0A", "ua"], lambda t=t: [
            g.affine_select(T.plm[:, 352 * t:352 * t + 352], T.plb[:], [[0, 22], [2 * t - 1, 16]], A.is_ge, 0.0,
                            7 - 15 * t, 0)])

    lo, fo = 48 * min(me, near), 48 * min(far)
    calls = {"n": [near], "f": far}

    def half(k, i, X):
        n = lambda r, kk=k: "%s%d%s" % (r, kk, X)
        j = 2 * k + i

        def ro(r, q, hard, emit, soft=(), sem=True, calls=1, role=None):
            op(n(r), q, hard, emit, soft, ("r_" + (role or r) + X) if sem else None, 1, calls)

        def group(mms):
            return [[P.matmul(o, l, r, u == 0, u == len(mms) - 1) for u, (o, l, r) in enumerate(mms)][-1]]

        prev = lambda *rs: [n(r, k - 1) for r in rs] if k > 0 else []
        pX, pY, pZ, pW = (T["p" + b + X] for b in "XYZW")
        a, b = (64 * i, 64 * i + 64) if k == 0 else (0, 128)
        at0 = lambda h: PL0 + 128 * i - 64 * h
        pl = lambda h: T.plb[a:b, at0(h):at0(h) + 128]
        ii = lambda h: cz[a:b, II + 64 - 64 * h:II + 192 - 64 * h]

        def slots(s0, s1, step):
            if k == 0:
                return [T.xs[a:b, s0:s1:step], T.xm[a:b, s0:s1:step]]
            if s0 // CAP == me:
                w = WIN * (j - 2) + BASE + (REG - CAP) * me
                return [T.win[:, w + s0:w + s1:step]]
            return [T.land[:, 384 * (j - 2) + s0:384 * (j - 2) + s1:step]]

        has = {"o": prev("scat"), "n": prev("arrn"), "f": prev("arrf")} if k > 0 else dict.fromkeys("onf", ["ldx"])
        if k == NP:
            for u, (B, c, pf, dep) in enumerate((("n", lo, pX, has["o"] + has["n"]),
                                                 ("f", fo, pY, has["f"] + prev("firee")))):
                yb = T.yb[:, 192 * i + 96 * u:192 * i + 96 * u + 96]
                ro("fin" + B, "p", dep + ["zz"], lambda c=c, pf=pf: group(
                    [(pf[:, 0:96], cz[:, ZZ + 1 - h:ZZ + 129 - h], slots(2 * c + 96 * h, 2 * c + 96 * h + 96, 1)[0])
                     for h in range(2)]), role="num" + B)
                ro("yev" + B, "v", [n("fin" + B)], lambda yb=yb, pf=pf: [
                    V.tensor_scalar(yb, pf[:, 0:96], FILL + SHIFT, -1.0, A.add, A.max)], role="cast" + B)
                op(n("st" + B), "y", [n("yev" + B)], lambda yb=yb, c=c: [
                    g.sync.dma_start(T.y[64 * i:64 * i + 64, 2 * c:2 * c + 192], yb)], [], "r_st" + B + X, 16)
            return
        c0 = 192 * j
        tiles = k > 0
        pls = ["pl" + X, "z1"] + (["pl" + X + "2"] if k > 0 else [])
        col = {"o": 48 * me - lo, "n": 48 * near - lo, "e": 96, "f": 144}
        for B, r, pn, free in (("o", me, pX, []), ("n", near, pZ, prev("firef"))):
            ro("num" + B, "p", has[B] + pls + free, lambda pn=pn, r=r: group(
                [(pn[:, 96:144], pl(h), slots(96 * r + h, 96 * r + 96, 2)[0]) for h in range(2)]))
        plain = lambda e, pn: group([(pn, pl(h), slots(2 * fo + 2 * e + h, 2 * fo + 192, 4)[0]) for h in range(2)])
        tile = lambda t: group([(pZ[:, 48 + 24 * t:72 + 24 * t],
                                 T.plm[:, 352 * t + at0(h) + 8 * (t - w):352 * t + at0(h) + 8 * (t - w) + 128],
                                 slots(2 * fo + 2 + 4 * w + h, 2 * fo + 192, 8)[0]) for h in range(2) for w in range(2)])
        ro("nume", "p", has["f"] + pls + prev("firee"), lambda: plain(0, pY[:, 0:48]))
        ro("numf", "p", has["f"] + pls + [n("castn")] + ["plm0", "plm1"] * tiles,
           lambda: tile(0) + tile(1) if tiles else plain(1, pZ[:, 48:96]), calls=1 + tiles)
        for B, pn in (("o", pX[:, 96:144]), ("n", pZ[:, 96:144]), ("e", pY[:, 0:48]), ("f", pZ[:, 48:96])):
            ro("cast" + B, "v", [n("num" + B)], lambda c=c0 + col[B], pn=pn: [
                V.tensor_scalar(T.off[:, c:c + 48], pn, 585.0 * (SHIFT - FILL) if k > 0 else 0.0, TAB - 1.0, A.add, A.min)])
        ro("mergen", "p", has["o"] + has["n"] + ["ii", "xm"] + ["ones"] * (j == 1), lambda: [group(
            [(pW[:, 128 + 48 * r:176 + 48 * r], ii(h), s) for h in range(2) for s in slots(96 * r + h, 96 * r + 96, 2)])[0]
            for r in (me, near)], sem=False)
        ro("mergef", "p", has["f"], lambda: group(
            [(pW[:, 128 + fo:224 + fo], ii(h), s) for h in range(2) for s in slots(2 * fo + h, 2 * fo + 192, 2)]),
           soft=[n("mergen")])
        v, inc, t = (buf[:, c0:c0 + 192] for buf in (T.v, T.inc, T.t))
        ro("evac", "s", [n("mergef")], lambda: [
            S.activation(v, pW[:, 128:320], F.Identity, bias=-FILL if k > 0 else -SHIFT)])
        ro("inc", "v", [n("evac")], lambda: [V.tensor_scalar(inc, v, -8.0, 1.0, A.mult, A.min)])
        G0 = 3072 * j
        tab = T.lutw[:, TAB * i:TAB * i + TAB]
        got = []
        for B in "onef":
            c = col[B]
            for p, piece in enumerate(PIECES[k][i][B].split()):
                q, w = piece[0], int(piece[1:])
                out, win = T.gat[:, G0 + 16 * c:G0 + 16 * (c + w)], tab.indirect(T.off[:, c0 + c:c0 + c + w])
                ro("g%s%d" % (B, p), q, [n("cast" + B), "lut" + X],
                   (lambda out=out, win=win: [S.activation(out, win, F.Copy)]) if q == "s" else
                   (lambda out=out, win=win: [V.tensor_copy(out, win)]))
                got.append((c, c + w, n("g%s%d" % (B, p))))
                c += w
        pieces = lambda c, w: [nm for c1, c2, nm in got if c1 < c + w and c < c2]
        po = T.po[:, 128 * i:128 * i + 128]
        for B, c, w, at, ph, free in (("n", 0, 96, slice(c0 + lo, c0 + lo + 96), pX, []),
                                      ("e", 96, 48, slice(c0 + fo, c0 + fo + 96, 2), pY, []),
                                      ("f", 144, 48, slice(c0 + fo + 1, c0 + fo + 96, 2), pZ, [n("castn")])):
            rh, z = T.rh[:, c0 + c:c0 + c + w], ph[:, 0:w]
            for u0, sfx in ((0, "a"), (8, "")):
                if B == "f" and tiles:
                    dep, g0 = pieces(c + 3 * u0, 24), G0 + 16 * c + 48 * u0
                    rhs = [T.gat[:, g0 + u:g0 + 384:8] for u in range(8)]
                else:
                    dep = pieces(c, w) if sfx else []
                    rhs = [T.gat[:, G0 + 16 * c + u:G0 + 16 * (c + w):16] for u in range(u0, u0 + 8)]
                ro("red" + B + sfx, "p", dep + (free + ["ident"] if sfx else []), lambda u0=u0, rhs=rhs, z=z: [[
                    P.matmul(z, T.ident[:], r, u0 + u == 0, u0 + u == 15) for u, r in enumerate(rhs)][-1]],
                   soft=[] if sfx else [n("red" + B + "a")], sem=not sfx)
            ro("relu" + B, "v", [n("red" + B)], lambda rh=rh, z=z: [V.tensor_scalar(rh, z, 0.0, None, A.max)])
            ro("pol" + B, "p", [n("relu" + B), "cv" + X], lambda rh=rh, z=z: group([(z, po, rh)]))
            ro("fire" + B, "v", [n("pol" + B)], lambda z=z, at=at: [V.tensor_scalar(T.fire[:, at], z, 0.0, None, A.is_gt)])
        for B, c, dep in (("n", c0 + lo, [n("firen")]), ("f", c0 + fo, [n("firee"), n("firef")])):
            ro("t" + B, "v", dep + [n("inc")], lambda c=c: [
                V.tensor_tensor(T.t[:, c:c + 96], T.fire[:, c:c + 96], T.inc[:, c:c + 96], A.mult)])
        lq = lambda q: cz[:, LB + 15 - q:LB + 143 - q]
        rows = lambda buf, qs: [(pW[:, 0:12], lq(q), buf[:, c0 + q:c0 + 192:16]) for q in qs]
        sums = [("su%d" % q0, rows(T.v, range(q0, q0 + 8)), [n("evac")]) for q0 in (0, 8) if k == 0]
        sums.append(("sfe", rows(T.fire, range(0, 16, 2)), [n("firen"), n("firee"), n("evac")]))
        if k > 0:
            ro("turn", "v", [n("inc")], lambda: [V.transpose(T.it[:, c0:c0 + 192], inc)])
            sums.append(("sj", [(pW[:, w:12:2], T.pw[:, 160 * w + 16 + 16 * (w - u):160 * w + 144 + 16 * (w - u)],
                                 T.it[:, c0 + 16 * u:c0 + 192:32]) for w in range(2) for u in range(2)], [n("turn"), "pw"]))
        sums.append(("sff", rows(T.fire, range(1, 16, 2)), [n("firen"), n("firef")]))
        for u, (nm, mms, dep) in enumerate(sums):
            ro(nm, "p", dep + ["lb"], lambda u=u, mms=mms: [[
                P.matmul(o, l, r, u == 0 and x == 0, u == len(sums) - 1 and x == 7) for x, (o, l, r) in enumerate(mms)][-1]],
               soft=[n(sums[u - 1][0])] if u else [], sem=u == len(sums) - 1)
        m0, e0, x0, s0, W0 = 5 * SEG * i, 64 * j, 48 * j, 16 * j, WIN * j
        ro("floor", "v", [n("sff")], lambda: [
            V.tensor_scalar(T.m[:, m0 + SEG * u + 1:m0 + SEG * u + SEG], pW[:, 0:12],
                            768 - 1.5 + 4 - u + (me - 1 if k else 16 * SHIFT), 512.0 if k else 1024.0, A.add,
                            A.max if k else A.min)
            for u in range(5)], calls=5)
        ro("scan", "v", [n("floor"), "rp"], lambda: [
            V.tensor_tensor_scan(T.e[:, e0:e0 + 4 * SEG], T.m[:, m0:m0 + 4 * SEG], T.m[:, m0 + SEG:m0 + 5 * SEG], 0.0,
                                 A.add, A.subtract)])
        ro("rankb", "p", [n("floor"), "ones", "beta"], lambda: [
            P.matmul(pW[:, 64:112], T.ones[:], T.beta[:], True, False)], sem=False)
        ro("rankm", "p", [n("floor"), "ua", "ub"], lambda: [[
            P.matmul(pW[:, 64 + r:112:4], u[:], T.m[:, m0 + SEG * (r + d) + 1:m0 + SEG * (r + d) + 13], False, False)
            for r in range(4) for u, d in ((T.ua, 0), (T.ub, 1))][-1]], soft=[n("rankb")], sem=False)
        ro("rank", "p", [n("scan")], lambda: [[
            P.matmul(pW[:, 64 + r:112:4], T.ones[:], T.e[:, e0 + SEG * r:e0 + SEG * r + 12], False, r == 3)
            for r in range(4)][-1]], soft=[n("rankm")])
        ro("smax", "v", [n("rank"), "tr"], lambda: [
            V.tensor_tensor_scan(T.sm[:, x0:x0 + 48], T.tr[:], pW[:, 64:112], 1.0e6, A.min, A.max)])
        ro("cidx", "v", [n("smax")], lambda: [
            V.tensor_scalar(T.idx[:, s0:s0 + 12], T.sm[:, x0 + 3:x0 + 48:4], 0.25, None, A.mult)])
        reg = lambda r: T.win[:, W0 + BASE + REG * r:W0 + BASE + REG * r + CAP]
        mark = int(FILL) if k < NP - 1 else -int(FILL)
        for r in range(NR):
            ro("fill%d_" % r, "g", prev("scat") or ["go"], lambda r=r: [iota(reg(r), [[0, CAP]], mark, 0)],
               soft=[n("fill%d_" % (r - 1))] if r else prev("sendf"), role="fill")
        ro("scat", "v", [n("cidx"), n("tn"), n("tf"), n("fill3_")], lambda: [
            V.tensor_tensor(T.win[:, W0:W0 + WIN].indirect(T.idx[:, s0:s0 + 12]), v, t, A.add)])
        mine = T.land[:, 384 * j + CAP * me:384 * j + CAP * me + CAP]

        def send(B):
            tr = []
            for u, r in enumerate(calls[B]):
                eng = topo.engines(T.cores[me], T.cores[r])
                w = len(eng) // len(calls[B])
                rid, pid, _ = topo.addr(T.cores[r])
                tr.append(RemoteDMATransfer(dst_ids=[DstId(rid=rid, pnc=pid)],
                                            dma_engine_mask=sum(1 << e for e in eng[u * w:(u + 1) * w]),
                                            remote_sem=T.sem[n("arr" + B)], src=reg(r), dst=mine))
            g.remote_dma_fused(tr, local_sem=T.sem["sent" + X])
            return []

        for B, soft in (("n", []), ("f", [n("sendn")])):
            ro("send" + B, "g", [n("scat")], lambda B=B: send(B), soft=soft, sem=False)
            come = sum(len(topo.engines(T.cores[r], T.cores[me])) // len(calls[B]) for r in calls[B])
            op(n("arr" + B), None, [], None, [n("send" + B)], n("arr" + B), come)

    for k in range(NP + 1):
        for i, X in enumerate("AB"):
            half(k, i, X)
    return ops, sum(len(topo.engines(T.cores[me], T.cores[r])) // len(c) for c in calls.values() for r in c)


def timetable(ops):
    tab = {c: dict(zip(t.split()[::2], map(float, t.split()[1::2]))) for c, t in TIME.items()}
    key = {}
    for n in ops:
        if n in tab[""]:
            key[n] = tab[""][n]
        else:
            k, X = int(n[-2]), n[-1]
            key[n] = tab.get(n[-2:], tab["*"]).get(n[:-2], 0.0) + OFFS[2 * k + "AB".index(X)]
    done, out, todo = set(), {}, sorted(ops, key=lambda n: key[n])
    while todo:
        n = next(n for n in todo if all(d in done for d in ops[n]["hard"] + ops[n]["soft"]))
        todo.remove(n)
        done.add(n)
        if ops[n]["q"]:
            out.setdefault(ops[n]["q"], []).append(n)
    return out


def waits(ops, order):
    at, known, done, need = {q: 0 for q in order}, {q: set() for q in order}, {}, {}
    for n in ops:
        if ops[n]["q"] is None:
            done[n] = {n}
    moved = True
    while moved:
        moved = False
        for q in order:
            while at[q] < len(order[q]) and all(d in done for d in ops[order[q][at[q]]]["hard"]):
                n = order[q][at[q]]
                hard = ops[n]["hard"]
                need[n] = [d for d in hard if d not in known[q] and not any(d != e and d in done[e] for e in hard)]
                for d in hard:
                    known[q] |= done[d]
                done[n] = known[q] | {n}
                at[q] += 1
                moved = True
    return need


def rank_program(g, core, T, topo):
    me = T.rank_of(core)
    if me is None:
        return
    ops, sent = graph(g, T, me, topo)
    order = timetable(ops)
    need = waits(ops, order)
    queue = {"v": g.vector, "s": g.scalar, "p": g.tensor, "y": g.sync, "g": g}
    total, mark = {}, {}
    for n, o in ops.items():
        if o["sem"]:
            total[o["sem"]] = total.get(o["sem"], 0) + o["calls"] * o["inc"]
            mark[n] = total[o["sem"]]
    waited = {}
    for q in order:
        for n in order[q]:
            o = ops[n]
            for d in dict.fromkeys(need[n]):
                s = ops[d]["sem"]
                queue[q].wait_ge(T.sem[s], mark[d])
                waited[s] = max(waited.get(s, 0), mark[d])
            for ins in o["emit"]():
                if o["sem"]:
                    ins.then_inc(T.sem[o["sem"]], o["inc"])
    for X in "AB":
        g.wait_ge(T.sem["sent" + X], NP * sent)
    for s in total:
        if waited.get(s, 0) < total[s]:
            g.wait_ge(T.sem[s], total[s])
